import numpy as np, ml_dtypes
CORES = [16,17,18,19,32,33,34,35]
N = 8
BF = ml_dtypes.bfloat16
def gentries(a):
    return np.ascontiguousarray(a.reshape(8, 16, -1).transpose(0, 2, 1)).reshape(8, -1)
def gtable(e):
    e = np.asarray(e); return np.ascontiguousarray(e.reshape(8, -1, 16).transpose(0, 2, 1)).reshape(128, -1).astype(np.int32)
S, B, D, T, J, L = 4096, 1536, 5, 3, 45, 4096
REC = np.array([0, 256, 128, 85, 64, 51], np.int64)
def sums(rng, tot, lo, hi, n):
    x = rng.integers(lo, hi + 1, n); e = int(tot - np.sum(x))
    room = np.repeat(np.arange(n), hi - x if e > 0 else x - lo)
    np.add.at(x, rng.permutation(room)[:abs(e)], 1 if e > 0 else -1)
    return x
def durs(rng):
    x = rng.integers(1, D + 1, (N, 8, B))
    for q in range(N):
        for g in range(8): x[q, g, :B - 1] = sums(rng, int(rng.integers(S // 8 * 7, S // 2 * 3 + 1)), 1, D, B - 1)
    return x
def gains(rng, e):
    return (1.0 + rng.random((N, 128, T))) * np.exp2(rng.integers(-e, 1, (N, 128, T))) * rng.choice(np.array([-1.0, 1.0]), (N, 128, T))
def pack(A, v, x, m, u):
    return {"am": np.ascontiguousarray(A.reshape(N, 128, B)).astype(np.float32).astype(BF), "ve": np.ascontiguousarray(v.reshape(N, 128, B)).astype(np.float32).astype(BF),
            "du": np.stack([gtable(a) for a in x]), "mp": np.stack([gtable(a) for a in m]), "gain": u.astype(np.float32)}
def setup_inputs(rng):
    return pack(rng.integers(-256, 257, (N, 8, 16, B)), rng.integers(-64, 65, (N, 8, 16, B)), durs(rng), rng.integers(0, B, (N, 8, B)), gains(rng, 1))
def setup_inputs_spread(rng):
    A = rng.integers(-256, 257, (N, 8, 16, B)) >> rng.integers(0, 2, (N, 8, 1, B)); v = rng.integers(-64, 65, (N, 8, 16, B)) >> rng.integers(0, 5, (N, 8, 1, B))
    x = durs(rng); x[:, 1::4] = np.sort(x[:, 1::4], axis=2); x[:, 2::4] = np.sort(x[:, 2::4], axis=2)[..., ::-1]
    m = np.minimum((B * rng.random((N, 8, B)) ** 3).astype(np.int64), B - 1)
    return pack(A, v, x, m, gains(rng, 0) * np.exp2(rng.integers(-1, 1, (N, 1, T))))
def setup_inputs_ends(rng):
    A = 256 * rng.choice(np.array([-1, 1]), (N, 8, 16, B)); one = 256 * rng.choice(np.array([-1, 1]), (N, 8, 1, B))
    for g in (0, 1, 4, 5): A[:, g] = one[:, g]
    for q in range(N):
        for g in (1, 5):
            i = int(rng.integers(0, 16)); A[q, g, i] = -A[q, g, i]
    A[:, 7, :, B - 1] = 256; A[:, 6, :, B - 1] = -256
    v = 64 * rng.choice(np.array([-1, 1]), (N, 8, 16, B))
    x = np.where(rng.random((N, 8, B)) < rng.choice(np.array([0.3, 0.5, 0.7]), (N, 8, 1)), D, 1)
    for q in range(N): x[q, (q + 8 - N) % 8] = D; x[q, (q + 11 - N) % 8] = 1
    return pack(A, v, x, (B - 1) * rng.integers(0, 2, (N, 8, B)), gains(rng, 1))
def setup_inputs_corners(rng):
    A = rng.integers(-256, 257, (N, 8, 16, B)); v = rng.choice(np.array([-64, -63, -1, 0, 0, 1, 63, 64]), (N, 8, 16, B))
    c = rng.integers(64, 257, 16) * rng.choice(np.array([-1, 1]), 16)
    for i in (0, 15): A[:, :, i] = c[i]; v[:, :, i] = 0
    x = rng.choice(np.array([1, D]), (N, 8, B)); m = rng.integers(0, B, (N, 8, B)); last = (S - 1, S, S + 1, S - 2, B - 1, D * (B - 1), S, S - 1)
    for q in range(N):
        for g in range(8):
            x[q, g, :B - 1] = sums(rng, last[(q + g) % 8], 1, D, B - 1); w = (q + 3 * g) % 4
            if w == 0: m[q, g] = np.arange(B)
            elif w == 1: m[q, g] = 0
            elif w == 2: m[q, g] = B - 1
    return pack(A, v, x, m, gains(rng, 0))
def setup_inputs_crowd(rng):
    mid = rng.integers(24, 49, (N, 8, 16)) * rng.choice(np.array([-1, 1]), (N, 8, 16))
    A = np.repeat(mid[..., None], B, axis=3); v = rng.integers(-3, 4, (N, 8, 16, B)); x = rng.integers(1, 4, (N, 8, B)); m = rng.integers(0, B, (N, 8, B))
    for q in range(N):
        for g in range(8):
            if g % 2 == 0:
                n = int(rng.choice(np.array([0, 1, 7, 8, 9, 15, 16])))
                if q == 0: n = (8, 9, 16, 0)[g // 2]
                if q == 1: n = (15, 7, 9, 8)[g // 2]
                o = rng.permutation(16); A[q, g] = rng.integers(112, 257, (16, B)); A[q, g, o[:n]] = -rng.integers(112, 257, (n, B))
                if n < 16: A[q, g, o[n]] = mid[(q + 1) % N, g + 1, o[n]]
            if (q + g // 2) % 2 == 1: x[q, g] = rng.integers(D - 2, D + 1, B)
            w = (q + g) % 4; a = int(rng.integers(0, B))
            if w < 2: m[q, g] = a
            if w == 1: m[q, g, int(rng.integers(0, B))] = (a + 1) % B
            if w == 2: m[q, g] = rng.choice(np.array([0, a, B - 1]), B)
    return pack(A, v, x, m, gains(rng, 0))
def setup_inputs_calm(rng):
    A = rng.integers(14, 27, (N, 8, 16, B)) * rng.choice(np.array([-1, 1]), (N, 8, 16, B)); A[:, ::2] = -rng.integers(32, 65, (N, 4, 16, B))
    A[:, 1::2, 3::4] = rng.integers(6, 9, (N, 4, 4, B)) * rng.choice(np.array([-1, 1]), (N, 4, 4, B)); A[:, ::2, 3::4] = -rng.integers(10, 14, (N, 4, 4, B))
    A[:, ::2, 11::4] = 2 + ((np.arange(B) + rng.integers(0, 2, (N, 4, 2, 1))) & 1)
    A[:, 1::2, 11::4] = 4 + ((np.arange(B) + rng.integers(0, 2, (N, 4, 2, 1))) & 1)
    v = rng.integers(0, 4, (N, 8, 16, B)); v[:, :, 3::4] = 0
    g0 = 2 * int(rng.integers(0, 4)); g1 = 2 * int(rng.integers(0, 4))
    two = rng.permutation(np.array([1, 2, 4, 5, 6, 9, 10, 12, 13, 14])); i0 = int(two[0]); i1 = int(two[1])
    A[:, g0, i0] = -256; A[:, g0 + 1, i0] = 256
    A[:, g1, i1] = -rng.integers(240, 257, (N, B)); A[:, g1 + 1, i1] = rng.integers(240, 257, (N, B))
    x = rng.integers(1, 5, (N, 8, B))
    for q in range(N):
        for g in range(0, 8, 2): x[q, g] = rng.integers(1, D, B); x[q, g, :B - 1] = sums(rng, S - 1 - (B - 1) + (0, 1, 2, -1)[(q + g // 2) % 4], 1, D - 1, B - 1)
    m = rng.integers(0, B, (N, 8, B))
    u = gains(rng, 0); u = np.sign(u) * (0.875 + 0.125 * np.abs(u))
    row = np.arange(128); full = (row % 8 == 0) | (row % 4 == 3); least = (row % 16 == 11) | (row % 16 == 15)
    low = np.zeros(128, bool); low[[16 * ((g0 + 7) % 8) + i0, 16 * g0 + i0, 16 * (g0 + 1) + i0]] = True
    near = np.zeros(128, bool); near[[16 * ((g1 + 7) % 8) + i1, 16 * (g1 + 1) + i1]] = True
    big = row == 16 * g1 + i1
    rest = ~(full | low | near | big)
    u[:, full] = 2.0 * np.sign(u[:, full]); u[:, least] = 2.5 * np.sign(u[:, least])
    u[:, low] = rng.choice(np.array([-1.0, 1.0]), (N, 3, 1)) * (0.125 + (rng.integers(0, 256, (N, 3, T)) + 0.47) * 2.0 ** -17)
    u[:, near] = 0.125 * np.sign(u[:, near])
    u[:, big] = rng.choice(np.array([-2.5, 2.5]), (N, 1, 1)) * np.where(np.arange(T) == 0, 1.0, -1.0 / (T - 1))
    y = np.mean(reference(**pack(A, v, x, m, u))["yo"].astype(np.float64) ** 2, axis=2)
    aim = (2.0 * T * (S // L) / 72.0) ** 2
    have = np.sum(y[:, ~rest], axis=1) / 128.0; more = np.sum(y[:, rest], axis=1) / 128.0
    c = np.clip(np.sqrt(np.maximum(aim - have, 0.0) / more), 0.125, 2.2)
    u[:, rest] = u[:, rest] * c[:, None, None]
    return pack(A, v, x, m, u)
def check_ranges(d):
    bad = []
    for k, lo, hi in (("am", -256, 256), ("ve", -64, 64), ("du", 1, D), ("mp", 0, B - 1)):
        a = np.asarray(d[k]).astype(np.float64)
        if not (np.min(a) >= lo and np.max(a) <= hi) or np.any(a != np.floor(a)): bad.append("range of " + k)
    u = np.abs(np.asarray(d["gain"]).astype(np.float64))
    if not np.all((u >= 0.125) & (u <= 2.5)): bad.append("range of gain")
    return bad
def reference(am, ve, du, mp, gain):
    A = am.astype(np.float32).astype(np.int64).reshape(N, 8, 16, B); v = ve.astype(np.float32).astype(np.int64).reshape(N, 8, 16, B)
    d = np.stack([gentries(a) for a in du]).astype(np.int64); m = np.stack([gentries(a) for a in mp]).astype(np.int64)
    u = gain.astype(np.float64).reshape(N, 8, 16, T); out = np.zeros((N, 8, 16, L)); n = np.arange(S)
    for t in range(T):
        O = np.add.accumulate(d, axis=2) - d
        seg, ks, ys = [], [], []
        for q in range(N):
            b = np.stack([np.searchsorted(O[q, g], n, side="right") - 1 for g in range(8)])
            k = n - np.take_along_axis(O[q], b, 1)
            w = np.minimum(k * np.take_along_axis(REC[d[q]], b, 1), 256)
            dif = np.roll(A[q], -1, axis=2) - A[q]
            ys.append(256 * np.take_along_axis(A[q], b[:, None, :], 2) + np.take_along_axis(dif, b[:, None, :], 2) * w[:, None, :])
            seg.append(b); ks.append(k)
        A2, v2, d2 = [], [], []
        for r in range(N):
            q = (r + 1 + t % (N - 1)) % N
            X = np.roll(ys[q], -1, axis=0); P = np.roll(O[q], -1, axis=0)
            at = (np.take_along_axis(np.take_along_axis(P, m[r], 1), seg[r], 1) + J * ks[r]) & (S - 1)
            z = (ys[r] * np.take_along_axis(X, at[:, None, :], 2)) * 2.0 ** -30
            out[r] += u[r, :, :, t][:, :, None] * np.add.reduce(np.tanh(z).reshape(8, 16, S // L, L), axis=2)
            if t < T - 1:
                s = np.take_along_axis(X, np.minimum(O[r], S - 1)[:, None, :], 2)
                up = np.add.reduce((s > 256 * A[r]).astype(np.int64), axis=1) >= 9; live = O[r] < S
                nd = np.where(up, np.where(d[r] == D, D - 1, d[r] + 1), np.where(d[r] == 1, 2, d[r] - 1))
                nv = np.clip(v[r] + (s >> 12), -64, 64); na = A[r] + nv
                na = np.where(na > 256, 512 - na, na); na = np.where(na < -256, -512 - na, na)
                d2.append(np.where(live, nd, d[r])); v2.append(np.where(live[:, None, :], nv, v[r])); A2.append(np.where(live[:, None, :], na, A[r]))
        if t < T - 1: A, v, d = np.stack(A2), np.stack(v2), np.stack(d2)
    return {"yo": out.reshape(N, 128, L).astype(np.float32)}

def check_inputs(d):
    bad = list(check_ranges(d))
    if not bad:
        for name, y in reference(**d).items():
            for q in range(N):
                v = np.abs(np.asarray(y[q], np.float64)); s = np.sqrt(np.mean(v * v))
                if v.max() > 12 * s or s < 2.0 ** -4: bad.append('%s of rank %d is uneven or too small' % (name, q))
    return bad

@@ -1,0 +1,613 @@
+from concourse.mybir import AluOpType as ALU, ActivationFunctionType as AF
+
+S, B, NB, N = 4096, 1536, 3, 8
+CH = 1024
+NC = S // CH
+JB = 1544
+TW = JB + 1 + B
+WP, WW = 16, 7712
+CUT = (504, 1016)
+MW = 1552
+F32, BF, F16, I32, U16 = "float32", "bfloat16", "float16", "int32", "uint16"
+
+SCRATCH = {}
+for _d, _w, _names in (
+        (BF, B, "A V0 RB RX cmp fb dead zv"), (F16, B, "uh a1 a2"), (F16, MW, "dif difx"), (BF, MW, "SS"), (BF, TW, "PM"),
+        (I32, 96, "dui mpi"), (F32, 4, "gn OJ OQ"), (U16, 96, "mpu dl offs"), (U16, 98, "offw"), (U16, 256, "idx idxr el0 el1 el2"),
+        (F32, 48, "K"), (F32, 16, "OH"), (I32, 16, "pi"),
+        (BF, 128, "qrow gq Ib Nb I4 N3 N3r M15 Irb Nrb"), (F16, 128, "Ih Nh Sh Ir Nr Sr"), (F32, 128, "If Sf Lf t1 t2 t3"),
+        (BF, 2048, "val GQ MV MO MI ME"), (BF, 512, "BQ BR"), (BF, 384, "FD FX GR GC HR HC"),
+        (BF, 2064, "zero"), (F32, 256, "c720 sa sb se"), (I32, 256, "ea eb"), (BF, WP + WW, "W"),
+        (BF, 288, "bun"), (F32, 100, "inc"), (F32, 96, "of"), (BF, 96, "lv x1 z2 dn e1 e5 u2"),
+        (F16, 264, "ph"), (F32, 260, "pf"), (F32, TW, "TY TX"), (F32, S + 8, "X0 X1"), (F32, S, "Y DX Z"),
+        (BF, 288, "lb0 lb1 lb2"), (F16, MW, "ld0 ld1 ld2"), (U16, 256, "li0 li1 li2")):
+    for _n in _names.split():
+        SCRATCH[_n] = ("sbuf", [128, _w], _d)
+for _n, _w in (("pA", B), ("pB", B), ("p6", 512), ("p7", 512)):
+    SCRATCH[_n] = ("psum", [128, _w], F32)
+
+SIM = 64
+SHIP = (0, 1)
+NDMA = 64
+SEMAPHORES = ["pe", "dve", "act", "pool", "hs"] + ["q%d" % i for i in range(NDMA)]
+for _t in range(NB):
+    for _m in "bdehij":
+        SEMAPHORES += ["s%s%d" % (_m, _t), "r%s%d" % (_m, _t)]
+for _t in SHIP:
+    SCRATCH["yd%d" % _t] = ("dram", [NC, 128, CH], F32)
+    for _c in range(NC):
+        SEMAPHORES += ["sy%d%d" % (_t, _c), "ry%d%d" % (_t, _c)]
+
+MODELS = [(0.00104, 0.0007, 1.55, 3.8, 1.0, 1.0, 0.12), (0.0009, 0.0009, 1.2, 2.5, 1.2, 1.4, 0.15),
+          (0.0011, 0.0005, 1.9, 5.0, 0.8, 0.9, 0.1)]
+OPT = {"merge": (2,), "tab": ((0, 1), (0, 1), (1, 0)), "lat": (18.0, 25.0, 12.0, 18.0)}
+ORDER = "0:000B020<0406080>0D4;4P700J4I0T1C0H150N13441=4T1?534V4J0S1;1A1E171O4=1H0@4N2B2I3:50461J54321L393<372N570F2E586V3R5:2F0L5F5<5>6<5@5J3T6>5B4R2J5N2S5I5M600V5D0P102Q26641Q2>6D5P1S291U3Q2:3M621W2<232@21185R3E666F3I8H6H255U726B5W6@41683?3A3W2W4M1G4?4C4E6::38U8K8V6M8L6O496P6S6U6J979R:574423531902U4G3C8N3K3G7B2L773O4A92787E9T7F7:9W7<7P7H7>7J7V7R7L7T94877@8P7N8R98:B81>P88829;:0:D848?:V9>8:9C9<:T;>;@9@9J9G9D9N8=9H9L:6:G8@;19P:::8:K:H;C8B:<:L;5;2:>:@:N;G;P>N;6AS;R:Q;T;8;V>4:S<0;DAJ>6<2;;AL<6;H;=8D8F<9<4<:AO<HAU><<<AP<L;J<J>>@@>@>:>R>8;M<N=0<T;O<B<><E@M<G@N<A@C<P>E=2@D<V<R>G>B@P>T>H>K>M@FAV=4?:>W@R@H?0?=@W?>?2?H?@?4?B?N?6?J?D?L@T@1@J?8?FA0?V@5B4G8B0A2?QA;?R=>=H=6B8A7A4A??TABA8@2B7A<AF@7C2=RA@C4AD@8B<C7B3AHB@B>CIC8B;@:BBC<BMBHBDBFC;CVI6CLD0BQBND2D4FLC>D6BRD8FNBJCA@<BT=TCCCFD:BWCDC1=J=9D@D<FRFPDCHD@>CJD?FTCNI9DRICDNCPG5G2EHDTE2DPED=@CSG6E6CUE5DDFVE9G0DHG:E:DKDMEJDGE>EF=;DVHQ=<HGE0E=HHEAEC=CHR=EELHJGJ=W=FHTHLIMG<GM=MHNENI3I:G?>1G@EV=OGN>2GBH0GPHVH6EQGD=PI<GFH2I>ESI0GHGRI4GTH4IDH9I@ETF8H:IFGVIQF0IUIHFBH<IRF3IJF5IVINF6FDJ9H>J=J0J5F:FGJ2FIJ6F=FJH@J:F?HBJ>JAF@JHJEJBJKK0JMJFK3JNJPK5K6K8JSJTK;JVK<K>"
+SEED = (0, 0.35, 0.0, 2.0)
+
+
+def bits(m):
+    return bin(m).count("1")
+
+
+def helper_of(c, topo):
+    mine = [k for k in topo.cores_of(c) if topo.die(k) == topo.die(c)]
+    other = [k for k in topo.cores_of(c) if topo.die(k) != topo.die(c)]
+    return other[mine.index(c)]
+
+
+def relayed(src, dst, T, topo):
+    h = helper_of(src, topo)
+    return topo.chip(src) != topo.chip(dst) and T.rank_of(h) is None and topo.may_write(h, dst)
+
+
+def engines(src, dst, part, topo):
+    e = topo.engines(src, dst)
+    if part is not None:
+        e = e[part * len(e) // 2:(part + 1) * len(e) // 2]
+    return sum(1 << k for k in e)
+
+
+def remote(g, T, topo, src, dst, out, in_, rsem, lsem, part=None):
+    rid, pid, _ = topo.addr(dst)
+    g.remote_dma(out, in_, T.sem[rsem], T.sem[lsem], pid, rid, engines(src, dst, part, topo))
+
+
+def way(src, dst, c, T, topo):
+    if not relayed(src, dst, T, topo):
+        return [src, dst]
+    h = helper_of(src, topo)
+    far = [f for f in range(SIM) if topo.mates(topo.chip(f), topo.chip(dst)) and topo.may_write(h, f) and topo.may_write(f, dst)
+           and topo.die(f) == topo.die(h)]
+    if c < NC // 2 and far:
+        return [src, h, far[T.rank_of(src) % len(far)], dst]
+    return [src, h, dst]
+
+
+def helper_program(g, core, T, topo):
+    sent = [0]
+
+    def back(t, chunks):
+        for c in chunks:
+            for r in range(N):
+                w = way(T.cores[r], T.cores[(r + 1 + t) % N], c, T, topo)
+                if core in w:
+                    k = w.index(core)
+                    stage = T["YZ"[t]][:, CH * c:CH * c + CH]
+                    g.wait_ge(T.sem["q%d" % (NC * t + c)], bits(engines(w[k - 1], core, 1, topo)))
+                    if k + 2 == len(w):
+                        remote(g, T, topo, core, w[k + 1], T["yd%d" % t][c], stage, "ry%d%d" % (t, c), "hs", 1)
+                    else:
+                        remote(g, T, topo, core, w[k + 1], stage, stage, "q%d" % (NC * t + c), "hs", 1)
+                    sent[0] += bits(engines(core, w[k + 1], 1, topo))
+
+    for t in range(NB):
+        for c in T.cores:
+            dst = T.cores[(T.rank_of(c) - 1 - t) % N]
+            if helper_of(c, topo) == core and relayed(c, dst, T, topo):
+                for m, x0, x1 in (("d", 0, CUT[0]), ("h", CUT[0], CUT[1])):
+                    part = T["ld%d" % t][:, x0:x1]
+                    g.wait_ge(T.sem["r%s%d" % (m, t)], bits(topo.mask(c, core)))
+                    remote(g, T, topo, core, dst, part, part, "r%s%d" % (m, t), "hs", 0)
+                    sent[0] += bits(engines(core, dst, 0, topo))
+        if t - 1 in SHIP:
+            back(t - 1, range(NC // 2, NC))
+        if t in SHIP:
+            back(t, range(NC // 2))
+    if sent[0]:
+        g.wait_ge(T.sem["hs"], sent[0])
+
+
+def build(g, core, T, topo, model):
+    CYC, PCY, GATH, SCAT, DS, RS, _ = model
+    r = T.rank_of(core)
+    ops = []
+    ndma = [0]
+    v, a, pe = g.vector, g.scalar, g.tensor
+
+    def add(alts, reads, writes, lat=0.0, tok=None):
+        ops.append({"alts": alts, "r": list(reads), "w": list(writes), "lat": lat, "tok": tok})
+
+    def dve(fn, n, reads, writes):
+        add({"dve": (fn, 0.06 + max(n, 64) * CYC)}, reads, writes)
+
+    def act(fn, n, reads, writes):
+        add({"act": (fn, 0.07 + max(n, 64) * CYC)}, reads, writes)
+
+    def either(fv, fa, n, reads, writes):
+        add({"dve": (fv, 0.06 + max(n, 64) * CYC), "act": (fa, 0.07 + max(n, 64) * CYC)}, reads, writes)
+
+    def pool(fn, n, writes):
+        add({"pool": (fn, 0.13 + 2 * n * CYC)}, [], writes)
+
+    def ts(out, in0, s1, s2, op0, op1, n, reads, writes):
+        if op1 is None:
+            dve(lambda: [v.tensor_scalar(out, in0, s1, None, op0)], n, reads, writes)
+        else:
+            dve(lambda: [v.tensor_scalar(out, in0, s1, s2, op0, op1)], n, reads, writes)
+
+    def tt(out, in0, in1, op, n, reads, writes):
+        dve(lambda: [v.tensor_tensor(out, in0, in1, op)], n, reads, writes)
+
+    def cp(out, in_, n, reads, writes):
+        dve(lambda: [v.tensor_copy(out, in_)], n, reads, writes)
+
+    def ms(out, c, n, writes):
+        dve(lambda: [v.memset(out, c)], n, [], writes)
+
+    def scan(out, d0, d1, ini, n, reads, writes):
+        dve(lambda: [v.tensor_tensor_scan(out, d0, d1, ini, ALU.add, ALU.add)], n, reads, writes)
+
+    def ac(out, in_, f, n, reads, writes, bias=0.0, scale=1.0):
+        act(lambda: [a.activation(out, in_, f, bias=bias, scale=scale)], n, reads, writes)
+
+    def lin(out, in_, scale, bias, n, reads, writes):
+        either(lambda: [v.tensor_scalar(out, in_, scale, bias, ALU.mult, ALU.add)],
+               lambda: [a.activation(out, in_, AF.Identity, bias=bias, scale=scale)], n, reads, writes)
+
+    def half(out, in_, scale, bias, n, reads, writes):
+        add({"dve": (lambda: [v.tensor_scalar(out, in_, scale, bias, ALU.mult, ALU.add)], 0.06 + n * CYC / 2),
+             "act": (lambda: [a.activation(out, in_, AF.Identity, bias=bias, scale=scale)], 0.07 + n * CYC)}, reads, writes)
+
+    def mm(groups, n, reads, writes, start=True, stop=True):
+        def fn():
+            last = []
+            for grp in groups:
+                for i, (o, l, x) in enumerate(grp):
+                    ins = pe.matmul(o, l, x, start and i == 0, stop and i == len(grp) - 1)
+                last.append(ins)
+            return last
+        add({"pe": (fn, 0.06 + n * PCY)}, reads, writes)
+
+    def dma(out, in_, lat, reads, writes, acc=False):
+        s = "q%d" % ndma[0]
+        ndma[0] += 1
+        if acc:
+            add({"g": (lambda: g.dma_start(out, in_, accum_op=ALU.add).then_inc(T.sem[s], 16), 0.6)}, reads, writes, lat * DS, [(s, 16)])
+        else:
+            pairs = list(zip(out, in_)) if isinstance(out, list) else [(out, in_)]
+            add({"sp": (lambda: [g.sync.dma_start(o, i).then_inc(T.sem[s], 16) for o, i in pairs], 0.08 * len(pairs))}, reads, writes,
+                lat * DS, [(s, 16 * len(pairs))])
+
+    def send(m, t, buf, src_ap, cols, lat, reads, land):
+        dst, src = T.cores[(r - 1 - t) % N], T.cores[(r + 1 + t) % N]
+        out = T[buf][:, cols[0]:cols[1]]
+        to, rs = dst, "r%s%d" % (m, t)
+        if m in "dh" and relayed(core, dst, T, topo):
+            to = helper_of(core, topo)
+        got = topo.mask(src, core)
+        if m in "dh" and relayed(src, core, T, topo):
+            got = engines(helper_of(src, topo), core, 0, topo)
+        key = "sent" + m + str(t)
+        add({"g": (lambda: remote(g, T, topo, core, to, out, src_ap, rs, "s%s%d" % (m, t)), 0.4 * RS)}, reads, [key], 1.0 * RS,
+            [("s%s%d" % (m, t), bits(topo.mask(core, to)))])
+        add({"none": (None, 0.0)}, [key], [land], lat * RS, [(rs, bits(got))])
+
+    def ship(t, c, X, xk, after):
+        w = way(core, T.cores[(r + 1 + t) % N], c, T, topo)
+        wi = way(T.cores[(r - 1 - t) % N], core, c, T, topo)
+        x = slice(CH * c, CH * c + CH)
+        out, rs = (T["yd%d" % t][c], "ry%d%d" % (t, c)) if len(w) == 2 else (T["YZ"[t]][:, x], "q%d" % (NC * t + c))
+        key, ls = "ship%d%d" % (t, c), "sy%d%d" % (t, c)
+        add({"g": (lambda: remote(g, T, topo, core, w[1], out, X[:, x], rs, ls, 1), 0.4 * RS)}, [xk] + after, [key], 3.0 * RS,
+            [(ls, bits(engines(core, w[1], 1, topo)))])
+        add({"none": (None, 0.0)}, [key], ["yd%d%d" % (t, c)], OPT["lat"][c] * RS, [("ry%d%d" % (t, c), bits(engines(wi[-2], core, 1, topo)))])
+
+    K, OH = T.K, T.OH
+    kn = {}
+
+    def kc(name):
+        if name not in kn:
+            kn[name] = len(kn)
+        return K[:, kn[name]:kn[name] + 1]
+
+    def oh(j):
+        return OH[:, j:j + 1]
+
+    def col(name, in0, s1, s2, op0, op1, reads):
+        ts(kc(name), in0, s1, s2, op0, op1, 1, reads, [name])
+
+    def lc(name, in_, scale, bias, reads):
+        lin(kc(name), in_, scale, bias, 1, reads, [name])
+
+    def blk(M, i):
+        return M[:, 128 * i:128 * i + 128]
+
+    dma(T.dui[:], T.du[:], 2.2, [], ["dui"])
+    dma(T.A[:], T.am[:], 2.8, [], ["A"])
+    dma(T.mpi[:], T.mp[:], 2.2, [], ["mpi"])
+    dma(T.V0[:], T.ve[:], 2.8, [], ["V0"])
+    dma(T.gn[:, 0:3], T.gain[:], 2.2, [], ["gn"])
+    pool(lambda: [g.iota(T.pi[:, 0:1], [[0, 1]], 0, 1)], 1, ["pi0"])
+    pool(lambda: [g.iota(T.qrow[:], [[1, 128]], 0, 0, allow_small_or_imprecise_dtypes=True)], 128, ["qrow"])
+    pool(lambda: [g.iota(T.val[:], [[-1, 16], [32, 8], [1, 16]], 0, 0, allow_small_or_imprecise_dtypes=True)], 2048, ["val"])
+    pool(lambda: [g.iota(T.gq[:], [[1, 8], [0, 16]], 0, 0, allow_small_or_imprecise_dtypes=True)], 128, ["gq"])
+    ms(T.zero[:], 0.0, 1032, ["zero"])
+    ts(T.pi[:, 4:5], T.pi[:, 0:1], 15, None, ALU.bitwise_and, None, 1, ["pi0"], ["pi4"])
+    ts(T.pi[:, 8:9], T.pi[:, 0:1], 3, None, ALU.bitwise_and, None, 1, ["pi0"], ["pi8"])
+    cp(kc("p"), T.pi[:, 0:1], 1, ["pi0"], ["p"])
+    cp(kc("r"), T.pi[:, 4:5], 1, ["pi4"], ["r"])
+    cp(kc("j"), T.pi[:, 8:9], 1, ["pi8"], ["j"])
+    col("s", kc("p"), kc("r"), 2.0, ALU.subtract, ALU.mult, ["p", "r"])
+    col("q", kc("r"), kc("j"), 0.25, ALU.subtract, ALU.mult, ["r", "j"])
+    lc("g", kc("s"), 1.0 / 32, 0.0, ["s"])
+    ts(OH[:], T.qrow[:, 0:16], kc("r"), None, ALU.is_equal, None, 16, ["qrow", "r"], ["OH"])
+    ts(T.OJ[:], T.qrow[:, 0:4], kc("j"), None, ALU.is_equal, None, 4, ["qrow", "j"], ["OJ"])
+    ts(T.OQ[:], T.qrow[:, 0:4], kc("q"), 1.0 / 256, ALU.is_equal, ALU.mult, 4, ["qrow", "q"], ["OQ"])
+    lc("wO", oh(0), 1.0, oh(8), ["OH"])
+    lc("one", oh(2), 1.0, oh(3), ["OH"])
+    lc("w1", oh(12), -45.0, kc("wO"), ["OH", "wO"])
+    col("w2", kc("w1"), oh(1), oh(9), ALU.subtract, ALU.subtract, ["OH", "w1"])
+    lc("thr", oh(3), -7.5, 8.0, ["OH"])
+    lc("b1", kc("s"), -1.0, -7.5, ["s"])
+    lc("beta", oh(3), 7.5, kc("b1"), ["b1", "OH"])
+    lc("wi", oh(3), float(JB), oh(2), ["OH"])
+    lc("c1", kc("r"), 1.0, 7690.0, ["r"])
+    lc("cv", oh(1), -7690.0, kc("c1"), ["c1", "OH"])
+    lc("ei", kc("r"), 45.0, -720.0, ["r"])
+    col("p1", kc("p"), 16.0, 128.0, ALU.is_lt, ALU.mult, ["p"])
+    col("pr", kc("p1"), kc("p"), -16.0, ALU.add, ALU.add, ["p1", "p"])
+    col("gr", kc("pr"), kc("r"), 1.0 / 16, ALU.subtract, ALU.mult, ["pr", "r"])
+    lc("n3", oh(3), -float(JB), 0.0, ["OH"])
+    lc("kn", kc("j"), 1.0, -5.0, ["j"])
+    for nm, sl, b0 in (("R", (13.0, 8.0, 22.0, 85.0), 51.0), ("C", (12.0, 10.0, 20.0, 86.0), 52.0)):
+        lc(nm + "0", T.OJ[:, 0:1], -sl[0], 0.0, ["OJ"])
+        for j in (1, 2, 3):
+            lc(nm + str(j), T.OJ[:, j:j + 1], -sl[j], kc(nm + str(j - 1)), ["OJ", nm + str(j - 1)])
+        lc(nm + "a", T.OJ[:, 0:1], b0, 0.0, ["OJ"])
+        lc(nm + "b", kc("kn"), kc(nm + "3"), kc(nm + "a"), ["kn", nm + "3", nm + "a"])
+    ts(T.MV[:], T.val[:], kc("s"), None, ALU.is_equal, None, 1024, ["val", "s"], ["MV"])
+    half(T.MO[:], T.MV[:], kc("wO"), 0.0, 2048, ["MV", "wO"], ["MO"])
+    ts(T.M15[:], blk(T.val, 1), kc("s"), oh(15), ALU.is_equal, ALU.mult, 64, ["val", "s", "OH"], ["M15"])
+    ac(T.ME[:], T.val[:], AF.Abs, 2048, ["val", "beta"], ["ME"], bias=kc("beta"))
+    ts(T.MI[:], T.ME[:], kc("thr"), kc("wi"), ALU.is_lt, ALU.mult, 1024, ["ME", "thr", "wi"], ["MI"])
+    ts(T.ME[:], T.ME[:], kc("thr"), kc("w2"), ALU.is_lt, ALU.mult, 1024, ["ME", "thr", "w2"], ["ME"])
+    ts(T.If[:], T.qrow[:], kc("p"), None, ALU.is_equal, None, 128, ["qrow", "p"], ["If"])
+    for name, w in (("Ib", 1.0), ("Nb", -1.0), ("I4", 4.0), ("Ih", 1.0), ("Nh", -1.0)):
+        lin(T[name][:], T.If[:], w, 0.0, 128, ["If"], [name])
+    ts(T.Ir[:], T.qrow[:], kc("pr"), None, ALU.is_equal, None, 64, ["qrow", "pr"], ["Ir"])
+    for name, w in (("Nr", -1.0), ("Irb", 1.0), ("Nrb", -1.0)):
+        lin(T[name][:], T.Ir[:], w, 0.0, 128, ["Ir"], [name])
+    ts(T.t3[:], T.gq[:], kc("g"), None, ALU.is_equal, None, 128, ["gq", "g"], ["t3"])
+    ts(T.t2[:], T.gq[:], kc("gr"), None, ALU.is_equal, None, 128, ["gq", "gr"], ["t2"])
+    lin(T.N3[:], T.t3[:], kc("n3"), 0.0, 128, ["t3", "n3"], ["N3"])
+    lin(T.N3r[:], T.t2[:], kc("n3"), 0.0, 128, ["t2", "n3"], ["N3r"])
+    for q in range(4):
+        lin(blk(T.BQ, q), T.t3[:], T.OQ[:, q:q + 1], 0.0, 128, ["t3", "OQ"], ["BQ%d" % q])
+        lin(blk(T.BR, q), T.t2[:], T.OQ[:, q:q + 1], 0.0, 128, ["t2", "OQ"], ["BR%d" % q])
+    lin(T.t1[:], T.t3[:], oh(15), 0.0, 128, ["t3", "OH"], ["t1"])
+    tt(T.Sf[:], T.t1[:], T.If[:], ALU.subtract, 256, ["t1", "If"], ["Sf"])
+    lin(T.Sh[:], T.Sf[:], 1.0, 0.0, 128, ["Sf"], ["Sh"])
+    lin(T.t1[:], T.t2[:], oh(15), 0.0, 128, ["t2", "OH"], ["t1"])
+    tt(T.Sr[:], T.t1[:], T.Ir[:], ALU.subtract, 256, ["t1", "Ir"], ["Sr"])
+    ts(T.Lf[:], T.qrow[:], kc("p"), None, ALU.is_gt, None, 128, ["qrow", "p"], ["Lf"])
+    tt(T.Lf[:], T.Lf[:], T.t3[:], ALU.mult, 256, ["Lf", "t3"], ["Lf"])
+    lin(T.c720[:], T.zero[:, 0:256], 0.0, 720.0, 256, ["zero"], ["c720"])
+    lin(T.inc[:, 0:1], T.zero[:, 0:1], 0.0, 0.0, 1, ["zero"], ["inc"])
+    lin(T.ph[:, 0:8], T.zero[:, 0:8], 0.0, 0.0, 1, ["zero"], ["phz"])
+    lin(T.pf[:, 0:4], T.zero[:, 0:4], 0.0, 0.0, 1, ["zero"], ["pf"])
+    lin(T.TY[:, B:JB], T.zero[:, 0:8], 0.0, 0.0, 1, ["zero"], ["TYz"])
+    lin(T.TX[:, B:JB], T.zero[:, 0:8], 0.0, 0.0, 1, ["zero"], ["TXz"])
+    lin(T.X0[:, S:S + 8], T.zero[:, 0:8], 0.0, -3336.0, 1, ["zero"], ["Xe0"])
+    lin(T.X1[:, S:S + 8], T.zero[:, 0:8], 0.0, -3336.0, 1, ["zero"], ["Xe1"])
+    lin(T.difx[:, B:MW], T.zero[:, 0:16], 0.0, 0.0, 1, ["zero"], ["drz", "dr4"])
+    half(T.SS[:], T.zero[:, 0:MW], 1.0, kc("one"), MW, ["zero", "one"], ["SS0", "SS1"])
+    lin(T.PM[:, B:JB], T.zero[:, 0:8], 0.0, 0.0, 1, ["zero"], ["PM3", "PM5"])
+    dma(T.RX[:], T.SS[:, 0:B], 2.5, ["SS0", "SS1"], ["RXh", "RXl", "RXH", "RXL"])
+    dma(T.RB[:], T.zero[:, 0:B], 2.5, ["zero"], ["RBh", "RBl"])
+    cp(T.mpu[:], T.mpi[:], 96, ["mpi"], ["mpu"])
+    cp(T.dl[:], T.dui[:], 96, ["dui"], ["dl"])
+
+    def gather(out, win, n, reads, writes):
+        either(lambda: [v.tensor_copy(out, win)], lambda: [a.activation(out, win, AF.Identity)], n * GATH, reads, writes)
+
+    for h in range(2):
+        gather(T.cmp[:, 768 * h:768 * h + 768], T.qrow[:, 0:16].indirect(T.dl[:, 48 * h:48 * h + 48]), 768, ["qrow", "dl"], ["cmp%d" % h])
+        mm([[(T.p6[:, 0:96], blk(T.MV, i), T.cmp[:, 96 * i:96 * i + 96]) for i in range(8 * h, 8 * h + 8)]], 768,
+           ["MV", "cmp%d" % h], ["b6"], h == 0, h == 1)
+    lin(T.bun[:, 0:96], T.p6[:, 0:96], 1.0 / 16, 0.0, 96, [], ["b6", "bd"])
+
+    bA, bB = ["b0", "b1", "b2"], ["b3", "b4", "b5"]
+    PIECES = ((0, 0, 384), (1, 384, 512), (1, 512, 768), (2, 768, 1024), (2, 1024, 1152), (3, 1152, 1536))
+
+    def tables(Tb, tk, dsrc, dk, F, GR, GC, M, mk, df, fk):
+        dma([F[j:128:4, :] for j in range(4)], [dsrc] * 4, 2.0, [dk], [tk + "F"])
+        Fk = [tk + "F"]
+        for G, nm, P, bk, out, ok in ((GR, "R", T.pA, bA, 0, tk), (GC, "C", T.pB, bB, JB + 1, tk + "j")):
+            ac(G[:], F[:], AF.Relu, 384, Fk + [nm + "3", nm + "b"], [tk + nm], bias=kc(nm + "b"), scale=kc(nm + "3"))
+            mm([[(P[:, x0:x1], blk(M, q), G[:, x0 - 384 * q:x1 - 384 * q])] for q, x0, x1 in PIECES], B,
+               [tk + nm] + [mk + str(q) for q in range(4)], bk)
+            for j, (x0, x1) in enumerate(((0, CUT[0]), CUT, (CUT[1], B))):
+                tt(Tb[:, out + x0:out + x1], df[:, x0:x1], P[:, x0:x1], ALU.mult, x1 - x0, fk[j], bk[max(j - 1, 0):j + 1] + [ok + "abc"[j]])
+        lin(Tb[:, JB:JB + 1], df[:, B:B + 1], 1.0, 0.0, 1, fk[2], [tk + "0"])
+        tt(Tb[:, TW - 1:TW], Tb[:, TW - 1:TW], Tb[:, B - 1:B], ALU.subtract, 1, [tk + "c"], [tk + "jc"])
+
+    def samples(Tb, tk, lst, lk, slots, Y, yk):
+        for c in range(NC):
+            k = slots[c % len(slots)]
+            o = T.DX[:, CH * k:CH * k + CH]
+            gather(o, Tb[:].indirect(lst[:, 64 * c:64 * c + 64]), CH, [tk + s for s in ("a", "b", "c", "ja", "jb", "jc", "0", "z")] + [lk[c // 2]], ["D%d" % k])
+            ini = 0.0 if c == 0 else Y[:, CH * c - 1:CH * c]
+            scan(Y[:, CH * c:CH * c + CH], o, T.zero[:, 0:CH], ini, CH,
+                 ["D%d" % k, "zero"] + ([yk + str(c - 1)] if c else []), [yk + str(c)])
+
+    def output(t):
+        X, XK = T["X%d" % (t % 2)], ["X%d%d" % (t % 2, c) for c in range(NC)]
+        for c in range(NC):
+            x = slice(CH * c, CH * c + CH)
+            z, zk, y = T.Z[:, x], "Z%d" % c, T.Y[:, x]
+            if t in SHIP:
+                yd, y = T["yd%d" % t], z
+                dma([T.Z[16:128, x], T.Z[0:16, x]], [yd[c, 0:112, :], yd[c, 112:128, :]], 3.0, ["yd%d%d" % (t, c)], [zk])
+            tt(z, X[:, 0:S].indirect(T["el%d" % t][:, 64 * c:64 * c + 64]), y, ALU.mult, CH * GATH,
+               XK + ["el%d" % t] + ([] if t in SHIP else ["Y%d" % c]), [zk])
+            ac(z, z, AF.Tanh, CH, [], [zk], scale=2.0 ** -14)
+            lin(z, z, T.gn[:, t:t + 1], 0.0, CH, ["gn"], [zk])
+            dma(T.yo[:, x], z, 3.0, [zk], ["yo%d" % c], acc=t > 0)
+
+    for t in range(NB):
+        lb, ld, li = T["lb%d" % t], T["ld%d" % t], T["li%d" % t]
+        X, XK, own = T["X%d" % (t % 2)], ["X%d%d" % (t % 2, c) for c in range(NC)], t not in SHIP
+        Xe = "Xe%d" % (t % 2)
+        scan(T.inc[:, 1:97], T.bun[:, 0:96], T.zero[:, 0:96], 0.0, 96, ["bd", "zero"], ["inc"])
+        mm([[(T.p7[:, 0:1], T.Lf[:], T.inc[:, 96:97])]], 256, ["Lf", "inc"], ["b7"])
+        ts(T.bun[:, 96:192], T.inc[:, 0:96], T.p7[:, 0:1], None, ALU.add, None, 96, ["inc"], ["b7", "bh"])
+        ts(T.of[:], T.inc[:, 0:96], T.p7[:, 0:1], None, ALU.add, None, 96, ["inc"], ["b7", "of"])
+        tt(T.bun[:, 192:288], T.of[:], T.bun[:, 96:192], ALU.subtract, 192, ["of", "bh"], ["bl"])
+        send("b", t, "lb%d" % t, T.bun[:], (0, 288), 2.2, ["bd", "bh", "bl"], "lb%d" % t)
+        Ac, I1, N1, ak = (T.A, T.Ib, T.Nb, ["A", "A", "A", "Ib", "Nb"]) if t == 0 else (T.a2, T.Ih, T.Nh, ["a20", "a21", "a22", "Ih", "Nh"])
+        A0 = 0.0 if t == 0 else -256.0
+        rk = ["Irb", "Nrb"] if t == 0 else ["Ir", "Nr"]
+        for P, bk, I2, N2, D, dk, mk in ((T.pA, bA, T[rk[0]], T[rk[1]], T.difx, "dr", rk), (T.pB, bB, I1, N1, T.dif, "df", ak[3:]))[0:1 + own]:
+            for j in range(3):
+                x0, x1 = max(512 * j, 1), 512 * j + 512
+                mm([[(P[:, x0:x1], I2[:], Ac[:, x0:x1]), (P[:, x0:x1], N2[:], Ac[:, x0 - 1:x1 - 1])]], 1024,
+                   [ak[j], ak[max(j - 1, 0)]] + mk, [bk[j]])
+                lin(D[:, x0 - 1:x1 - 1], P[:, x0:x1], 1.0, 0.0, 512, [], [bk[j], dk + str(j)])
+            mm([[(P[:, 0:1], I2[:], Ac[:, 0:1]), (P[:, 0:1], N2[:], Ac[:, B - 1:B])], [(P[:, 1:2], I2[:], Ac[:, 0:1])]], 192, ak + mk, [bk[0]])
+            lin(D[:, B - 1:B], P[:, 0:1], 1.0, 0.0, 1, [], [bk[0], dk + "3"])
+            lin(D[:, B:B + 1], P[:, 1:2], 1.0, A0, 1, [], [bk[0], dk + "4"])
+            if dk == "dr":
+                send("d", t, "ld%d" % t, D[:, 0:CUT[0]], (0, CUT[0]), 5.5 + t, ["dr0", "ship%d0" % (t - 1), "ship%d1" % (t - 1)], "ld%d0" % t)
+                send("h", t, "ld%d" % t, D[:, CUT[0]:CUT[1]], CUT, 6.0 + 2 * t, ["dr0", "dr1"], "ld%d1" % t)
+                send("e", t, "ld%d" % t, D[:, CUT[1]:MW], (CUT[1], MW), 3.5 + t, ["dr1", "dr2", "dr3", "dr4", "drz"], "ld%d2" % t)
+        if t - 1 in SHIP:
+            for c in range(NC // 2, NC):
+                ship(t - 1, c, T["X%d" % ((t - 1) % 2)], "X%d%d" % ((t - 1) % 2, c), ["senth%d" % t])
+        if t > 0:
+            output(t - 1)
+        dma(T.RB[0:128:16, :], T.bun[:, 96:192], 2.0, ["bh"], ["RBh"])
+        dma(T.RB[8:128:16, :], T.bun[:, 192:288], 2.0, ["bl"], ["RBl"])
+        for row, c0, k in ((0, 96, "h"), (8, 192, "l")):
+            dma([T.RX[row:112:16, :], T.RX[112 + row:113 + row, :]], [lb[16:128, c0:c0 + 96], lb[0:16, c0:c0 + 96]], 2.0,
+                ["lb%d" % t], ["RX" + k, "RX" + k.upper()])
+        mm([[(T.p6[:, 0:96], blk(T.MO, i), T.RB[:, i:B:16]) for i in range(16)],
+            [(T.p6[:, 96:97], T.M15[:], T.bun[:, c:c + 1]) for c in (95, 191, 287)]],
+           B + 192, ["MO", "M15", "RBh", "RBl", "bd", "bh", "bl"], ["b6"])
+        cp(T.offw[:, 0:96], T.p6[:, 0:96], 96, [], ["b6", "offw"])
+        ts(T.offw[:, 96:97], T.p6[:, 96:97], kc("cv"), None, ALU.add, None, 1, ["cv"], ["b6", "offw"])
+        if t < NB - 1:
+            ts(T.offs[:], T.p6[:, 0:96], float(S), None, ALU.min, None, 96, [], ["b6", "offs"])
+        merged = t in OPT["merge"]
+        for h in range(2):
+            gather((T.SS if merged else T.PM)[:, 768 * h:768 * h + 768], T.RX[:].indirect(T.mpu[:, 48 * h:48 * h + 48]), 768,
+                   ["RXh", "RXl", "RXH", "RXL", "mpu"], [("SS%d" if merged else "PM%d") % h])
+        if merged:
+            dma([T.SS[1:128:8, 1:B + 1], T.SS[12:128:16, 1:B + 1]], [T.SS[0:128:8, 0:B], T.bun[:, 0:96]], 2.0, ["bd"], ["SS0", "SS1"])
+        else:
+            dma(T.PM[:, JB:JB + B], T.PM[:, 0:B], 2.6, ["PM0", "PM1"], ["PM2"])
+            lin(T.PM[:, B:B + 1], T.PM[:, B - 1:B], 1.0, 0.0, 1, ["PM1"], ["PM3"])
+            lin(T.PM[:, TW - 1:TW], T.PM[:, B - 1:B], 1.0, 0.0, 1, ["PM1"], ["PM4"])
+            dma(T.SS[12:128:16, 1:B + 1], T.bun[:, 0:96], 2.0, ["bd"], ["SS0", "SS1"])
+        dma([T.W[:, 0:2056], T.W[:, 2056:4112]], [T.zero[:, 0:2056]] * 2, 3.2, ["zero"], ["W", "W2"])
+        cp(T.W[:, WP:WP + WW].indirect(T.offw[:, 0:97]), T.SS[:], MW * SCAT, ["offw", "SS0", "SS1"], ["W", "W2"])
+        for h, P, bk in ((0, T.p6, "b6"), (1, T.p7, "b7")):
+            w0 = WP + 2048 * h
+            mm([[(P[:, 0:128], blk(T.MI, i), T.W[:, w0 + i:w0 + 2048:16]) for i in range(16)]], 2048, ["MI", "W", "W2"], [bk])
+            c0 = 8 + 128 * h
+            lin(T.ph[:, c0:c0 + 128], P[:, 0:128], 1.0, 0.0, 128, [], [bk, "ph%d" % h])
+            mm([[(P[:, 128:256], T.Ir[:], T.ph[:, c0:c0 + 128]), (P[:, 128:256], T.Sr[:], T.ph[:, c0 - 1:c0 + 127]),
+                 (P[:, 128:256], T.N3r[:], T.W[:, w0 - 1:w0 + 2047:16])]], 384,
+               ["Ir", "Sr", "N3r", "ph0", "phz", "ph%d" % h, "W", "W2"], [bk])
+            scan(T.sb[:, 128 * h:128 * h + 128], P[:, 128:256], T.zero[:, 0:128], -1.0 if h == 0 else T.sb[:, 127:128], 128,
+                 ["zero", "sb0"] if h else ["zero"], [bk, "sb%d" % h])
+            cp(T.idxr[:, 128 * h:128 * h + 128], T.sb[:, 128 * h:128 * h + 128], 128, ["sb%d" % h], ["idxr%d" % h])
+            send("ij"[h], t, "li%d" % t, T.idxr[:, 128 * h:128 * h + 128], (128 * h, 128 * h + 128), 2.2, ["idxr%d" % h], "li%d%d" % (t, h))
+        if own or not merged:
+            P = T.p6[:, 256:512]
+            mm([[(P, T.Ih[:], T.ph[:, 8:264]), (P, T.Sh[:], T.ph[:, 7:263]), (P, T.N3[:], T.W[:, WP - 1:WP - 1 + S:16])]], 768,
+               ["Ih", "Sh", "N3", "ph0", "ph1", "phz", "W", "W2"], ["b6"])
+            scan(T.sa[:], P, T.zero[:, 0:256], -1.0, 256, ["zero"], ["b6", "sa"])
+            cp(T.idx[:], T.sa[:], 256, ["sa"], ["idx"])
+        mm([[(T.p7[:, 256:512], blk(T.ME, i), T.W[:, WP + i:WP + S:16]) for i in range(16)]], S, ["ME", "W", "W2"], ["b7"])
+        ac(T.pf[:, 4:260], T.p7[:, 256:512], AF.Identity, 256, [], ["b7", "pf"])
+        mm([[(T.p7[:, 0:256], T.If[:], T.pf[:, 4:260]), (T.p7[:, 0:256], T.Sf[:], T.pf[:, 3:259])]], 2048, ["If", "Sf", "pf"], ["b7"])
+        scan(T.se[:], T.p7[:, 0:256], T.c720[:], kc("ei"), 256, ["c720", "ei"], ["b7", "se"])
+        for h, G, gk in ((0, T.val, "val"), (1, T.GQ, "GQ"))[0:0 if merged else 2]:
+            for c in range(2):
+                gather(G[:, CH * c:CH * c + CH], T.PM[:].indirect(T.idx[:, 128 * h + 64 * c:128 * h + 64 * c + 64]), CH,
+                       ["PM%d" % k for k in range(6)] + ["idx"], [gk + str(c)] + ([gk] if c == 0 else []))
+            mm([[(T.p7[:, 256 + 128 * h:384 + 128 * h], blk(T.MO, i), G[:, i:2048:16]) for i in range(16)]], 2048,
+               ["MO", gk + "0", gk + "1"], ["b7"])
+        if merged:
+            cp(T.ea[:], T.se[:], 256, ["se"], ["ea"])
+        else:
+            tt(T.ea[:], T.se[:], T.p7[:, 256:512], ALU.add, 256, ["se"], ["b7", "ea"])
+        ts(T.eb[:], T.ea[:], S - 1, None, ALU.bitwise_and, None, 256, ["ea"], ["eb"])
+        cp(T["el%d" % t][:], T.eb[:], 256, ["eb"], ["el%d" % t])
+        tabs = [lambda: tables(T.TY, "TY", T.bun[:, 0:96], "bd", T.FD, T.GR, T.GC, T.BQ, "BQ", T.dif,
+                               [["df0"], ["df0", "df1"], ["df1", "df2", "df3", "df4"]]),
+                lambda: tables(T.TX, "TX", lb[:, 0:96], "lb%d" % t, T.FX, T.HR, T.HC, T.BR, "BR", ld, [["ld%d%d" % (t, j)] for j in range(3)])]
+        for k in OPT["tab"][t]:
+            if k == 1 or own:
+                tabs[k]()
+        samples(T.TX, "TX", li, ["li%d0" % t, "li%d1" % t], (0, 1) if own else (0, 1, 2, 3), X, "X%d" % (t % 2))
+        if own:
+            samples(T.TY, "TY", T.idx, ["idx", "idx"], (2, 3), T.Y, "Y")
+        else:
+            for c in range(NC // 2):
+                ship(t, c, X, XK[c], [])
+        if t < NB - 1:
+            ts(T.lv[:], T.of[:], float(S), None, ALU.is_lt, None, 96, ["of"], ["lv"])
+            tt(T.x1[:], T.bun[:, 0:96], T.lv[:], ALU.subtract, 96, ["bd", "lv"], ["x1"])
+            ac(T.z2[:], T.x1[:], AF.Relu, 96, ["x1"], ["z2"], bias=2.0, scale=-2.0)
+            tt(T.dn[:], T.x1[:], T.z2[:], ALU.add, 96, ["x1", "z2"], ["dn"])
+            ac(T.e1[:], T.bun[:, 0:96], AF.Abs, 96, ["bd"], ["e1"], bias=-3.0)
+            ac(T.e5[:], T.e1[:], AF.Relu, 96, ["e1"], ["e5"], bias=-32.0, scale=32.0)
+            if t > 0:
+                half(T.a1[:], T.a2[:], 1.0, -256.0, B, ak[0:3], ["a10", "a11", "a12"])
+                for j in range(3):
+                    x, sj = slice(512 * j, 512 * j + 512), str(j)
+                    mm([[(T.pB[:, x], T.Ib[:], T.V0[:, x]), (T.pB[:, x], T.I4[:], T.dead[:, x])]], 1024, ["Ib", "I4", "V0", "dead" + sj], [bB[j]])
+                    ac(T.zv[:, x], T.pB[:, x], AF.Relu, 512, [], [bB[j], "zv" + sj], bias=-192.0)
+            for h in range(2):
+                tt(T.cmp[:, 768 * h:768 * h + 768], X[:, 0:S + 1].indirect(T.offs[:, 48 * h:48 * h + 48]),
+                   (T.A if t == 0 else T.a1)[:, 768 * h:768 * h + 768], ALU.is_gt, 768 * GATH,
+                   XK + [Xe, "offs", "A", "a1%d" % h, "a1%d" % (h + 1)], ["cmp%d" % h])
+                mm([([(T.p6[:, 0:96], T.Nb[:], T.e5[:])] if h == 0 else []) +
+                    [(T.p6[:, 0:96], blk(T.MV, i), T.cmp[:, 96 * i:96 * i + 96]) for i in range(8 * h, 8 * h + 8)]], 768 + 96,
+                   ["MV", "Nb", "cmp%d" % h, "e5"], ["b6"], h == 0, h == 1)
+            ts(T.u2[:], T.p6[:, 0:96], 8.5, 2.0, ALU.is_ge, ALU.mult, 96, [], ["b6", "u2"])
+            tt(T.bun[:, 0:96], T.u2[:], T.dn[:], ALU.add, 96, ["u2", "dn"], ["bd"])
+            off = 145.0 * (t + 1)
+            for j in range(3):
+                x, sj = slice(512 * j, 512 * j + 512), str(j)
+                old = [(T.Ib, T.V0)] if t == 0 else [(T.Ih, T.uh), (T.Ib, T.zv)]
+                mm([[(T.pA[:, x], l[:], w[:, x]) for l, w in old]], 512 * len(old), ["Ib", "Ih", "V0", "uh" + sj, "zv" + sj], [bA[j]], True, False)
+                mm([[(T.pB[:, x], I1[:], Ac[:, x])]], 512, [ak[j]] + ak[3:], [bB[j]], True, False)
+                ac(T.fb[:, x], X[:, 0:S + 1].indirect(T.offs[:, 32 * j:32 * j + 32]), AF.Identity, 512 * GATH, XK + [Xe, "offs"], ["fb" + sj],
+                   bias=145.0 - 2047.5 / 4096, scale=1.0 / 16)
+                mm([[(T.pA[:, x], T.Ib[:], T.fb[:, x])]], 512, ["Ib", "fb" + sj], [bA[j]], False, True)
+                add({"dve": (lambda x=x: [v.tensor_scalar(T.dead[:, x], T.fb[:, x], -1.0, 0.0, ALU.mult, ALU.max)], 0.06 + 256 * CYC),
+                     "act": (lambda x=x: [a.activation(T.dead[:, x], T.fb[:, x], AF.Relu, scale=-1.0)], 0.07 + 512 * CYC)}, ["fb" + sj], ["dead" + sj])
+                ts(T.uh[:, x], T.pA[:, x], off - 64, off + 64, ALU.max, ALU.min, 512, [], [bA[j], "uh" + sj])
+                mm([[(T.pB[:, x], T.Ib[:], T.dead[:, x]), (T.pB[:, x], T.Ih[:], T.uh[:, x])]], 1024, ["Ib", "Ih", "dead" + sj, "uh" + sj],
+                   [bB[j]], False, True)
+                ac(T.a1[:, x], T.pB[:, x], AF.Abs, 512, [], [bB[j], "a1" + sj], bias=-(off + 256.0 * (t + 1)))
+                ac(T.a2[:, x], T.a1[:, x], AF.Abs, 512, ["a1" + sj], ["a2" + sj], bias=512.0, scale=-1.0)
+    output(NB - 1)
+    lastw, readers = {}, {}
+    for i, o in enumerate(ops):
+        d = set()
+        for k in o["r"]:
+            if k in lastw:
+                d.add(lastw[k])
+        for k in o["w"]:
+            if k in lastw:
+                d.add(lastw[k])
+            d.update(readers.get(k, []))
+        for k in o["r"]:
+            readers.setdefault(k, []).append(i)
+        for k in o["w"]:
+            lastw[k] = i
+            readers[k] = []
+        d.discard(i)
+        o["deps"] = sorted(d)
+    return ops
+
+
+ENG = {"dve": "dve", "act": "act", "pe": "pe", "pool": "g", "g": "g", "sp": "sp", "none": "none"}
+
+
+def order(ops, wake, par):
+    seed, delta, noise, bias = par
+    n = len(ops)
+    pri = [0.0] * n
+    x = seed * 7919 + 1
+    for i in range(n - 1, -1, -1):
+        o = ops[i]
+        pri[i] += min(c for _, c in o["alts"].values()) + o["lat"] + wake
+        for j in o["deps"]:
+            pri[j] = max(pri[j], pri[i])
+    for i in range(n):
+        x = (x * 1103515245 + 12345) % 2147483648
+        pri[i] += noise * (x / 2147483648.0)
+    left = [len(o["deps"]) for o in ops]
+    users = [[] for _ in ops]
+    for i, o in enumerate(ops):
+        for j in o["deps"]:
+            users[j].append(i)
+    fin, free, seq, rdy = [0.0] * n, {}, [], [0.0] * n
+    ready = [i for i in range(n) if left[i] == 0]
+    while ready:
+        cand = []
+        for i in ready:
+            al = ops[i]["alts"]
+            q = min((max(rdy[i], free.get(ENG[q], 0.0)) + c + (bias * c if q == "dve" else 0.0), q) for q, (_, c) in al.items())[1]
+            cand.append((max(rdy[i], free.get(ENG[q], 0.0)), i, q))
+        t1, _, q1 = min(cand)
+        st, i, q = max([c for c in cand if ENG[c[2]] == ENG[q1] and c[0] <= t1 + delta], key=lambda c: (pri[c[1]], -c[1]))
+        c = ops[i]["alts"][q][1]
+        if q != "none":
+            free[ENG[q]] = st + c
+        fin[i] = st + c + ops[i]["lat"]
+        seq.append((i, q))
+        ready.remove(i)
+        for u in users[i]:
+            left[u] -= 1
+            rdy[u] = max(rdy[u], fin[i] + wake)
+            if left[u] == 0:
+                ready.append(u)
+    return seq
+
+
+def decode(ops, text):
+    seq = []
+    for k in range(0, len(text), 2):
+        i, on_act = divmod((ord(text[k]) - 48) * 40 + ord(text[k + 1]) - 48, 2)
+        seq.append((i, "act" if on_act else list(ops[i]["alts"])[0]))
+    assert sorted(i for i, _ in seq) == list(range(len(ops)))
+    return seq
+
+
+def rank_program(g, core, T, topo):
+    if T.rank_of(core) is None:
+        helper_program(g, core, T, topo)
+        return
+    ops = build(g, core, T, topo, MODELS[0])
+    seq = decode(ops, ORDER) if ORDER else order(ops, MODELS[0][6], SEED)
+    queue = {"dve": g.vector, "act": g.scalar, "pe": g.tensor, "g": g, "sp": g.sync}
+    count = {"dve": 0, "act": 0, "pe": 0, "pool": 0}
+    waited = {}
+    total = {}
+    for i, q in seq:
+        o = ops[i]
+        if q != "none":
+            need = {}
+            for j in o["deps"]:
+                for s, n in ops[j]["tok"]:
+                    need[s] = max(need.get(s, 0), n)
+            for s, n in need.items():
+                if waited.get((ENG[q], s), 0) < n:
+                    queue[ENG[q]].wait_ge(T.sem[s], n)
+                    waited[(ENG[q], s)] = n
+            res = o["alts"][q][0]()
+            if q in count:
+                for ins in res:
+                    ins.then_inc(T.sem[q], 1)
+                    count[q] += 1
+                o["tok"] = [(q, count[q])]
+        for s, n in o["tok"]:
+            total[s] = max(total.get(s, 0), n)
+    for s, n in total.items():
+        if waited.get(("g", s), 0) < n:
+            g.wait_ge(T.sem[s], n)

@@ -4,45 +4,81 @@ S, B, NB, N = 4096, 1536, 3, 8
 CH = 1024
 NC = S // CH
 JB = 1544
-TW = JB + 1 + B
-WP, WW = 16, 7712
-CUT = (504, 1016)
-MW = 1552
+TW = JB + B + 8
+WW = 7712
+AW = B + 8
 F32, BF, F16, I32, U16 = "float32", "bfloat16", "float16", "int32", "uint16"
 
 SCRATCH = {}
 for _d, _w, _names in (
-        (BF, B, "A V0 RB RX cmp fb dead zv"), (F16, B, "uh a1 a2"), (F16, MW, "dif difx"), (BF, MW, "SS"), (BF, TW, "PM"),
-        (I32, 96, "dui mpi"), (F32, 4, "gn OJ OQ"), (U16, 96, "mpu dl offs"), (U16, 98, "offw"), (U16, 256, "idx idxr el0 el1 el2"),
-        (F32, 48, "K"), (F32, 16, "OH"), (I32, 16, "pi"),
-        (BF, 128, "qrow gq Ib Nb I4 N3 N3r M15 Irb Nrb"), (F16, 128, "Ih Nh Sh Ir Nr Sr"), (F32, 128, "If Sf Lf t1 t2 t3"),
-        (BF, 2048, "val GQ MV MO MI ME"), (BF, 512, "BQ BR"), (BF, 384, "FD FX GR GC HR HC"),
-        (BF, 2064, "zero"), (F32, 256, "c720 sa sb se"), (I32, 256, "ea eb"), (BF, WP + WW, "W"),
-        (BF, 288, "bun"), (F32, 100, "inc"), (F32, 96, "of"), (BF, 96, "lv x1 z2 dn e1 e5 u2"),
-        (F16, 264, "ph"), (F32, 260, "pf"), (F32, TW, "TY TX"), (F32, S + 8, "X0 X1"), (F32, S, "Y DX Z"),
-        (BF, 288, "lb0 lb1 lb2"), (F16, MW, "ld0 ld1 ld2"), (U16, 256, "li0 li1 li2")):
+        (BF, B, "V0 RX RD RR cmp fb zv uh"), (F16, B, "a1"), (BF, AW, "A la0 PM PT"), (F16, AW, "a2 la1 la2"), (BF, 2 * B, "RC"),
+        (I32, 96, "dui dur mpi"), (F32, 4, "gn yl"), (U16, 96, "mpu dl offs"), (U16, 98, "offw lo0 lo1 lo2"), (U16, 256, "idx el0 el1 el2"),
+        (U16, 384, "lst ll0 ll1 ll2"), (F32, 32, "K"), (F32, 16, "OH"), (I32, 16, "pi"),
+        (BF, 128, "Nb I32 Nrb Z1 Z2 Z3 Z4 t2 t3"), (F16, 128, "T1 T2 Ih Nh Irh Nrh"), (BF, 384, "C Cr rp"), (F32, 384, "F Fr"),
+        (BF, 144, "MV UB VB"), (F32, 128, "Lf t1"), (BF, 256, "qrow c45 mask"), (F16, 256, "Ej"), (BF, 2048, "G ones"), (BF, CH, "zero"),
+        (BF, 64, "c16"), (BF, 104, "dr"), (F32, 256, "sa vm Dg"), (I32, 256, "ea eb"), (BF, WW, "W0 W1"),
+        (BF, 192, "bun0 bun1 lb0 lb1 lb2"), (BF, 384, "Ro lr0 lr1 lr2"), (BF, 768, "Rb"), (BF, 512, "Q Qr"), (BF, 128, "q4"), (BF, 200, "dd lv x1 z2 dn e1 e5 u2"), (F32, 100, "inc orot"), (F32, 200, "of"),
+        (F16, 264, "ph"), (F32, TW, "TY TX"), (F32, S + 8, "X0 X1"), (F32, S, "Y DX Z")):
     for _n in _names.split():
         SCRATCH[_n] = ("sbuf", [128, _w], _d)
 for _n, _w in (("pA", B), ("pB", B), ("p6", 512), ("p7", 512)):
     SCRATCH[_n] = ("psum", [128, _w], F32)
 
 SIM = 64
-SHIP = (0, 1)
-NDMA = 64
+BACK = ("ffnn", "ffnn", "----")
+RELAY = (1, 2)
+STAGE = ("Y", "Z", "DX")
+NDMA = 56
 SEMAPHORES = ["pe", "dve", "act", "pool", "hs"] + ["q%d" % i for i in range(NDMA)]
 for _t in range(NB):
-    for _m in "bdehij":
+    for _m in "obrdefl":
         SEMAPHORES += ["s%s%d" % (_m, _t), "r%s%d" % (_m, _t)]
-for _t in SHIP:
     SCRATCH["yd%d" % _t] = ("dram", [NC, 128, CH], F32)
     for _c in range(NC):
         SEMAPHORES += ["sy%d%d" % (_t, _c), "ry%d%d" % (_t, _c)]
+FIRST = 0
+V, A_ = "dve", "act"
 
-MODELS = [(0.00104, 0.0007, 1.55, 3.8, 1.0, 1.0, 0.12), (0.0009, 0.0009, 1.2, 2.5, 1.2, 1.4, 0.15),
-          (0.0011, 0.0005, 1.9, 5.0, 0.8, 0.9, 0.1)]
-OPT = {"merge": (2,), "tab": ((0, 1), (0, 1), (1, 0)), "lat": (18.0, 25.0, 12.0, 18.0)}
-ORDER = "0:000B020<0406080>0D4;4P700J4I0T1C0H150N13441=4T1?534V4J0S1;1A1E171O4=1H0@4N2B2I3:50461J54321L393<372N570F2E586V3R5:2F0L5F5<5>6<5@5J3T6>5B4R2J5N2S5I5M600V5D0P102Q26641Q2>6D5P1S291U3Q2:3M621W2<232@21185R3E666F3I8H6H255U726B5W6@41683?3A3W2W4M1G4?4C4E6::38U8K8V6M8L6O496P6S6U6J979R:574423531902U4G3C8N3K3G7B2L773O4A92787E9T7F7:9W7<7P7H7>7J7V7R7L7T94877@8P7N8R98:B81>P88829;:0:D848?:V9>8:9C9<:T;>;@9@9J9G9D9N8=9H9L:6:G8@;19P:::8:K:H;C8B:<:L;5;2:>:@:N;G;P>N;6AS;R:Q;T;8;V>4:S<0;DAJ>6<2;;AL<6;H;=8D8F<9<4<:AO<HAU><<<AP<L;J<J>>@@>@>:>R>8;M<N=0<T;O<B<><E@M<G@N<A@C<P>E=2@D<V<R>G>B@P>T>H>K>M@FAV=4?:>W@R@H?0?=@W?>?2?H?@?4?B?N?6?J?D?L@T@1@J?8?FA0?V@5B4G8B0A2?QA;?R=>=H=6B8A7A4A??TABA8@2B7A<AF@7C2=RA@C4AD@8B<C7B3AHB@B>CIC8B;@:BBC<BMBHBDBFC;CVI6CLD0BQBND2D4FLC>D6BRD8FNBJCA@<BT=TCCCFD:BWCDC1=J=9D@D<FRFPDCHD@>CJD?FTCNI9DRICDNCPG5G2EHDTE2DPED=@CSG6E6CUE5DDFVE9G0DHG:E:DKDMEJDGE>EF=;DVHQ=<HGE0E=HHEAEC=CHR=EELHJGJ=W=FHTHLIMG<GM=MHNENI3I:G?>1G@EV=OGN>2GBH0GPHVH6EQGD=PI<GFH2I>ESI0GHGRI4GTH4IDH9I@ETF8H:IFGVIQF0IUIHFBH<IRF3IJF5IVINF6FDJ9H>J=J0J5F:FGJ2FIJ6F=FJH@J:F?HBJ>JAF@JHJEJBJKK0JMJFK3JNJPK5K6K8JSJTK;JVK<K>"
-SEED = (0, 0.35, 0.0, 2.0)
+PLAN = """
+sums_matrix, first_lists, onset_sums 0, onset_list 0, const_blocks, own_sums, rows 1 v, send_onsets 0, send_amp 0 1, const_back,
+own_list, rows 0 a, blocks, const_dead, blocks_out, ramps 0, send_amp 0 0, const_quarters 0, ramp_sum 0, send_rates 0, first_ones,
+block_scan, block_sum, amp_turn 0 0, const_counts, const_even, block_parts 0, live, const_walk, diffs 0 0, amp_table 0 0 a, clear_rows,
+dead_sum 0, send_amp 0 2, rate_rows 0, dead_sum 1, diffs 0 1, marks 0 0, lower, marks 0 1, amp_turn 0 2, dead 1 a, slopes 0, dead 0 a,
+edge, count 0 0, amp_table 0 2 a, slopes 1, bounce, count_out 0 a, amp_turn 0 1, amp_table 0 1 a, diffs 0 2, slopes 2, count 0 1,
+send_blocks 0, onset_rows 0, count_sums 0, count 0 2, count_out 1 a, places 0, count_out 2 v, steps 0 0 a, count_sums 1, places 1,
+steps 1 1 a, mp_list, count 0 3, count_out 3 v, count_sums 2, places 2, steps 2 2 a, votes_open 1, count_sums 3, places 3, named 1 a,
+samples 0 0 0, open_a 0 0, steps 3 3 v, list_back, samples 0 1 1, const_half, samples 0 2 2, ship 0 0, dead_sum 2, list_out, dead 2 a,
+open_v 0 2, more_ones, fill 1, open_a 0 1, open_v 0 0, open_a 0 2, samples 0 3 3, force 0 0 v, force 0 1 a, own_rows 0, own_last,
+compare 0 0, open_v 0 1, send_list 0, force 0 2 a, add_force 0, velocity 0 0, votes_open 0, compare 0 1, add_force 1, named 0 a,
+velocity 0 1, votes 0 0, fallen, add_velocity 0, reflect 0 0, send_amp 1 0, ship 0 1, add_force 2, votes 0 1, votes 1 0, durations 0,
+velocity 0 2, add_velocity 1, named_rows, onset_sums 1, onset_list 1, reflect 0 1, send_onsets 1, add_velocity 2, votes 1 1,
+durations 1, block_scan, send_amp 1 1, block_sum, block_parts 1, send_blocks 1, ship 0 2, reflect 0 2, ship 0 3, edge, ramps 0,
+send_amp 1 2, evens 0 0 a, own_sums, const_late, own_list, marks 1 0, onset_rows 1, odd_marks 0, amplitudes a, evens 0 1 v, marks 1 1,
+ramp_sum 0, amp_turn 1 1, count 1 0, const_positions, live, send_rates 1, diffs 1 0, amp_turn 1 0, const_quarters 1, position_sums 0,
+rate_rows 1, count_out 0 a, positions 0, count_sums 0, places 0, amp_table 1 0 a, diffs 1 2, slopes 2, diffs 1 1, amp_table 1 1 a,
+slopes 0, count 1 1, count_out 1 a, amp_turn 1 2, count 1 2, slopes 1, count_sums 1, places 1, fetch 0 1, fetch 0 0, amp_table 1 2 a,
+count 1 3, count_out 2 v, count_sums 2, votes_open 1, count_out 3 v, count_sums 3, places 2, places 3, steps 0 0 a, samples 1 0 0,
+open_v 1 0, steps 1 1 a, steps 3 3 v, list_back, steps 2 2 a, open_a 1 0, samples 1 1 1, list_out, ship 1 0, open_a 1 1, named 1 a,
+open_v 1 1, samples 1 2 2, samples 1 3 3, compare 1 0, open_v 1 2, votes_open 0, lower, force 1 0 a, add_force 0, force 1 1 a,
+compare 1 1, velocity 1 0, named 0 a, fetch 0 3, bounce, votes 0 0, force 1 2 a, named_rows, add_force 1, votes 0 1, velocity 1 1,
+add_velocity 1, fallen, fill 2, add_force 2, durations 0, reflect 1 1, onset_sums 2, onset_list 2, own_rows 1, fetch 0 2,
+add_velocity 0, reflect 1 0, send_list 1, odd_marks 1, velocity 1 2, send_onsets 2, votes 1 0, votes 1 1, own_last, evens 1 1 a,
+ship 1 1, durations 1, ramps 1, ramps 0, product 0 2, send_amp 2 1, block_scan, open_a 1 2, add_velocity 2, product 0 0, send_amp 2 0,
+reflect 1 2, tanh 0 2, block_sum, send_amp 2 2, ramp_sum 0, tanh 0 0, amp_turn 2 1, ramp_sum 1, product 0 3, evens 1 0 a, tanh 0 3,
+send_rates 2, ramp_sum 2, diffs 2 2, diffs 2 1, amp_turn 2 2, gain 0 0 a, rate_rows 2, marks 2 0, amp_table 2 2 a, block_parts 2,
+diffs 2 0, amp_turn 2 0, amp_table 2 0 a, ship 1 2, count 2 0, count_out 0 a, marks 2 1, product 0 1, amp_table 2 1 a, count 2 1,
+count_out 1 a, count 2 2, count_out 2 a, send_blocks 2, count_sums 0, places 0, count 2 3, slopes 1, own_rows 2, tanh 0 1, gain 0 1 a,
+count_sums 2, count_out 3 v, count_sums 3, slopes 2, slopes 0, count_sums 1, places 1, places 2, steps 0 0 a, onset_rows 2, fetch 1 0,
+steps 2 2 a, gain 0 3 v, position_sums 1, own_rates, named 0 v, store 0 1, named 1 a, named_rows, gain 0 2 a, samples 2 0 0, places 3,
+positions 1, own_diffs 0, store 0 0, own_table 0, steps 1 1 a, steps 3 3 a, list_back, fetch 1 2, list_out, product 1 0, own_diffs 1,
+tanh 1 0, own_table 1, own_diffs 2, samples 2 1 1, ship 1 3, samples 2 2 2, send_list 2, own_table 2, gain 1 0 a, own_last,
+evens 2 0 a, own_table 3, own_ends, fetch 1 1, evens 2 1 a, store 0 3, own_steps 0 0 a, product 1 1, tanh 1 1, store 1 0, product 1 2,
+samples 2 3 3, tanh 1 2, gain 1 1 a, odd_marks 2, position_sums 2, own_samples 0 0, store 0 2, fetch 1 3, positions 2, own_steps 2 2 a,
+own_steps 1 1 a, product 2 0, product 1 3, gain 1 2 a, own_steps 3 3 a, store 1 1, tanh 1 3, store 1 2, gain 1 3 a, store 1 3,
+own_samples 1 1, own_samples 2 2, tanh 2 0, gain 2 0 a, store 2 0, product 2 1, tanh 2 1, gain 2 1 a, store 2 1, own_samples 3 3,
+product 2 3, product 2 2, tanh 2 3 0, gain 2 3 v 0, store 2 3 0, tanh 2 3 1, gain 2 3 v 1, store 2 3 1, tanh 2 2, gain 2 2 a,
+store 2 2
+"""
 
 
 def bits(m):
@@ -55,559 +91,715 @@ def helper_of(c, topo):
     return other[mine.index(c)]
 
 
-def relayed(src, dst, T, topo):
-    h = helper_of(src, topo)
-    return topo.chip(src) != topo.chip(dst) and T.rank_of(h) is None and topo.may_write(h, dst)
-
-
-def engines(src, dst, part, topo):
+def engines(src, dst, part, T, topo):
     e = topo.engines(src, dst)
-    if part is not None:
+    if T.rank_of(src) is not None and topo.chip(src) == topo.chip(dst):
         e = e[part * len(e) // 2:(part + 1) * len(e) // 2]
     return sum(1 << k for k in e)
 
 
-def remote(g, T, topo, src, dst, out, in_, rsem, lsem, part=None):
+def remote(g, T, topo, src, dst, out, in_, rsem, lsem, part):
     rid, pid, _ = topo.addr(dst)
-    g.remote_dma(out, in_, T.sem[rsem], T.sem[lsem], pid, rid, engines(src, dst, part, topo))
+    g.remote_dma(out, in_, T.sem[rsem], T.sem[lsem], pid, rid, engines(src, dst, part, T, topo))
 
 
-def way(src, dst, c, T, topo):
-    if not relayed(src, dst, T, topo):
-        return [src, dst]
+def way(src, dst, t, c, T, topo):
     h = helper_of(src, topo)
+    if topo.chip(src) == topo.chip(dst) or BACK[t][c] == "s" or T.rank_of(h) is not None or not topo.may_write(h, dst):
+        return [src, dst]
     far = [f for f in range(SIM) if topo.mates(topo.chip(f), topo.chip(dst)) and topo.may_write(h, f) and topo.may_write(f, dst)
            and topo.die(f) == topo.die(h)]
-    if c < NC // 2 and far:
+    if BACK[t][c] == "f" and far:
         return [src, h, far[T.rank_of(src) % len(far)], dst]
     return [src, h, dst]
 
 
-def helper_program(g, core, T, topo):
-    sent = [0]
+def relay(src, t, T, topo):
+    dst, mine = T.cores[(T.rank_of(src) - 1 - t) % N], [k for k in T.cores if topo.chip(k) == topo.chip(src)]
+    if t not in RELAY or topo.chip(src) == topo.chip(dst):
+        return None
+    k = mine.index(src)
+    return helper_of(mine[k % 2], topo), slice(512 * (k // 2), 512 * (k // 2) + 512), "r%s%d" % ("de"[k // 2], t), dst
 
-    def back(t, chunks):
-        for c in chunks:
+
+def helper_program(g, core, T, topo):
+    sent = 0
+    for t in RELAY:
+        for src in T.cores:
+            h, x, sem, dst = relay(src, t, T, topo) or [None] * 4
+            if h == core:
+                g.wait_ge(T.sem[sem], bits(engines(src, core, 0, T, topo)))
+                remote(g, T, topo, core, dst, T["la%d" % t][:, 0:512], T["la%d" % t][:, x], "rd%d" % t, "hs", 0)
+                sent += bits(engines(core, dst, 0, T, topo))
+    for t in range(NB):
+        for c in range(NC):
             for r in range(N):
-                w = way(T.cores[r], T.cores[(r + 1 + t) % N], c, T, topo)
-                if core in w:
+                w = way(T.cores[r], T.cores[(r + 1 + t) % N], t, c, T, topo)
+                if core in w and BACK[t][c] != "-":
                     k = w.index(core)
-                    stage = T["YZ"[t]][:, CH * c:CH * c + CH]
-                    g.wait_ge(T.sem["q%d" % (NC * t + c)], bits(engines(w[k - 1], core, 1, topo)))
+                    stage = T[STAGE[t]][:, CH * c:CH * c + CH]
+                    g.wait_ge(T.sem["q%d" % (NC * t + c)], bits(engines(w[k - 1], core, 1, T, topo)))
                     if k + 2 == len(w):
                         remote(g, T, topo, core, w[k + 1], T["yd%d" % t][c], stage, "ry%d%d" % (t, c), "hs", 1)
                     else:
                         remote(g, T, topo, core, w[k + 1], stage, stage, "q%d" % (NC * t + c), "hs", 1)
-                    sent[0] += bits(engines(core, w[k + 1], 1, topo))
-
-    for t in range(NB):
-        for c in T.cores:
-            dst = T.cores[(T.rank_of(c) - 1 - t) % N]
-            if helper_of(c, topo) == core and relayed(c, dst, T, topo):
-                for m, x0, x1 in (("d", 0, CUT[0]), ("h", CUT[0], CUT[1])):
-                    part = T["ld%d" % t][:, x0:x1]
-                    g.wait_ge(T.sem["r%s%d" % (m, t)], bits(topo.mask(c, core)))
-                    remote(g, T, topo, core, dst, part, part, "r%s%d" % (m, t), "hs", 0)
-                    sent[0] += bits(engines(core, dst, 0, topo))
-        if t - 1 in SHIP:
-            back(t - 1, range(NC // 2, NC))
-        if t in SHIP:
-            back(t, range(NC // 2))
-    if sent[0]:
-        g.wait_ge(T.sem["hs"], sent[0])
-
-
-def build(g, core, T, topo, model):
-    CYC, PCY, GATH, SCAT, DS, RS, _ = model
-    r = T.rank_of(core)
-    ops = []
-    ndma = [0]
-    v, a, pe = g.vector, g.scalar, g.tensor
-
-    def add(alts, reads, writes, lat=0.0, tok=None):
-        ops.append({"alts": alts, "r": list(reads), "w": list(writes), "lat": lat, "tok": tok})
-
-    def dve(fn, n, reads, writes):
-        add({"dve": (fn, 0.06 + max(n, 64) * CYC)}, reads, writes)
-
-    def act(fn, n, reads, writes):
-        add({"act": (fn, 0.07 + max(n, 64) * CYC)}, reads, writes)
-
-    def either(fv, fa, n, reads, writes):
-        add({"dve": (fv, 0.06 + max(n, 64) * CYC), "act": (fa, 0.07 + max(n, 64) * CYC)}, reads, writes)
-
-    def pool(fn, n, writes):
-        add({"pool": (fn, 0.13 + 2 * n * CYC)}, [], writes)
-
-    def ts(out, in0, s1, s2, op0, op1, n, reads, writes):
-        if op1 is None:
-            dve(lambda: [v.tensor_scalar(out, in0, s1, None, op0)], n, reads, writes)
-        else:
-            dve(lambda: [v.tensor_scalar(out, in0, s1, s2, op0, op1)], n, reads, writes)
-
-    def tt(out, in0, in1, op, n, reads, writes):
-        dve(lambda: [v.tensor_tensor(out, in0, in1, op)], n, reads, writes)
-
-    def cp(out, in_, n, reads, writes):
-        dve(lambda: [v.tensor_copy(out, in_)], n, reads, writes)
-
-    def ms(out, c, n, writes):
-        dve(lambda: [v.memset(out, c)], n, [], writes)
-
-    def scan(out, d0, d1, ini, n, reads, writes):
-        dve(lambda: [v.tensor_tensor_scan(out, d0, d1, ini, ALU.add, ALU.add)], n, reads, writes)
-
-    def ac(out, in_, f, n, reads, writes, bias=0.0, scale=1.0):
-        act(lambda: [a.activation(out, in_, f, bias=bias, scale=scale)], n, reads, writes)
-
-    def lin(out, in_, scale, bias, n, reads, writes):
-        either(lambda: [v.tensor_scalar(out, in_, scale, bias, ALU.mult, ALU.add)],
-               lambda: [a.activation(out, in_, AF.Identity, bias=bias, scale=scale)], n, reads, writes)
-
-    def half(out, in_, scale, bias, n, reads, writes):
-        add({"dve": (lambda: [v.tensor_scalar(out, in_, scale, bias, ALU.mult, ALU.add)], 0.06 + n * CYC / 2),
-             "act": (lambda: [a.activation(out, in_, AF.Identity, bias=bias, scale=scale)], 0.07 + n * CYC)}, reads, writes)
-
-    def mm(groups, n, reads, writes, start=True, stop=True):
-        def fn():
-            last = []
-            for grp in groups:
-                for i, (o, l, x) in enumerate(grp):
-                    ins = pe.matmul(o, l, x, start and i == 0, stop and i == len(grp) - 1)
-                last.append(ins)
-            return last
-        add({"pe": (fn, 0.06 + n * PCY)}, reads, writes)
-
-    def dma(out, in_, lat, reads, writes, acc=False):
-        s = "q%d" % ndma[0]
-        ndma[0] += 1
-        if acc:
-            add({"g": (lambda: g.dma_start(out, in_, accum_op=ALU.add).then_inc(T.sem[s], 16), 0.6)}, reads, writes, lat * DS, [(s, 16)])
-        else:
-            pairs = list(zip(out, in_)) if isinstance(out, list) else [(out, in_)]
-            add({"sp": (lambda: [g.sync.dma_start(o, i).then_inc(T.sem[s], 16) for o, i in pairs], 0.08 * len(pairs))}, reads, writes,
-                lat * DS, [(s, 16 * len(pairs))])
-
-    def send(m, t, buf, src_ap, cols, lat, reads, land):
-        dst, src = T.cores[(r - 1 - t) % N], T.cores[(r + 1 + t) % N]
-        out = T[buf][:, cols[0]:cols[1]]
-        to, rs = dst, "r%s%d" % (m, t)
-        if m in "dh" and relayed(core, dst, T, topo):
-            to = helper_of(core, topo)
-        got = topo.mask(src, core)
-        if m in "dh" and relayed(src, core, T, topo):
-            got = engines(helper_of(src, topo), core, 0, topo)
-        key = "sent" + m + str(t)
-        add({"g": (lambda: remote(g, T, topo, core, to, out, src_ap, rs, "s%s%d" % (m, t)), 0.4 * RS)}, reads, [key], 1.0 * RS,
-            [("s%s%d" % (m, t), bits(topo.mask(core, to)))])
-        add({"none": (None, 0.0)}, [key], [land], lat * RS, [(rs, bits(got))])
-
-    def ship(t, c, X, xk, after):
-        w = way(core, T.cores[(r + 1 + t) % N], c, T, topo)
-        wi = way(T.cores[(r - 1 - t) % N], core, c, T, topo)
-        x = slice(CH * c, CH * c + CH)
-        out, rs = (T["yd%d" % t][c], "ry%d%d" % (t, c)) if len(w) == 2 else (T["YZ"[t]][:, x], "q%d" % (NC * t + c))
-        key, ls = "ship%d%d" % (t, c), "sy%d%d" % (t, c)
-        add({"g": (lambda: remote(g, T, topo, core, w[1], out, X[:, x], rs, ls, 1), 0.4 * RS)}, [xk] + after, [key], 3.0 * RS,
-            [(ls, bits(engines(core, w[1], 1, topo)))])
-        add({"none": (None, 0.0)}, [key], ["yd%d%d" % (t, c)], OPT["lat"][c] * RS, [("ry%d%d" % (t, c), bits(engines(wi[-2], core, 1, topo)))])
-
-    K, OH = T.K, T.OH
-    kn = {}
-
-    def kc(name):
-        if name not in kn:
-            kn[name] = len(kn)
-        return K[:, kn[name]:kn[name] + 1]
-
-    def oh(j):
-        return OH[:, j:j + 1]
-
-    def col(name, in0, s1, s2, op0, op1, reads):
-        ts(kc(name), in0, s1, s2, op0, op1, 1, reads, [name])
-
-    def lc(name, in_, scale, bias, reads):
-        lin(kc(name), in_, scale, bias, 1, reads, [name])
-
-    def blk(M, i):
-        return M[:, 128 * i:128 * i + 128]
-
-    dma(T.dui[:], T.du[:], 2.2, [], ["dui"])
-    dma(T.A[:], T.am[:], 2.8, [], ["A"])
-    dma(T.mpi[:], T.mp[:], 2.2, [], ["mpi"])
-    dma(T.V0[:], T.ve[:], 2.8, [], ["V0"])
-    dma(T.gn[:, 0:3], T.gain[:], 2.2, [], ["gn"])
-    pool(lambda: [g.iota(T.pi[:, 0:1], [[0, 1]], 0, 1)], 1, ["pi0"])
-    pool(lambda: [g.iota(T.qrow[:], [[1, 128]], 0, 0, allow_small_or_imprecise_dtypes=True)], 128, ["qrow"])
-    pool(lambda: [g.iota(T.val[:], [[-1, 16], [32, 8], [1, 16]], 0, 0, allow_small_or_imprecise_dtypes=True)], 2048, ["val"])
-    pool(lambda: [g.iota(T.gq[:], [[1, 8], [0, 16]], 0, 0, allow_small_or_imprecise_dtypes=True)], 128, ["gq"])
-    ms(T.zero[:], 0.0, 1032, ["zero"])
-    ts(T.pi[:, 4:5], T.pi[:, 0:1], 15, None, ALU.bitwise_and, None, 1, ["pi0"], ["pi4"])
-    ts(T.pi[:, 8:9], T.pi[:, 0:1], 3, None, ALU.bitwise_and, None, 1, ["pi0"], ["pi8"])
-    cp(kc("p"), T.pi[:, 0:1], 1, ["pi0"], ["p"])
-    cp(kc("r"), T.pi[:, 4:5], 1, ["pi4"], ["r"])
-    cp(kc("j"), T.pi[:, 8:9], 1, ["pi8"], ["j"])
-    col("s", kc("p"), kc("r"), 2.0, ALU.subtract, ALU.mult, ["p", "r"])
-    col("q", kc("r"), kc("j"), 0.25, ALU.subtract, ALU.mult, ["r", "j"])
-    lc("g", kc("s"), 1.0 / 32, 0.0, ["s"])
-    ts(OH[:], T.qrow[:, 0:16], kc("r"), None, ALU.is_equal, None, 16, ["qrow", "r"], ["OH"])
-    ts(T.OJ[:], T.qrow[:, 0:4], kc("j"), None, ALU.is_equal, None, 4, ["qrow", "j"], ["OJ"])
-    ts(T.OQ[:], T.qrow[:, 0:4], kc("q"), 1.0 / 256, ALU.is_equal, ALU.mult, 4, ["qrow", "q"], ["OQ"])
-    lc("wO", oh(0), 1.0, oh(8), ["OH"])
-    lc("one", oh(2), 1.0, oh(3), ["OH"])
-    lc("w1", oh(12), -45.0, kc("wO"), ["OH", "wO"])
-    col("w2", kc("w1"), oh(1), oh(9), ALU.subtract, ALU.subtract, ["OH", "w1"])
-    lc("thr", oh(3), -7.5, 8.0, ["OH"])
-    lc("b1", kc("s"), -1.0, -7.5, ["s"])
-    lc("beta", oh(3), 7.5, kc("b1"), ["b1", "OH"])
-    lc("wi", oh(3), float(JB), oh(2), ["OH"])
-    lc("c1", kc("r"), 1.0, 7690.0, ["r"])
-    lc("cv", oh(1), -7690.0, kc("c1"), ["c1", "OH"])
-    lc("ei", kc("r"), 45.0, -720.0, ["r"])
-    col("p1", kc("p"), 16.0, 128.0, ALU.is_lt, ALU.mult, ["p"])
-    col("pr", kc("p1"), kc("p"), -16.0, ALU.add, ALU.add, ["p1", "p"])
-    col("gr", kc("pr"), kc("r"), 1.0 / 16, ALU.subtract, ALU.mult, ["pr", "r"])
-    lc("n3", oh(3), -float(JB), 0.0, ["OH"])
-    lc("kn", kc("j"), 1.0, -5.0, ["j"])
-    for nm, sl, b0 in (("R", (13.0, 8.0, 22.0, 85.0), 51.0), ("C", (12.0, 10.0, 20.0, 86.0), 52.0)):
-        lc(nm + "0", T.OJ[:, 0:1], -sl[0], 0.0, ["OJ"])
-        for j in (1, 2, 3):
-            lc(nm + str(j), T.OJ[:, j:j + 1], -sl[j], kc(nm + str(j - 1)), ["OJ", nm + str(j - 1)])
-        lc(nm + "a", T.OJ[:, 0:1], b0, 0.0, ["OJ"])
-        lc(nm + "b", kc("kn"), kc(nm + "3"), kc(nm + "a"), ["kn", nm + "3", nm + "a"])
-    ts(T.MV[:], T.val[:], kc("s"), None, ALU.is_equal, None, 1024, ["val", "s"], ["MV"])
-    half(T.MO[:], T.MV[:], kc("wO"), 0.0, 2048, ["MV", "wO"], ["MO"])
-    ts(T.M15[:], blk(T.val, 1), kc("s"), oh(15), ALU.is_equal, ALU.mult, 64, ["val", "s", "OH"], ["M15"])
-    ac(T.ME[:], T.val[:], AF.Abs, 2048, ["val", "beta"], ["ME"], bias=kc("beta"))
-    ts(T.MI[:], T.ME[:], kc("thr"), kc("wi"), ALU.is_lt, ALU.mult, 1024, ["ME", "thr", "wi"], ["MI"])
-    ts(T.ME[:], T.ME[:], kc("thr"), kc("w2"), ALU.is_lt, ALU.mult, 1024, ["ME", "thr", "w2"], ["ME"])
-    ts(T.If[:], T.qrow[:], kc("p"), None, ALU.is_equal, None, 128, ["qrow", "p"], ["If"])
-    for name, w in (("Ib", 1.0), ("Nb", -1.0), ("I4", 4.0), ("Ih", 1.0), ("Nh", -1.0)):
-        lin(T[name][:], T.If[:], w, 0.0, 128, ["If"], [name])
-    ts(T.Ir[:], T.qrow[:], kc("pr"), None, ALU.is_equal, None, 64, ["qrow", "pr"], ["Ir"])
-    for name, w in (("Nr", -1.0), ("Irb", 1.0), ("Nrb", -1.0)):
-        lin(T[name][:], T.Ir[:], w, 0.0, 128, ["Ir"], [name])
-    ts(T.t3[:], T.gq[:], kc("g"), None, ALU.is_equal, None, 128, ["gq", "g"], ["t3"])
-    ts(T.t2[:], T.gq[:], kc("gr"), None, ALU.is_equal, None, 128, ["gq", "gr"], ["t2"])
-    lin(T.N3[:], T.t3[:], kc("n3"), 0.0, 128, ["t3", "n3"], ["N3"])
-    lin(T.N3r[:], T.t2[:], kc("n3"), 0.0, 128, ["t2", "n3"], ["N3r"])
-    for q in range(4):
-        lin(blk(T.BQ, q), T.t3[:], T.OQ[:, q:q + 1], 0.0, 128, ["t3", "OQ"], ["BQ%d" % q])
-        lin(blk(T.BR, q), T.t2[:], T.OQ[:, q:q + 1], 0.0, 128, ["t2", "OQ"], ["BR%d" % q])
-    lin(T.t1[:], T.t3[:], oh(15), 0.0, 128, ["t3", "OH"], ["t1"])
-    tt(T.Sf[:], T.t1[:], T.If[:], ALU.subtract, 256, ["t1", "If"], ["Sf"])
-    lin(T.Sh[:], T.Sf[:], 1.0, 0.0, 128, ["Sf"], ["Sh"])
-    lin(T.t1[:], T.t2[:], oh(15), 0.0, 128, ["t2", "OH"], ["t1"])
-    tt(T.Sr[:], T.t1[:], T.Ir[:], ALU.subtract, 256, ["t1", "Ir"], ["Sr"])
-    ts(T.Lf[:], T.qrow[:], kc("p"), None, ALU.is_gt, None, 128, ["qrow", "p"], ["Lf"])
-    tt(T.Lf[:], T.Lf[:], T.t3[:], ALU.mult, 256, ["Lf", "t3"], ["Lf"])
-    lin(T.c720[:], T.zero[:, 0:256], 0.0, 720.0, 256, ["zero"], ["c720"])
-    lin(T.inc[:, 0:1], T.zero[:, 0:1], 0.0, 0.0, 1, ["zero"], ["inc"])
-    lin(T.ph[:, 0:8], T.zero[:, 0:8], 0.0, 0.0, 1, ["zero"], ["phz"])
-    lin(T.pf[:, 0:4], T.zero[:, 0:4], 0.0, 0.0, 1, ["zero"], ["pf"])
-    lin(T.TY[:, B:JB], T.zero[:, 0:8], 0.0, 0.0, 1, ["zero"], ["TYz"])
-    lin(T.TX[:, B:JB], T.zero[:, 0:8], 0.0, 0.0, 1, ["zero"], ["TXz"])
-    lin(T.X0[:, S:S + 8], T.zero[:, 0:8], 0.0, -3336.0, 1, ["zero"], ["Xe0"])
-    lin(T.X1[:, S:S + 8], T.zero[:, 0:8], 0.0, -3336.0, 1, ["zero"], ["Xe1"])
-    lin(T.difx[:, B:MW], T.zero[:, 0:16], 0.0, 0.0, 1, ["zero"], ["drz", "dr4"])
-    half(T.SS[:], T.zero[:, 0:MW], 1.0, kc("one"), MW, ["zero", "one"], ["SS0", "SS1"])
-    lin(T.PM[:, B:JB], T.zero[:, 0:8], 0.0, 0.0, 1, ["zero"], ["PM3", "PM5"])
-    dma(T.RX[:], T.SS[:, 0:B], 2.5, ["SS0", "SS1"], ["RXh", "RXl", "RXH", "RXL"])
-    dma(T.RB[:], T.zero[:, 0:B], 2.5, ["zero"], ["RBh", "RBl"])
-    cp(T.mpu[:], T.mpi[:], 96, ["mpi"], ["mpu"])
-    cp(T.dl[:], T.dui[:], 96, ["dui"], ["dl"])
-
-    def gather(out, win, n, reads, writes):
-        either(lambda: [v.tensor_copy(out, win)], lambda: [a.activation(out, win, AF.Identity)], n * GATH, reads, writes)
-
-    for h in range(2):
-        gather(T.cmp[:, 768 * h:768 * h + 768], T.qrow[:, 0:16].indirect(T.dl[:, 48 * h:48 * h + 48]), 768, ["qrow", "dl"], ["cmp%d" % h])
-        mm([[(T.p6[:, 0:96], blk(T.MV, i), T.cmp[:, 96 * i:96 * i + 96]) for i in range(8 * h, 8 * h + 8)]], 768,
-           ["MV", "cmp%d" % h], ["b6"], h == 0, h == 1)
-    lin(T.bun[:, 0:96], T.p6[:, 0:96], 1.0 / 16, 0.0, 96, [], ["b6", "bd"])
-
-    bA, bB = ["b0", "b1", "b2"], ["b3", "b4", "b5"]
-    PIECES = ((0, 0, 384), (1, 384, 512), (1, 512, 768), (2, 768, 1024), (2, 1024, 1152), (3, 1152, 1536))
-
-    def tables(Tb, tk, dsrc, dk, F, GR, GC, M, mk, df, fk):
-        dma([F[j:128:4, :] for j in range(4)], [dsrc] * 4, 2.0, [dk], [tk + "F"])
-        Fk = [tk + "F"]
-        for G, nm, P, bk, out, ok in ((GR, "R", T.pA, bA, 0, tk), (GC, "C", T.pB, bB, JB + 1, tk + "j")):
-            ac(G[:], F[:], AF.Relu, 384, Fk + [nm + "3", nm + "b"], [tk + nm], bias=kc(nm + "b"), scale=kc(nm + "3"))
-            mm([[(P[:, x0:x1], blk(M, q), G[:, x0 - 384 * q:x1 - 384 * q])] for q, x0, x1 in PIECES], B,
-               [tk + nm] + [mk + str(q) for q in range(4)], bk)
-            for j, (x0, x1) in enumerate(((0, CUT[0]), CUT, (CUT[1], B))):
-                tt(Tb[:, out + x0:out + x1], df[:, x0:x1], P[:, x0:x1], ALU.mult, x1 - x0, fk[j], bk[max(j - 1, 0):j + 1] + [ok + "abc"[j]])
-        lin(Tb[:, JB:JB + 1], df[:, B:B + 1], 1.0, 0.0, 1, fk[2], [tk + "0"])
-        tt(Tb[:, TW - 1:TW], Tb[:, TW - 1:TW], Tb[:, B - 1:B], ALU.subtract, 1, [tk + "c"], [tk + "jc"])
-
-    def samples(Tb, tk, lst, lk, slots, Y, yk):
-        for c in range(NC):
-            k = slots[c % len(slots)]
-            o = T.DX[:, CH * k:CH * k + CH]
-            gather(o, Tb[:].indirect(lst[:, 64 * c:64 * c + 64]), CH, [tk + s for s in ("a", "b", "c", "ja", "jb", "jc", "0", "z")] + [lk[c // 2]], ["D%d" % k])
-            ini = 0.0 if c == 0 else Y[:, CH * c - 1:CH * c]
-            scan(Y[:, CH * c:CH * c + CH], o, T.zero[:, 0:CH], ini, CH,
-                 ["D%d" % k, "zero"] + ([yk + str(c - 1)] if c else []), [yk + str(c)])
-
-    def output(t):
-        X, XK = T["X%d" % (t % 2)], ["X%d%d" % (t % 2, c) for c in range(NC)]
-        for c in range(NC):
-            x = slice(CH * c, CH * c + CH)
-            z, zk, y = T.Z[:, x], "Z%d" % c, T.Y[:, x]
-            if t in SHIP:
-                yd, y = T["yd%d" % t], z
-                dma([T.Z[16:128, x], T.Z[0:16, x]], [yd[c, 0:112, :], yd[c, 112:128, :]], 3.0, ["yd%d%d" % (t, c)], [zk])
-            tt(z, X[:, 0:S].indirect(T["el%d" % t][:, 64 * c:64 * c + 64]), y, ALU.mult, CH * GATH,
-               XK + ["el%d" % t] + ([] if t in SHIP else ["Y%d" % c]), [zk])
-            ac(z, z, AF.Tanh, CH, [], [zk], scale=2.0 ** -14)
-            lin(z, z, T.gn[:, t:t + 1], 0.0, CH, ["gn"], [zk])
-            dma(T.yo[:, x], z, 3.0, [zk], ["yo%d" % c], acc=t > 0)
-
-    for t in range(NB):
-        lb, ld, li = T["lb%d" % t], T["ld%d" % t], T["li%d" % t]
-        X, XK, own = T["X%d" % (t % 2)], ["X%d%d" % (t % 2, c) for c in range(NC)], t not in SHIP
-        Xe = "Xe%d" % (t % 2)
-        scan(T.inc[:, 1:97], T.bun[:, 0:96], T.zero[:, 0:96], 0.0, 96, ["bd", "zero"], ["inc"])
-        mm([[(T.p7[:, 0:1], T.Lf[:], T.inc[:, 96:97])]], 256, ["Lf", "inc"], ["b7"])
-        ts(T.bun[:, 96:192], T.inc[:, 0:96], T.p7[:, 0:1], None, ALU.add, None, 96, ["inc"], ["b7", "bh"])
-        ts(T.of[:], T.inc[:, 0:96], T.p7[:, 0:1], None, ALU.add, None, 96, ["inc"], ["b7", "of"])
-        tt(T.bun[:, 192:288], T.of[:], T.bun[:, 96:192], ALU.subtract, 192, ["of", "bh"], ["bl"])
-        send("b", t, "lb%d" % t, T.bun[:], (0, 288), 2.2, ["bd", "bh", "bl"], "lb%d" % t)
-        Ac, I1, N1, ak = (T.A, T.Ib, T.Nb, ["A", "A", "A", "Ib", "Nb"]) if t == 0 else (T.a2, T.Ih, T.Nh, ["a20", "a21", "a22", "Ih", "Nh"])
-        A0 = 0.0 if t == 0 else -256.0
-        rk = ["Irb", "Nrb"] if t == 0 else ["Ir", "Nr"]
-        for P, bk, I2, N2, D, dk, mk in ((T.pA, bA, T[rk[0]], T[rk[1]], T.difx, "dr", rk), (T.pB, bB, I1, N1, T.dif, "df", ak[3:]))[0:1 + own]:
-            for j in range(3):
-                x0, x1 = max(512 * j, 1), 512 * j + 512
-                mm([[(P[:, x0:x1], I2[:], Ac[:, x0:x1]), (P[:, x0:x1], N2[:], Ac[:, x0 - 1:x1 - 1])]], 1024,
-                   [ak[j], ak[max(j - 1, 0)]] + mk, [bk[j]])
-                lin(D[:, x0 - 1:x1 - 1], P[:, x0:x1], 1.0, 0.0, 512, [], [bk[j], dk + str(j)])
-            mm([[(P[:, 0:1], I2[:], Ac[:, 0:1]), (P[:, 0:1], N2[:], Ac[:, B - 1:B])], [(P[:, 1:2], I2[:], Ac[:, 0:1])]], 192, ak + mk, [bk[0]])
-            lin(D[:, B - 1:B], P[:, 0:1], 1.0, 0.0, 1, [], [bk[0], dk + "3"])
-            lin(D[:, B:B + 1], P[:, 1:2], 1.0, A0, 1, [], [bk[0], dk + "4"])
-            if dk == "dr":
-                send("d", t, "ld%d" % t, D[:, 0:CUT[0]], (0, CUT[0]), 5.5 + t, ["dr0", "ship%d0" % (t - 1), "ship%d1" % (t - 1)], "ld%d0" % t)
-                send("h", t, "ld%d" % t, D[:, CUT[0]:CUT[1]], CUT, 6.0 + 2 * t, ["dr0", "dr1"], "ld%d1" % t)
-                send("e", t, "ld%d" % t, D[:, CUT[1]:MW], (CUT[1], MW), 3.5 + t, ["dr1", "dr2", "dr3", "dr4", "drz"], "ld%d2" % t)
-        if t - 1 in SHIP:
-            for c in range(NC // 2, NC):
-                ship(t - 1, c, T["X%d" % ((t - 1) % 2)], "X%d%d" % ((t - 1) % 2, c), ["senth%d" % t])
-        if t > 0:
-            output(t - 1)
-        dma(T.RB[0:128:16, :], T.bun[:, 96:192], 2.0, ["bh"], ["RBh"])
-        dma(T.RB[8:128:16, :], T.bun[:, 192:288], 2.0, ["bl"], ["RBl"])
-        for row, c0, k in ((0, 96, "h"), (8, 192, "l")):
-            dma([T.RX[row:112:16, :], T.RX[112 + row:113 + row, :]], [lb[16:128, c0:c0 + 96], lb[0:16, c0:c0 + 96]], 2.0,
-                ["lb%d" % t], ["RX" + k, "RX" + k.upper()])
-        mm([[(T.p6[:, 0:96], blk(T.MO, i), T.RB[:, i:B:16]) for i in range(16)],
-            [(T.p6[:, 96:97], T.M15[:], T.bun[:, c:c + 1]) for c in (95, 191, 287)]],
-           B + 192, ["MO", "M15", "RBh", "RBl", "bd", "bh", "bl"], ["b6"])
-        cp(T.offw[:, 0:96], T.p6[:, 0:96], 96, [], ["b6", "offw"])
-        ts(T.offw[:, 96:97], T.p6[:, 96:97], kc("cv"), None, ALU.add, None, 1, ["cv"], ["b6", "offw"])
-        if t < NB - 1:
-            ts(T.offs[:], T.p6[:, 0:96], float(S), None, ALU.min, None, 96, [], ["b6", "offs"])
-        merged = t in OPT["merge"]
-        for h in range(2):
-            gather((T.SS if merged else T.PM)[:, 768 * h:768 * h + 768], T.RX[:].indirect(T.mpu[:, 48 * h:48 * h + 48]), 768,
-                   ["RXh", "RXl", "RXH", "RXL", "mpu"], [("SS%d" if merged else "PM%d") % h])
-        if merged:
-            dma([T.SS[1:128:8, 1:B + 1], T.SS[12:128:16, 1:B + 1]], [T.SS[0:128:8, 0:B], T.bun[:, 0:96]], 2.0, ["bd"], ["SS0", "SS1"])
-        else:
-            dma(T.PM[:, JB:JB + B], T.PM[:, 0:B], 2.6, ["PM0", "PM1"], ["PM2"])
-            lin(T.PM[:, B:B + 1], T.PM[:, B - 1:B], 1.0, 0.0, 1, ["PM1"], ["PM3"])
-            lin(T.PM[:, TW - 1:TW], T.PM[:, B - 1:B], 1.0, 0.0, 1, ["PM1"], ["PM4"])
-            dma(T.SS[12:128:16, 1:B + 1], T.bun[:, 0:96], 2.0, ["bd"], ["SS0", "SS1"])
-        dma([T.W[:, 0:2056], T.W[:, 2056:4112]], [T.zero[:, 0:2056]] * 2, 3.2, ["zero"], ["W", "W2"])
-        cp(T.W[:, WP:WP + WW].indirect(T.offw[:, 0:97]), T.SS[:], MW * SCAT, ["offw", "SS0", "SS1"], ["W", "W2"])
-        for h, P, bk in ((0, T.p6, "b6"), (1, T.p7, "b7")):
-            w0 = WP + 2048 * h
-            mm([[(P[:, 0:128], blk(T.MI, i), T.W[:, w0 + i:w0 + 2048:16]) for i in range(16)]], 2048, ["MI", "W", "W2"], [bk])
-            c0 = 8 + 128 * h
-            lin(T.ph[:, c0:c0 + 128], P[:, 0:128], 1.0, 0.0, 128, [], [bk, "ph%d" % h])
-            mm([[(P[:, 128:256], T.Ir[:], T.ph[:, c0:c0 + 128]), (P[:, 128:256], T.Sr[:], T.ph[:, c0 - 1:c0 + 127]),
-                 (P[:, 128:256], T.N3r[:], T.W[:, w0 - 1:w0 + 2047:16])]], 384,
-               ["Ir", "Sr", "N3r", "ph0", "phz", "ph%d" % h, "W", "W2"], [bk])
-            scan(T.sb[:, 128 * h:128 * h + 128], P[:, 128:256], T.zero[:, 0:128], -1.0 if h == 0 else T.sb[:, 127:128], 128,
-                 ["zero", "sb0"] if h else ["zero"], [bk, "sb%d" % h])
-            cp(T.idxr[:, 128 * h:128 * h + 128], T.sb[:, 128 * h:128 * h + 128], 128, ["sb%d" % h], ["idxr%d" % h])
-            send("ij"[h], t, "li%d" % t, T.idxr[:, 128 * h:128 * h + 128], (128 * h, 128 * h + 128), 2.2, ["idxr%d" % h], "li%d%d" % (t, h))
-        if own or not merged:
-            P = T.p6[:, 256:512]
-            mm([[(P, T.Ih[:], T.ph[:, 8:264]), (P, T.Sh[:], T.ph[:, 7:263]), (P, T.N3[:], T.W[:, WP - 1:WP - 1 + S:16])]], 768,
-               ["Ih", "Sh", "N3", "ph0", "ph1", "phz", "W", "W2"], ["b6"])
-            scan(T.sa[:], P, T.zero[:, 0:256], -1.0, 256, ["zero"], ["b6", "sa"])
-            cp(T.idx[:], T.sa[:], 256, ["sa"], ["idx"])
-        mm([[(T.p7[:, 256:512], blk(T.ME, i), T.W[:, WP + i:WP + S:16]) for i in range(16)]], S, ["ME", "W", "W2"], ["b7"])
-        ac(T.pf[:, 4:260], T.p7[:, 256:512], AF.Identity, 256, [], ["b7", "pf"])
-        mm([[(T.p7[:, 0:256], T.If[:], T.pf[:, 4:260]), (T.p7[:, 0:256], T.Sf[:], T.pf[:, 3:259])]], 2048, ["If", "Sf", "pf"], ["b7"])
-        scan(T.se[:], T.p7[:, 0:256], T.c720[:], kc("ei"), 256, ["c720", "ei"], ["b7", "se"])
-        for h, G, gk in ((0, T.val, "val"), (1, T.GQ, "GQ"))[0:0 if merged else 2]:
-            for c in range(2):
-                gather(G[:, CH * c:CH * c + CH], T.PM[:].indirect(T.idx[:, 128 * h + 64 * c:128 * h + 64 * c + 64]), CH,
-                       ["PM%d" % k for k in range(6)] + ["idx"], [gk + str(c)] + ([gk] if c == 0 else []))
-            mm([[(T.p7[:, 256 + 128 * h:384 + 128 * h], blk(T.MO, i), G[:, i:2048:16]) for i in range(16)]], 2048,
-               ["MO", gk + "0", gk + "1"], ["b7"])
-        if merged:
-            cp(T.ea[:], T.se[:], 256, ["se"], ["ea"])
-        else:
-            tt(T.ea[:], T.se[:], T.p7[:, 256:512], ALU.add, 256, ["se"], ["b7", "ea"])
-        ts(T.eb[:], T.ea[:], S - 1, None, ALU.bitwise_and, None, 256, ["ea"], ["eb"])
-        cp(T["el%d" % t][:], T.eb[:], 256, ["eb"], ["el%d" % t])
-        tabs = [lambda: tables(T.TY, "TY", T.bun[:, 0:96], "bd", T.FD, T.GR, T.GC, T.BQ, "BQ", T.dif,
-                               [["df0"], ["df0", "df1"], ["df1", "df2", "df3", "df4"]]),
-                lambda: tables(T.TX, "TX", lb[:, 0:96], "lb%d" % t, T.FX, T.HR, T.HC, T.BR, "BR", ld, [["ld%d%d" % (t, j)] for j in range(3)])]
-        for k in OPT["tab"][t]:
-            if k == 1 or own:
-                tabs[k]()
-        samples(T.TX, "TX", li, ["li%d0" % t, "li%d1" % t], (0, 1) if own else (0, 1, 2, 3), X, "X%d" % (t % 2))
-        if own:
-            samples(T.TY, "TY", T.idx, ["idx", "idx"], (2, 3), T.Y, "Y")
-        else:
-            for c in range(NC // 2):
-                ship(t, c, X, XK[c], [])
-        if t < NB - 1:
-            ts(T.lv[:], T.of[:], float(S), None, ALU.is_lt, None, 96, ["of"], ["lv"])
-            tt(T.x1[:], T.bun[:, 0:96], T.lv[:], ALU.subtract, 96, ["bd", "lv"], ["x1"])
-            ac(T.z2[:], T.x1[:], AF.Relu, 96, ["x1"], ["z2"], bias=2.0, scale=-2.0)
-            tt(T.dn[:], T.x1[:], T.z2[:], ALU.add, 96, ["x1", "z2"], ["dn"])
-            ac(T.e1[:], T.bun[:, 0:96], AF.Abs, 96, ["bd"], ["e1"], bias=-3.0)
-            ac(T.e5[:], T.e1[:], AF.Relu, 96, ["e1"], ["e5"], bias=-32.0, scale=32.0)
-            if t > 0:
-                half(T.a1[:], T.a2[:], 1.0, -256.0, B, ak[0:3], ["a10", "a11", "a12"])
-                for j in range(3):
-                    x, sj = slice(512 * j, 512 * j + 512), str(j)
-                    mm([[(T.pB[:, x], T.Ib[:], T.V0[:, x]), (T.pB[:, x], T.I4[:], T.dead[:, x])]], 1024, ["Ib", "I4", "V0", "dead" + sj], [bB[j]])
-                    ac(T.zv[:, x], T.pB[:, x], AF.Relu, 512, [], [bB[j], "zv" + sj], bias=-192.0)
-            for h in range(2):
-                tt(T.cmp[:, 768 * h:768 * h + 768], X[:, 0:S + 1].indirect(T.offs[:, 48 * h:48 * h + 48]),
-                   (T.A if t == 0 else T.a1)[:, 768 * h:768 * h + 768], ALU.is_gt, 768 * GATH,
-                   XK + [Xe, "offs", "A", "a1%d" % h, "a1%d" % (h + 1)], ["cmp%d" % h])
-                mm([([(T.p6[:, 0:96], T.Nb[:], T.e5[:])] if h == 0 else []) +
-                    [(T.p6[:, 0:96], blk(T.MV, i), T.cmp[:, 96 * i:96 * i + 96]) for i in range(8 * h, 8 * h + 8)]], 768 + 96,
-                   ["MV", "Nb", "cmp%d" % h, "e5"], ["b6"], h == 0, h == 1)
-            ts(T.u2[:], T.p6[:, 0:96], 8.5, 2.0, ALU.is_ge, ALU.mult, 96, [], ["b6", "u2"])
-            tt(T.bun[:, 0:96], T.u2[:], T.dn[:], ALU.add, 96, ["u2", "dn"], ["bd"])
-            off = 145.0 * (t + 1)
-            for j in range(3):
-                x, sj = slice(512 * j, 512 * j + 512), str(j)
-                old = [(T.Ib, T.V0)] if t == 0 else [(T.Ih, T.uh), (T.Ib, T.zv)]
-                mm([[(T.pA[:, x], l[:], w[:, x]) for l, w in old]], 512 * len(old), ["Ib", "Ih", "V0", "uh" + sj, "zv" + sj], [bA[j]], True, False)
-                mm([[(T.pB[:, x], I1[:], Ac[:, x])]], 512, [ak[j]] + ak[3:], [bB[j]], True, False)
-                ac(T.fb[:, x], X[:, 0:S + 1].indirect(T.offs[:, 32 * j:32 * j + 32]), AF.Identity, 512 * GATH, XK + [Xe, "offs"], ["fb" + sj],
-                   bias=145.0 - 2047.5 / 4096, scale=1.0 / 16)
-                mm([[(T.pA[:, x], T.Ib[:], T.fb[:, x])]], 512, ["Ib", "fb" + sj], [bA[j]], False, True)
-                add({"dve": (lambda x=x: [v.tensor_scalar(T.dead[:, x], T.fb[:, x], -1.0, 0.0, ALU.mult, ALU.max)], 0.06 + 256 * CYC),
-                     "act": (lambda x=x: [a.activation(T.dead[:, x], T.fb[:, x], AF.Relu, scale=-1.0)], 0.07 + 512 * CYC)}, ["fb" + sj], ["dead" + sj])
-                ts(T.uh[:, x], T.pA[:, x], off - 64, off + 64, ALU.max, ALU.min, 512, [], [bA[j], "uh" + sj])
-                mm([[(T.pB[:, x], T.Ib[:], T.dead[:, x]), (T.pB[:, x], T.Ih[:], T.uh[:, x])]], 1024, ["Ib", "Ih", "dead" + sj, "uh" + sj],
-                   [bB[j]], False, True)
-                ac(T.a1[:, x], T.pB[:, x], AF.Abs, 512, [], [bB[j], "a1" + sj], bias=-(off + 256.0 * (t + 1)))
-                ac(T.a2[:, x], T.a1[:, x], AF.Abs, 512, ["a1" + sj], ["a2" + sj], bias=512.0, scale=-1.0)
-    output(NB - 1)
-    lastw, readers = {}, {}
-    for i, o in enumerate(ops):
-        d = set()
-        for k in o["r"]:
-            if k in lastw:
-                d.add(lastw[k])
-        for k in o["w"]:
-            if k in lastw:
-                d.add(lastw[k])
-            d.update(readers.get(k, []))
-        for k in o["r"]:
-            readers.setdefault(k, []).append(i)
-        for k in o["w"]:
-            lastw[k] = i
-            readers[k] = []
-        d.discard(i)
-        o["deps"] = sorted(d)
-    return ops
-
-
-ENG = {"dve": "dve", "act": "act", "pe": "pe", "pool": "g", "g": "g", "sp": "sp", "none": "none"}
-
-
-def order(ops, wake, par):
-    seed, delta, noise, bias = par
-    n = len(ops)
-    pri = [0.0] * n
-    x = seed * 7919 + 1
-    for i in range(n - 1, -1, -1):
-        o = ops[i]
-        pri[i] += min(c for _, c in o["alts"].values()) + o["lat"] + wake
-        for j in o["deps"]:
-            pri[j] = max(pri[j], pri[i])
-    for i in range(n):
-        x = (x * 1103515245 + 12345) % 2147483648
-        pri[i] += noise * (x / 2147483648.0)
-    left = [len(o["deps"]) for o in ops]
-    users = [[] for _ in ops]
-    for i, o in enumerate(ops):
-        for j in o["deps"]:
-            users[j].append(i)
-    fin, free, seq, rdy = [0.0] * n, {}, [], [0.0] * n
-    ready = [i for i in range(n) if left[i] == 0]
-    while ready:
-        cand = []
-        for i in ready:
-            al = ops[i]["alts"]
-            q = min((max(rdy[i], free.get(ENG[q], 0.0)) + c + (bias * c if q == "dve" else 0.0), q) for q, (_, c) in al.items())[1]
-            cand.append((max(rdy[i], free.get(ENG[q], 0.0)), i, q))
-        t1, _, q1 = min(cand)
-        st, i, q = max([c for c in cand if ENG[c[2]] == ENG[q1] and c[0] <= t1 + delta], key=lambda c: (pri[c[1]], -c[1]))
-        c = ops[i]["alts"][q][1]
-        if q != "none":
-            free[ENG[q]] = st + c
-        fin[i] = st + c + ops[i]["lat"]
-        seq.append((i, q))
-        ready.remove(i)
-        for u in users[i]:
-            left[u] -= 1
-            rdy[u] = max(rdy[u], fin[i] + wake)
-            if left[u] == 0:
-                ready.append(u)
-    return seq
-
-
-def decode(ops, text):
-    seq = []
-    for k in range(0, len(text), 2):
-        i, on_act = divmod((ord(text[k]) - 48) * 40 + ord(text[k + 1]) - 48, 2)
-        seq.append((i, "act" if on_act else list(ops[i]["alts"])[0]))
-    assert sorted(i for i, _ in seq) == list(range(len(ops)))
-    return seq
+                    sent += bits(engines(core, w[k + 1], 1, T, topo))
+    if sent:
+        g.wait_ge(T.sem["hs"], sent)
 
 
 def rank_program(g, core, T, topo):
     if T.rank_of(core) is None:
         helper_program(g, core, T, topo)
         return
-    ops = build(g, core, T, topo, MODELS[0])
-    seq = decode(ops, ORDER) if ORDER else order(ops, MODELS[0][6], SEED)
-    queue = {"dve": g.vector, "act": g.scalar, "pe": g.tensor, "g": g, "sp": g.sync}
-    count = {"dve": 0, "act": 0, "pe": 0, "pool": 0}
-    waited = {}
-    total = {}
-    for i, q in seq:
-        o = ops[i]
-        if q != "none":
-            need = {}
-            for j in o["deps"]:
-                for s, n in ops[j]["tok"]:
-                    need[s] = max(need.get(s, 0), n)
-            for s, n in need.items():
-                if waited.get((ENG[q], s), 0) < n:
-                    queue[ENG[q]].wait_ge(T.sem[s], n)
-                    waited[(ENG[q], s)] = n
-            res = o["alts"][q][0]()
-            if q in count:
-                for ins in res:
-                    ins.then_inc(T.sem[q], 1)
-                    count[q] += 1
-                o["tok"] = [(q, count[q])]
-        for s, n in o["tok"]:
-            total[s] = max(total.get(s, 0), n)
+    r = T.rank_of(core)
+    v, a, pe = g.vector, g.scalar, g.tensor
+    queue = {"dve": v, "act": a, "pe": pe, "pool": g, "g": g, "sp": g.sync}
+    issued = {"dve": 0, "act": 0, "pe": 0, "pool": 0}
+    lastw, readers, waited, total, ndma = {}, {}, {}, {}, [0]
+
+    def call(q, fn, reads, writes, tok=None):
+        need = {}
+        for s, n in [lastw[k] for k in reads + writes if k in lastw] + [x for k in writes for x in readers.get(k, [])]:
+            need[s] = max(need.get(s, 0), n)
+        qq = "g" if q == "pool" else q
+        for s, n in need.items():
+            if waited.get((qq, s), 0) < n:
+                queue[q].wait_ge(T.sem[s], n)
+                waited[(qq, s)] = n
+        ins = fn()
+        if tok is None:
+            ins.then_inc(T.sem[q], 1)
+            issued[q] += 1
+            tok = (q, issued[q])
+        total[tok[0]] = tok[1]
+        for k in reads:
+            readers.setdefault(k, []).append(tok)
+        for k in writes:
+            lastw[k], readers[k] = tok, []
+
+    def lands(key, sem, n):
+        lastw[key] = (sem, n)
+        total[sem] = n
+
+    def select(out, in_, pat, op, fill_, base, cm, rk, wk):
+        call("pool", lambda: g.affine_select(out, in_, pat, op, fill_, base, cm), [rk], [wk])
+
+    def ts(out, in0, s1, s2, op0, op1, reads, writes):
+        call(V, lambda: v.tensor_scalar(out, in0, s1, s2, op0, op1) if op1 else v.tensor_scalar(out, in0, s1, None, op0), reads, writes)
+
+    def tt(out, in0, in1, op, reads, writes):
+        call(V, lambda: v.tensor_tensor(out, in0, in1, op), reads, writes)
+
+    def cp(out, in_, reads, writes, q=V):
+        call(q, lambda: v.tensor_copy(out, in_) if q == V else a.activation(out, in_, AF.Identity), reads, writes)
+
+    def ms(out, c, writes):
+        call(V, lambda: v.memset(out, c), [], writes)
+
+    def scan(out, d0, d1, ini, reads, writes, op0=ALU.add):
+        call(V, lambda: v.tensor_tensor_scan(out, d0, d1, ini, op0, ALU.add), reads, writes)
+
+    def ac(out, in_, f, reads, writes, bias=0.0, scale=1.0):
+        call(A_, lambda: a.activation(out, in_, f, bias=bias, scale=scale), reads, writes)
+
+    def lin(q, out, in_, scale, bias, reads, writes):
+        if q == V:
+            ts(out, in_, scale, bias, ALU.mult, ALU.add, reads, writes)
+        else:
+            ac(out, in_, AF.Identity, reads, writes, bias, scale)
+
+    def mm(grp, reads, writes, start=True, stop=True):
+        def fn():
+            for i, (o, l, x) in enumerate(grp):
+                ins = pe.matmul(o, l, x, start and i == 0, stop and i == len(grp) - 1)
+            return ins
+        call("pe", fn, reads, writes)
+
+    def dma(outs, ins, reads, writes, how="sp"):
+        s = "q%d" % ndma[0]
+        ndma[0] += 1
+
+        def fn():
+            for o, i in zip(outs, ins):
+                d = g.dma_start(o, i, accum_op=ALU.add) if how == "add" else queue[how].dma_start(o, i)
+                d.then_inc(T.sem[s], 16)
+        call("g" if how == "add" else how, fn, reads, writes, (s, 16 * len(outs)))
+
+    def send(m, t, out, src_ap, reads, land, back=False):
+        dst, src = T.cores[(r - 1 - t) % N], T.cores[(r + 1 + t) % N]
+        if back:
+            dst, src = src, dst
+        ls, rs, got = "s%s%d" % (m, t), "r%s%d" % (m, t), "r%s%d" % (m, t)
+        if m == "d" and relay(core, t, T, topo):
+            dst, x, rs, _ = relay(core, t, T, topo)
+            out = T["la%d" % t][:, x]
+        if m == "d" and relay(src, t, T, topo):
+            src = relay(src, t, T, topo)[0]
+        call("g", lambda: remote(g, T, topo, core, dst, out, src_ap, rs, ls, 0), reads, [], (ls, bits(engines(core, dst, 0, T, topo))))
+        lands(land, got, bits(engines(src, core, 0, T, topo)))
+
+    kn = {}
+
+    def kc(name):
+        return T.K[:, kn.setdefault(name, len(kn)):kn[name] + 1]
+
+    def oh(j):
+        return T.OH[:, j:j + 1]
+
+    def mv(i):
+        return T.MV[:, 15 - i:143 - i]
+
+    def third(j):
+        return slice(512 * j, 512 * j + 512)
+
+    def chunk(c):
+        return slice(CH * c, CH * c + CH)
+
+    def fills(what):
+        for out, w, c, key in what:
+            lin(A_, out, T.zero[:, 0:w], 0.0, c, ["zero"], [key])
+
+    XB, WB, OB = [T.X0, T.X1, T.X0], [T.W0, T.W1, T.W0], "YZY"
+    XK = [["X%d%d" % (t % 2, c) for c in range(NC)] for t in range(NB)]
+    WK = [["W%d%d" % (t % 2, k) for k in range(2)] for t in range(NB)]
+    bA, bB, AK = ["b0", "b1", "b2"], ["b3", "b4", "b5"], ["A0", "A1", "A2", "A3"]
+    TXK = ["TX0", "TX1", "TX2", "TXz", "TXa0", "TXa1", "TXa2"]
+    TYK = ["TY0", "TY1", "TY2", "TY3", "TJ0", "TJ1", "TJ2", "TJ3", "TYz", "TYa"]
+    Lb, Ub, Ib = (T.C[:, 128 * k:128 * k + 128] for k in range(3))
+    Lr, Ur, Irb = (T.Cr[:, 128 * k:128 * k + 128] for k in range(3))
+    LB = [(T.p6, 0, "b6"), (T.pB, 0, "b3"), (T.pB, 512, "b4"), (T.pB, 1024, "b5")]
+    PB = [(T.p7, "b7")] * NB
+    step = {}
+
+    def unit(f):
+        step[str(f).split(".")[-1].split()[0]] = f
+        return f
+
+    dma([T.dur[0:112, :], T.dur[112:128, :]], [T.du[16:128, :], T.du[0:16, :]], [], ["dur"])
+    dma([T.dui[:]], [T.du[:]], [], ["dui"])
+    dma([T.A[:, 0:B]], [T.am[:]], [], AK[0:3])
+    dma([T.V0[:], T.mpi[:], T.gn[:, 0:3]], [T.ve[:], T.mp[:], T.gain[:]], [], ["V0", "mpi", "gn"])
+    call("pool", lambda: g.iota(T.pi[:, 0:1], [[0, 1]], 0, 1), [], ["pi0"])
+    call("pool", lambda: g.iota(T.qrow[:], [[1, 256]], 0, 0, allow_small_or_imprecise_dtypes=True), [], ["qrow"])
+    ms(T.ones[:, 0:CH], 1.0, ["ones"])
+    ms(T.zero[:], 0.0, ["zero"])
+    select(T.t2[:], T.ones[:, 0:128], [[-16, 8], [0, 16]], ALU.is_ge, 0.0, 0, 1, "ones", "t2")
+    select(T.t3[:], T.t2[:], [[16, 8], [0, 16]], ALU.is_ge, 0.0, 15, -1, "t2", "t3")
+    select(Lb, T.t3[:], [[1, 128]], ALU.is_gt, 0.0, 0, -1, "t3", "Lb")
+    select(Ub, T.t3[:], [[-1, 128]], ALU.is_ge, 0.0, 0, 1, "t3", "Ub")
+    select(Ib, T.zero[:, 0:128], [[-1, 128]], ALU.not_equal, 1.0, 0, 1, "zero", "Ib")
+    dma([T.Cr[16:128, :], T.Cr[0:16, :]], [T.C[0:112, :], T.C[112:128, :]], ["Lb", "Ub", "Ib"], ["Cr"])
+    ts(T.pi[:, 4:5], T.pi[:, 0:1], 15, None, ALU.bitwise_and, None, ["pi0"], ["pi4"])
+    cp(kc("p"), T.pi[:, 0:1], ["pi0"], ["p"])
+    cp(kc("r"), T.pi[:, 4:5], ["pi4"], ["r"])
+    ms(T.offw[:, 96:98], 0, ["ow1"])
+    ms(T.RD[:], 0.0, ["RD"])
+    lin(A_, kc("cap"), kc("r"), 1.0, 7690.0 - CH, ["r"], ["cap"])
+    lin(A_, kc("g"), kc("r"), -1.0, kc("p"), ["p", "r"], ["g"])
+    fills(((T.dd[:, 96:104], 8, 2560.0, "dz"), (T.dr[:, 96:104], 8, 2560.0, "dz"), (T.A[:, B:AW], 8, 0.0, "A3")))
+
+    @unit
+    def sums_matrix():
+        ts(T.MV[:], T.qrow[:, 0:144], -15.0, kc("g"), ALU.add, ALU.is_equal, ["qrow", "g"], ["MV"])
+
+    @unit
+    def const_quarters(n):
+        if n == 0:
+            call("pool", lambda: g.iota(T.q4[:], [[16, 8], [0, 4], [4, 4]], 0, 0, allow_small_or_imprecise_dtypes=True), [], ["q4"])
+            ts(kc("p1"), kc("p"), 16.0, 128.0, ALU.is_lt, ALU.mult, ["p"], ["p1"])
+            ts(kc("pr"), kc("p1"), kc("p"), -16.0, ALU.add, ALU.add, ["p1", "p"], ["pr"])
+        for y in range(4):
+            ts((T.Qr, T.Q)[n][:, 128 * y:128 * y + 128], T.q4[:], float(y), kc(("pr", "p")[n]), ALU.add, ALU.is_equal, ["q4", "pr"], [("Qr", "Q")[n]])
+
+    @unit
+    def first_ones():
+        ms(T.W0[:, 0:S], 1.0, WK[0])
+
+    @unit
+    def clear_rows():
+        for x in (slice(0, CH), slice(CH, B)):
+            cp(T.RX[:, x], T.zero[:, 0:x.stop - x.start], ["zero"], ["RX"], A_)
+
+    @unit
+    def const_blocks():
+        cp(T.Lf[:], Lb, ["Lb"], ["Lf"], A_)
+        fills(((T.inc[:, 0:1], 1, 0.0, "inc"), (T.of[:, 96:104], 8, 0.0, "ofz")))
+        cp(T.dd[:, 0:96], T.dui[:], ["dui"], ["dl"])
+        ts(T.OH[:], T.qrow[:, 0:16], kc("r"), None, ALU.is_equal, None, ["qrow", "r"], ["OH"])
+
+    @unit
+    def mp_list():
+        cp(T.mpu[:], T.mpi[:], ["mpi"], ["mpu"])
+
+    @unit
+    def const_counts():
+        select(T.T1[:], Lb, [[-1, 128]], ALU.not_equal, JB + 1.0, 0, 1, "Lb", "T1")
+        select(T.T2[:], Ub, [[-1, 128]], ALU.not_equal, -float(JB), 0, 1, "Ub", "T2")
+        fills(((T.c16[:], 64, 16.0, "c16"), (T.ph[:, 0:8], 8, -1.0, "phz"), (T.TX[:, B:JB], 8, 0.0, "TXz")))
+        lin(A_, T.Nrb[:], Irb, -1.0, 0.0, ["Cr"], ["Nrb"])
+
+    @unit
+    def const_dead():
+        for name, w in (("Z1", -256.0), ("Z2", -64.0), ("Z3", 64.0), ("Z4", 720.0)):
+            lin(A_, kc(name), oh(0), w, 0.0, ["OH"], ["k" + name])
+            lin(A_, T[name][:], T.t3[:], kc(name), 0.0, ["t3", "k" + name], [name])
+
+    @unit
+    def const_back():
+        lin(A_, kc("x0"), kc("r"), 0.5, kc("g"), ["r", "g"], ["x"])
+        lin(A_, kc("x1"), kc("x0"), 1.0, 8.0, [], ["x"])
+        lin(A_, T.F[:, 0:128], Ib, 1.0, 0.0, ["Ib"], ["F"])
+        for k in range(2):
+            ac(T.t1[:], T.qrow[:, 0:128], AF.Abs, ["qrow", "x"], ["t1"], kc("x%d" % k), -1.0)
+            ac(T.F[:, 128 + 128 * k:256 + 128 * k], T.t1[:], AF.Relu, ["t1"], ["F"], 1.0, -2.0)
+        dma([T.Fr[0:112, :], T.Fr[112:128, :]], [T.F[16:128, :], T.F[0:16, :]], ["F"], ["Fr"])
+
+    @unit
+    def const_even():
+        lin(A_, T.Ej[:], T.Fr[:, 128:384], -float(JB), 0.0, ["Fr"], ["Ej"])
+
+    @unit
+    def const_walk():
+        for name, w in (("Nb", -1.0), ("I32", 32.0)):
+            lin(A_, T[name][:], Ib, w, 0.0, ["Ib"], [name])
+        fills(((T.X0[:, S:S + 8], 8, 0.0, "Xe0"), (T.a2[:, B:AW], 8, 0.0, "a23"), (T.X1[:, S:S + 8], 8, 0.0, "Xe1")))
+
+    @unit
+    def const_half():
+        for name, w in (("Irh", 1.0), ("Nrh", -1.0)):
+            lin(A_, T[name][:], Irb, w, 0.0, ["Cr"], [name])
+        dma([T.PT[:, 0:CH], T.PT[:, CH:AW]], [T.zero[:], T.zero[:, 0:AW - CH]], ["zero"], ["PTm", "PTo"])
+        fills(((T.c45[:], 256, 45.0, "c45"),))
+
+    @unit
+    def const_late():
+        for name, w in (("Ih", 1.0), ("Nh", -1.0)):
+            lin(A_, T[name][:], Ib, w, 0.0, ["Ib"], [name])
+        fills(((T.TY[:, B:JB], 8, 0.0, "TYz"),))
+
+    @unit
+    def const_positions():
+        for name, x, w, y in (("w0", oh(0), 1.0, oh(8)), ("w1", oh(1), 1.0, oh(9)), ("wU", kc("w1"), -45.0, kc("w0")),
+                              ("w4", oh(4), 1.0, oh(12)), ("w5", oh(5), 1.0, oh(13)), ("w6", kc("w5"), -45.0, kc("w4")),
+                              ("wV", kc("wU"), -1.0, kc("w6")), ("g14", kc("g"), 1.0, 14.5)):
+            lin(A_, kc(name), x, w, y, ["OH", "g"], ["w"])
+        lin(A_, T.VB[:], T.MV[:], kc("wV"), 0.0, ["MV", "w"], ["VB"])
+        ac(T.UB[:], T.qrow[:, 0:144], AF.Abs, ["qrow", "w"], ["UB"], kc("g14"), -1.0)
+        ac(T.UB[:], T.UB[:], AF.Relu, [], ["UB"], 2.0, -2.0)
+        lin(A_, T.UB[:], T.UB[:], kc("wU"), 0.0, ["w"], ["UB"])
+
+    @unit
+    def first_lists():
+        cp(T.dr[:, 0:96], T.dur[:], ["dur"], ["dr"])
+        cp(T.dl[:], T.dui[:], ["dui"], ["du16"])
+
+    @unit
+    def rows(h, q):
+        cp(T.cmp[:, 768 * h:768 * h + 768], T.qrow[:, 0:16].indirect(T.dl[:, 48 * h:48 * h + 48]), ["qrow", "du16"], ["cmp%d" % h], q)
+
+    @unit
+    def blocks():
+        mm([(T.p7[:, 0:96], mv(i), T.cmp[:, 96 * i:96 * i + 96]) for i in range(16)], ["MV", "cmp0", "cmp1"], ["b7"])
+
+    @unit
+    def blocks_out():
+        lin(A_, T.dd[:, 104:200], T.p7[:, 0:96], 1.0 / 16, 0.0, [], ["b7", "db"])
+
+    @unit
+    def onset_sums(t):
+        L, U, d, ks = (Lr, Ur, T.dd, ["Cr", "dl"]) if t else (Lb, Ub, T.dr, ["Lb", "Ub", "dr"])
+        mm([(T.p6[:, 0:97], L, d[:, 0:97]), (T.p6[:, 1:97], U, d[:, 0:96])], ks + ["dz"], ["b6"])
+
+    @unit
+    def onset_list(t):
+        scan(T.orot[:, 0:97], T.p6[:, 0:97], T.zero[:, 0:97], 0.0, ["zero"], ["b6", "orot"])
+        cp(T.offw[:, 0:64], T.orot[:, 0:64], ["orot"], ["ow0"])
+        ts(T.offw[:, 64:96], T.orot[:, 64:96], -float(CH), None, ALU.add, None, ["orot"], ["ow2"])
+        ts(T.offw[:, 96:97], T.orot[:, 96:97], 1.0 - CH, kc("cap"), ALU.add, ALU.min, ["orot", "cap"], ["ow1"])
+
+    @unit
+    def send_onsets(t):
+        send("o", t, T["lo%d" % t][:], T.offw[:], ["ow0", "ow1", "ow2"], "lo%d" % t)
+
+    @unit
+    def send_amp(t, j):
+        src, k, x = T.a2 if t else T.A, "a2" if t else "A", slice(512 * j, AW if j == 2 else 512 * j + 512)
+        if j == 0:
+            cp(src[:, B:B + 1], src[:, 0:1], [k + "0"], [k + "3"], A_)
+        send("def"[j], t, T["la%d" % t][:, x], src[:, x], [k + str(j)] + [k + "3"] * (j == 2), "la%d%d" % (t, j))
+
+    @unit
+    def ramps(k):
+        for j, (b0, sl) in enumerate((((97.0, 21.0), (236.0, 107.0)), ((100.0, 22.0), (232.0, 106.0)))[k]):
+            ac(T.rp[:, 192 * k + 96 * j:192 * k + 96 * j + 96], T.dd[:, 104:200], AF.Relu, ["db"], ["rp%d%d" % (k, j)], b0 / 256, -sl / 256)
+
+    @unit
+    def ramp_sum(n):
+        k, M, out, base = ((0, T.Qr, T.Ro[:], 51.0), (0, T.Q, T.Rb[:, 0:384], 51.0), (1, T.Q, T.Rb[:, 384:768], 52.0))[n]
+        for y in range(4):
+            mm([(T.p7[:, 96 * y:96 * y + 96], M[:, 128 * y:128 * y + 128], T.rp[:, 192 * k + 96 * j:192 * k + 96 * j + 96]) for j in range(2)],
+               ["Qr" if n == 0 else "Q", "rp%d0" % k, "rp%d1" % k], ["b7"])
+        lin(A_, out, T.p7[:, 0:384], 1.0, base / 256, [], ["b7", "Rb%d" % n])
+
+    @unit
+    def send_rates(t):
+        send("r", t, T["lr%d" % t][:], T.Ro[:], ["Rb0"], "lr%d" % t)
+
+    @unit
+    def block_scan():
+        scan(T.inc[:, 1:97], T.dd[:, 104:200], T.zero[:, 0:96], 0.0, ["db", "zero"], ["inc"])
+
+    @unit
+    def block_sum():
+        mm([(T.p6[:, 0:1], T.Lf[:], T.inc[:, 96:97])], ["Lf", "inc"], ["b6"])
+
+    @unit
+    def block_parts(t):
+        bun, bh, bl = T["bun%d" % (t % 2)], "bh%d" % (t % 2), "bl%d" % (t % 2)
+        ts(bun[:, 0:96], T.inc[:, 0:96], T.p6[:, 0:1], None, ALU.add, None, ["inc"], ["b6", bh])
+        ts(T.of[:, 104:200], T.inc[:, 0:96], T.p6[:, 0:1], None, ALU.add, None, ["inc"], ["b6", "ofb"])
+        tt(bun[:, 96:192], T.of[:, 104:200], bun[:, 0:96], ALU.subtract, ["ofb", bh], [bl])
+
+    @unit
+    def send_blocks(t):
+        send("b", t, T["lb%d" % t][:], T["bun%d" % (t % 2)][:], ["bh%d" % (t % 2), "bl%d" % (t % 2)], "lb%d" % t)
+
+    @unit
+    def rate_rows(t):
+        dma([T.RR[i:128:4, :] for i in range(4)], [T["lr%d" % t][:]] * 4, ["lr%d" % t], ["RR"])
+
+    @unit
+    def amp_turn(t, j):
+        mm([(T.pB[:, third(j)], T.Irh[:] if t else Irb, T["la%d" % t][:, third(j)])], ["Irh" if t else "Cr", "la%d%d" % (t, j)], [bB[j]])
+
+    @unit
+    def amp_table(t, j, q):
+        x0 = JB + 512 * j
+        lin(q, T.TX[:, x0:x0 + 512], T.pB[:, third(j)], 1.0, -256.0 if t else 0.0, [], [bB[j], "TXa%d" % j])
+        if j == 0:
+            cp(T.TX[:, JB + B:JB + B + 1], T.TX[:, JB:JB + 1], [], ["TXa0"], q)
+
+    @unit
+    def diffs(t, j):
+        la, x0 = T["la%d" % t], 512 * j
+        I, N_, ks = (T.Irh[:], T.Nrh[:], ["Irh", "Nrh"]) if t else (Irb, T.Nrb[:], ["Cr", "Nrb"])
+        mm([(T.pA[:, third(j)], I, la[:, x0 + 1:x0 + 513]), (T.pA[:, third(j)], N_, la[:, third(j)])],
+           ks + ["la%d%d" % (t, j), "la%d%d" % (t, min(j + 1, 2))], [bA[j]])
+
+    @unit
+    def slopes(j):
+        tt(T.TX[:, third(j)], T.RR[:, third(j)], T.pA[:, third(j)], ALU.mult, ["RR"], [bA[j], "TX%d" % j])
+
+    @unit
+    def fill(t):
+        dma([WB[t][:, 0:S // 2], WB[t][:, S // 2:S]], [T.ones[:]] * 2, ["ones", "ones2"], WK[t])
+
+    @unit
+    def more_ones():
+        lin(A_, T.ones[:, CH:2 * CH], T.zero[:], 0.0, 1.0, ["zero"], ["ones2"])
+
+    @unit
+    def marks(t, k):
+        lo = T["lo%d" % t]
+        if k == 0:
+            cp(WB[t][:].indirect(lo[:, 0:64]), T.zero[:, 0:CH], ["lo%d" % t, "zero"], WK[t])
+        else:
+            cp(WB[t][:, CH:WW].indirect(lo[:, 64:97]), T.zero[:, 0:528], ["lo%d" % t, "zero"], WK[t][1:])
+
+    @unit
+    def count(t, c):
+        P, x0, bk = LB[c]
+        mm([(P[:, x0:x0 + 64], mv(i), WB[t][:, CH * c + i:CH * c + CH:16]) for i in range(16)], ["MV"] + WK[t][0:1 + (c > 0)], [bk])
+
+    @unit
+    def count_out(c, q):
+        P, x0, bk = LB[c]
+        lin(q, T.ph[:, 8 + 64 * c:72 + 64 * c], P[:, x0:x0 + 64], -1.0 / 16, 0.0, [], [bk, "ph%d" % c])
+
+    @unit
+    def count_sums(c):
+        P, x0, bk = LB[c]
+        mm([(P[:, x0 + 64:x0 + 128], T.T1[:], T.ph[:, 8 + 64 * c:72 + 64 * c]), (P[:, x0 + 64:x0 + 128], T.T2[:], T.ph[:, 7 + 64 * c:71 + 64 * c])],
+           ["T1", "T2", "ph%d" % c, "ph%d" % (c - 1) if c else "phz"], [bk])
+
+    @unit
+    def places(c):
+        (P, x0, bk), x = LB[c], slice(64 * c, 64 * c + 64)
+        scan(T.sa[:, x], P[:, x0 + 64:x0 + 128], T.c16[:], T.sa[:, 64 * c - 1:64 * c] if c else -1.0, ["c16"] + ["sa%d" % (c - 1)] * (c > 0),
+             [bk, "sa%d" % c])
+        cp(T.idx[:, x], T.sa[:, x], ["sa%d" % c], ["idx%d" % c])
+
+    @unit
+    def steps(c, k, q):
+        cp(T.DX[:, chunk(k)], T.TX[:, 0:JB + B + 1].indirect(T.idx[:, 64 * c:64 * c + 64]), TXK + ["idx%d" % c], ["D%d" % k], q)
+
+    @unit
+    def samples(t, c, k):
+        X = XB[t]
+        scan(X[:, chunk(c)], WB[t][:, chunk(c)], T.DX[:, chunk(k)], X[:, CH * c - 1:CH * c] if c else 0.0,
+             ["D%d" % k] + WK[t][0:1 + (c > 0)] + XK[t][c - 1:c], [XK[t][c]], ALU.mult)
+
+    @unit
+    def ship(t, c):
+        w = way(core, T.cores[(r + 1 + t) % N], t, c, T, topo)
+        wi = way(T.cores[(r - 1 - t) % N], core, t, c, T, topo)
+        out, rs = (T["yd%d" % t][c], "ry%d%d" % (t, c)) if len(w) == 2 else (T[STAGE[t]][:, chunk(c)], "q%d" % (NC * t + c))
+        ls = "sy%d%d" % (t, c)
+        call("g", lambda: remote(g, T, topo, core, w[1], out, XB[t][:, chunk(c)], rs, ls, 1), [XK[t][c]], [],
+             (ls, bits(engines(core, w[1], 1, T, topo))))
+        lands("yd%d%d" % (t, c), "ry%d%d" % (t, c), bits(engines(wi[-2], core, 1, T, topo)))
+
+    @unit
+    def list_back():
+        ks = ["sa%d" % c for c in range(NC)]
+        mm([(T.p6[:, 0:256], T.Fr[:, 0:128], T.sa[:])], ["Fr"] + ks, ["b6"])
+        mm([(T.p6[:, 256:384], T.Fr[:, 128 + 128 * k:256 + 128 * k], T.sa[:, k:256:2]) for k in range(2)] +
+           [(T.p6[:, 256:384], T.Ej[:, 128 * k:128 * k + 128], T.ph[:, 8 + k:264:2]) for k in range(2)],
+           ["Fr", "Ej"] + ks + ["ph%d" % c for c in range(NC)], ["b6"])
+
+    @unit
+    def list_out():
+        cp(T.lst[:, 0:256], T.p6[:, 0:256], [], ["b6", "lst"])
+        ts(T.lst[:, 256:384], T.p6[:, 256:384], 1.0 - JB, float(B), ALU.add, ALU.min, [], ["b6", "lst"])
+
+    @unit
+    def send_list(t):
+        send("l", t, T["ll%d" % t][:], T.lst[:], ["lst"], "ll%d" % t, True)
+
+    @unit
+    def onset_rows(t):
+        lb = T["lb%d" % t]
+        dma([T.RX[0:112:16, :], T.RX[112:113, :], T.RX[8:112:16, :], T.RX[120:121, :]],
+            [lb[16:128, 0:96], lb[0:16, 0:96], lb[16:128, 96:192], lb[0:16, 96:192]], ["lb%d" % t], ["RX"])
+
+    @unit
+    def named(h, q):
+        cp(T.PM[:, 768 * h:768 * h + 768], T.RX[:].indirect(T.mpu[:, 48 * h:48 * h + 48]), ["RX", "mpu"], ["PM%d" % h], q)
+
+    @unit
+    def named_rows():
+        cp(T.PM[:, B:B + 1], T.PM[:, B - 1:B], [], ["PM1"], A_)
+        dma([T.PT[0:128:8, 1:B + 2], T.PT[4:128:8, 0:B + 1]], [T.PM[0:128:8, 0:B + 1]] * 2, ["PM0", "PM1"], ["PTm"], A_)
+
+    @unit
+    def own_rows(t):
+        bun = T["bun%d" % (t % 2)]
+        dma([T.PT[row:128:16, x0:x0 + B] for row, x0 in ((1, 1), (9, 1), (5, 0), (13, 0))], [bun[:, 0:96], bun[:, 96:192]] * 2,
+            ["bh%d" % (t % 2), "bl%d" % (t % 2)], ["PTo"])
+
+    @unit
+    def own_last():
+        dma([T.PT[5:128:8, B:B + 1]], [T.PT[1:128:8, B:B + 1]], [], ["PTo"])
+
+    @unit
+    def evens(t, c, q):
+        cp(T.G[:, chunk(c)], T.PT[:].indirect(T["ll%d" % t][:, 256 + 64 * c:320 + 64 * c]), ["PTm", "PTo", "ll%d" % t], ["G%d" % c], q)
+
+    @unit
+    def position_sums(t):
+        P, bk = PB[t]
+        mm([(P[:, 0:256], T.VB[:, 14 - 2 * i:142 - 2 * i], T.G[:, i:2048:8]) for i in range(8)], ["VB", "G0", "G1"], [bk])
+        mm([(P[:, 256:512], T.Z4[:], T.qrow[:]), (P[:, 256:512], Lb, T.c45[:])] +
+           [(P[:, 256:512], T.UB[:, 14 - 2 * i:142 - 2 * i], T.G[:, i:2048:8]) for i in range(8)], ["UB", "Z4", "Lb", "qrow", "c45", "G0", "G1"], [bk])
+
+    @unit
+    def odd_marks(t):
+        ts(T.mask[:], T["ll%d" % t][:, 0:256], float(JB), None, ALU.is_ge, None, ["ll%d" % t], ["mask"])
+
+    @unit
+    def positions(t):
+        P, bk = PB[t]
+        tt(T.vm[:], T.mask[:], P[:, 0:256], ALU.mult, ["mask"], [bk, "vm"])
+        tt(T.ea[:], T.vm[:], P[:, 256:512], ALU.add, ["vm"], [bk, "ea"])
+        ts(T.eb[:], T.ea[:], S - 1, None, ALU.bitwise_and, None, ["ea"], ["eb"])
+        cp(T["el%d" % t][:], T.eb[:], ["eb"], ["el%d" % t])
+
+    def piece(t, c, h=None):
+        x0, x1 = {None: (0, CH), 0: (0, 512), 1: (512, CH)}[h]
+        x = slice(CH * c + x0, CH * c + x1)
+        return x, T[OB[t]][:, x], ["%s%d%s" % (OB[t], c, k) for k in ("ab" if h is None else "ab"[h])]
+
+    @unit
+    def fetch(t, c):
+        yd, z = T["yd%d" % t], T[OB[t]]
+        dma([z[16:128, chunk(c)], z[0:16, chunk(c)]], [yd[c, 0:112, :], yd[c, 112:128, :]], ["yd%d%d" % (t, c)], piece(t, c)[2])
+
+    @unit
+    def product(t, c):
+        x, z, ks = piece(t, c)
+        tt(z, XB[t][:, 0:S].indirect(T["el%d" % t][:, 64 * c:64 * c + 64]), z, ALU.mult, XK[t] + ["el%d" % t], ks)
+
+    @unit
+    def tanh(t, c, h=None):
+        x, z, ks = piece(t, c, h)
+        ac(z, z, AF.Tanh, [], ks, scale=2.0 ** -14)
+
+    @unit
+    def gain(t, c, q, h=None):
+        x, z, ks = piece(t, c, h)
+        lin(q, z, z, T.gn[:, t:t + 1], 0.0, ["gn"], ks)
+
+    @unit
+    def store(t, c, h=None):
+        x, z, ks = piece(t, c, h)
+        dma([T.yo[:, x]], [z], ks, ["yo" + k[1:] for k in ks], "add" if t > FIRST else "sp")
+
+    @unit
+    def gains():
+        for t in range(2):
+            lin(A_, T.Dg[:, 128 * t:128 * t + 128], T.F[:, 0:128], T.gn[:, t:t + 1], 0.0, ["F", "gn"], ["Dg"])
+
+    @unit
+    def mix(c, h):
+        j = (2 * c + h) % 3
+        mm([(T.pA[:, third(j)], T.Dg[:, 128 * t:128 * t + 128], piece(t, c, h)[1]) for t in range(2)],
+           ["Dg"] + piece(0, c, h)[2] + piece(1, c, h)[2], [bA[j]])
+
+    @unit
+    def mix_out(c, h, q):
+        j = (2 * c + h) % 3
+        cp(piece(1, c, h)[1], T.pA[:, third(j)], [], [bA[j]] + piece(1, c, h)[2], q)
+
+    @unit
+    def own_rates():
+        dma([T.RC[i:128:4, :] for i in range(4)], [T.Rb[:]] * 4, ["Rb1", "Rb2"], ["RC"])
+
+    @unit
+    def own_diffs(j):
+        x0 = 512 * j
+        mm([(T.pB[:, third(j)], T.Ih[:], T.a2[:, x0 + 1:x0 + 513]), (T.pB[:, third(j)], T.Nh[:], T.a2[:, third(j)])],
+           ["Ih", "Nh", "a2%d" % j, "a2%d" % (j + 1)], [bB[j]])
+
+    @unit
+    def own_table(j):
+        x0, banks = 384 * j, bB[max(j - 1, 0):j + 1]
+        for h, out, key in ((0, 0, "TY%d"), (1, JB + 1, "TJ%d")):
+            tt(T.TY[:, out + x0:out + x0 + 384], T.RC[:, 2 * x0 + 384 * h:2 * x0 + 384 * h + 384], T.pB[:, x0:x0 + 384], ALU.mult,
+               ["RC"], banks + [key % j])
+
+    @unit
+    def own_ends():
+        lin(V, T.TY[:, JB:JB + 1], T.a2[:, 0:1], 1.0, -256.0, ["a20"], ["TYa"])
+        tt(T.TY[:, JB + B:JB + B + 1], T.TY[:, JB + B:JB + B + 1], T.TY[:, B - 1:B], ALU.subtract, ["TY3"], ["TJ3"])
+
+    @unit
+    def own_steps(c, k, q):
+        cp(T.DX[:, chunk(k)], T.TY[:, 0:JB + B + 1].indirect(T.ll2[:, 64 * c:64 * c + 64]), TYK + ["ll2"], ["D%d" % k], q)
+
+    @unit
+    def own_samples(c, k):
+        scan(T.Y[:, chunk(c)], T.DX[:, chunk(k)], T.zero[:], T.yl[:, c - 1:c] if c else 0.0, ["D%d" % k, "zero"] + ["yl%d" % (c - 1)] * (c > 0),
+             piece(2, c)[2])
+        if BACK[2][c + 1:c + 2] == "-":
+            cp(T.yl[:, c:c + 1], T.Y[:, CH * c + CH - 1:CH * c + CH], piece(2, c)[2], ["yl%d" % c])
+
+    @unit
+    def own_sums():
+        mm([(T.p7[:, 0:96], Lb, T.dd[:, 0:96]), (T.p7[:, 1:96], Ub, T.dd[:, 0:95])], ["Lb", "Ub", "dl"], ["b7"])
+
+    @unit
+    def own_list():
+        scan(T.of[:, 0:96], T.p7[:, 0:96], T.zero[:, 0:96], 0.0, ["zero"], ["b7", "ofl"])
+        ts(T.offs[:], T.of[:, 0:96], float(S), None, ALU.min, None, ["ofl"], ["offs"])
+
+    @unit
+    def live():
+        ts(T.lv[:], T.of[:], float(S), None, ALU.is_lt, None, ["ofl", "ofb", "ofz"], ["lv"])
+        dma([T.RD[0:128:16, :]], [T.lv[:, 104:200]], ["lv"], ["RD"])
+
+    @unit
+    def lower():
+        tt(T.x1[:], T.dd[:], T.lv[:], ALU.subtract, ["dl", "db", "dz", "lv"], ["x1"])
+
+    @unit
+    def edge():
+        ac(T.e1[:], T.dd[:], AF.Abs, ["dl", "db", "dz"], ["e1"], -3.0)
+        ac(T.e5[:], T.e1[:], AF.Relu, ["e1"], ["e5"], -32.0, 32.0)
+
+    @unit
+    def bounce():
+        ac(T.z2[:], T.x1[:], AF.Relu, ["x1"], ["z2"], 2.0, -2.0)
+
+    @unit
+    def fallen():
+        tt(T.dn[:], T.x1[:], T.z2[:], ALU.add, ["x1", "z2"], ["dn"])
+
+    @unit
+    def dead_sum(j):
+        mm([(T.pB[:, third(j)], Ib, T.V0[:, third(j)]), (T.pB[:, third(j)], T.Z1[:], T.RD[:, third(j)])], ["Ib", "Z1", "V0", "RD"], [bB[j]])
+
+    @unit
+    def dead(j, q):
+        if q == V:
+            ts(T.zv[:, third(j)], T.pB[:, third(j)], 64.0, 0.0, ALU.add, ALU.max, [], [bB[j], "zv%d" % j])
+        else:
+            ac(T.zv[:, third(j)], T.pB[:, third(j)], AF.Relu, [], [bB[j], "zv%d" % j], 64.0)
+
+    @unit
+    def open_v(t, j):
+        old, ks = ([(Ib, T.uh), (T.Z1[:], T.RD)], ["Z1", "RD", "uh%d" % j]) if t else ([(Ib, T.V0)], ["V0"])
+        mm([(T.pA[:, third(j)], l, w[:, third(j)]) for l, w in old], ["Ib"] + ks, [bA[j]], True, False)
+
+    @unit
+    def open_a(t, j):
+        old, ks = ([(T.Z3[:], T.RD)], ["Z3"]) if t else ([(T.Z2[:], T.RD), (T.Nb[:], T.zv)], ["Z2", "Nb", "zv%d" % j])
+        mm([(T.pB[:, third(j)], l, w[:, third(j)]) for l, w in [(Ib, T.A)] + old], ["Ib", "RD", AK[j]] + ks, [bB[j]], True, False)
+
+    @unit
+    def votes_open(f):
+        x = slice(104 * f, 104 * f + 96)
+        P = (T.p6, T.p7)[f]
+        mm([(P[:, 0:96], T.Nb[:], T.e5[:, x]), (P[:, 0:96], T.I32[:], T.lv[:, x])], ["Nb", "I32", "e5", "lv"], ["b%d" % (6 + f)], True, False)
+
+    @unit
+    def compare(t, h):
+        tt(T.cmp[:, 768 * h:768 * h + 768], XB[t][:, 0:S + 1].indirect(T.offs[:, 48 * h:48 * h + 48]), T.A[:, 768 * h:768 * h + 768],
+           ALU.is_gt, XK[t] + ["Xe%d" % t, "offs", AK[h], AK[h + 1]], ["cmp%d" % h])
+
+    @unit
+    def votes(f, h):
+        if f == 0:
+            mm([(T.p6[:, 48 * h:48 * h + 48], mv(i), T.cmp[:, 768 * h + i:768 * h + 768:16]) for i in range(16)], ["MV", "cmp%d" % h], ["b6"], False, h == 1)
+        else:
+            mm([(T.p7[:, 0:96], mv(i), T.cmp[:, 96 * i:96 * i + 96]) for i in range(8 * h, 8 * h + 8)], ["MV", "cmp%d" % h], ["b7"], False, h == 1)
+
+    @unit
+    def durations(f):
+        x, P, bk, dk = slice(104 * f, 104 * f + 96), (T.p6, T.p7)[f], "b%d" % (6 + f), ("dl", "db")[f]
+        ts(T.u2[:, x], P[:, 0:96], 40.5, 2.0, ALU.is_ge, ALU.mult, [], [bk, "u2" + dk])
+        tt(T.dd[:, x], T.u2[:, x], T.dn[:, x], ALU.add, ["u2" + dk, "dn"], [dk])
+
+    @unit
+    def force(t, j, q):
+        lin(q, T.fb[:, third(j)], XB[t][:, 0:S + 1].indirect(T.offs[:, 32 * j:32 * j + 32]), 1.0 / 16, 145.0 - 2047.5 / 4096,
+            XK[t] + ["Xe%d" % t, "offs"], ["fb%d" % j])
+
+    @unit
+    def add_force(j):
+        mm([(T.pA[:, third(j)], Ib, T.fb[:, third(j)])], ["Ib", "fb%d" % j], [bA[j]], False, True)
+
+    @unit
+    def velocity(t, j):
+        mid = (145.0, 34.0)[t]
+        ts(T.uh[:, third(j)], T.pA[:, third(j)], mid - 64, mid + 64, ALU.max, ALU.min, [], [bA[j], "uh%d" % j])
+
+    @unit
+    def add_velocity(j):
+        mm([(T.pB[:, third(j)], Ib, T.uh[:, third(j)])], ["Ib", "uh%d" % j], [bB[j]], False, True)
+
+    @unit
+    def reflect(t, j):
+        ac(T.a1[:, third(j)], T.pB[:, third(j)], AF.Abs, [], [bB[j], "a1%d" % j], -(337.0, 354.0)[t])
+        ac(T.a2[:, third(j)], T.a1[:, third(j)], AF.Abs, ["a1%d" % j], ["a2%d" % j], 512.0, -1.0)
+
+    @unit
+    def amplitudes(q):
+        lin(q, T.A[:, 0:B], T.a2[:, 0:B], 1.0, -256.0, ["a20", "a21", "a22"], AK[0:3])
+
+    for line in PLAN.split(","):
+        name, *args = line.split()
+        step[name](*[{"v": V, "a": A_}.get(x) or int(x) for x in args])
     for s, n in total.items():
         if waited.get(("g", s), 0) < n:
             g.wait_ge(T.sem[s], n)

from concourse.mybir import AluOpType as ALU, ActivationFunctionType as AF

S, B, NB, N = 4096, 1536, 3, 8
CH = 1024
NC = S // CH
JB = 1544
TW = JB + B + 8
WW = 7712
AW = B + 8
F32, BF, F16, I32, U16 = "float32", "bfloat16", "float16", "int32", "uint16"

SCRATCH = {}
for _d, _w, _names in (
        (BF, B, "V0 RX RD RR cmp fb zv uh"), (F16, B, "a1"), (BF, AW, "A la0 PM PT"), (F16, AW, "a2 la1 la2"), (BF, 2 * B, "RC"),
        (I32, 96, "dui dur mpi"), (F32, 4, "gn yl"), (U16, 96, "mpu dl offs"), (U16, 98, "offw lo0 lo1 lo2"), (U16, 256, "idx el0 el1 el2"),
        (U16, 384, "lst ll0 ll1 ll2"), (F32, 32, "K"), (F32, 16, "OH"), (I32, 16, "pi"),
        (BF, 128, "Nb I32 Nrb Z1 Z2 Z3 Z4 t2 t3"), (F16, 128, "T1 T2 Ih Nh Irh Nrh"), (BF, 384, "C Cr rp"), (F32, 384, "F Fr"),
        (BF, 144, "MV UB VB"), (F32, 128, "Lf t1"), (BF, 256, "qrow c45 mask"), (F16, 256, "Ej"), (BF, 2048, "G ones"), (BF, CH, "zero"),
        (BF, 64, "c16"), (BF, 104, "dr"), (F32, 256, "sa vm Dg"), (I32, 256, "ea eb"), (BF, WW, "W0 W1"),
        (BF, 192, "bun0 bun1 lb0 lb1 lb2"), (BF, 384, "Ro lr0 lr1 lr2"), (BF, 768, "Rb"), (BF, 512, "Q Qr"), (BF, 128, "q4"), (BF, 200, "dd lv x1 z2 dn e1 e5 u2"), (F32, 100, "inc orot"), (F32, 200, "of"),
        (F16, 264, "ph"), (F32, TW, "TY TX"), (F32, S + 8, "X0 X1"), (F32, S, "Y DX Z")):
    for _n in _names.split():
        SCRATCH[_n] = ("sbuf", [128, _w], _d)
for _n, _w in (("pA", B), ("pB", B), ("p6", 512), ("p7", 512)):
    SCRATCH[_n] = ("psum", [128, _w], F32)

SIM = 64
BACK = ("ffnn", "ffnn", "----")
RELAY = (1, 2)
STAGE = ("Y", "Z", "DX")
NDMA = 56
SEMAPHORES = ["pe", "dve", "act", "pool", "hs"] + ["q%d" % i for i in range(NDMA)]
for _t in range(NB):
    for _m in "obrdefl":
        SEMAPHORES += ["s%s%d" % (_m, _t), "r%s%d" % (_m, _t)]
    SCRATCH["yd%d" % _t] = ("dram", [NC, 128, CH], F32)
    for _c in range(NC):
        SEMAPHORES += ["sy%d%d" % (_t, _c), "ry%d%d" % (_t, _c)]
FIRST = 0
V, A_ = "dve", "act"

PLAN = """
sums_matrix, first_lists, onset_sums 0, onset_list 0, const_blocks, own_sums, rows 1 v, send_onsets 0, send_amp 0 1, const_back,
own_list, rows 0 a, blocks, const_dead, blocks_out, ramps 0, send_amp 0 0, const_quarters 0, ramp_sum 0, send_rates 0, first_ones,
block_scan, block_sum, amp_turn 0 0, const_counts, const_even, block_parts 0, live, const_walk, diffs 0 0, amp_table 0 0 a, clear_rows,
dead_sum 0, send_amp 0 2, rate_rows 0, dead_sum 1, diffs 0 1, marks 0 0, lower, marks 0 1, amp_turn 0 2, dead 1 a, slopes 0, dead 0 a,
edge, count 0 0, amp_table 0 2 a, slopes 1, bounce, count_out 0 a, amp_turn 0 1, amp_table 0 1 a, diffs 0 2, slopes 2, count 0 1,
send_blocks 0, onset_rows 0, count_sums 0, count 0 2, count_out 1 a, places 0, count_out 2 v, steps 0 0 a, count_sums 1, places 1,
steps 1 1 a, mp_list, count 0 3, count_out 3 v, count_sums 2, places 2, steps 2 2 a, votes_open 1, count_sums 3, places 3, named 1 a,
samples 0 0 0, open_a 0 0, steps 3 3 v, list_back, samples 0 1 1, const_half, samples 0 2 2, ship 0 0, dead_sum 2, list_out, dead 2 a,
open_v 0 2, more_ones, fill 1, open_a 0 1, open_v 0 0, open_a 0 2, samples 0 3 3, force 0 0 v, force 0 1 a, own_rows 0, own_last,
compare 0 0, open_v 0 1, send_list 0, force 0 2 a, add_force 0, velocity 0 0, votes_open 0, compare 0 1, add_force 1, named 0 a,
velocity 0 1, votes 0 0, fallen, add_velocity 0, reflect 0 0, send_amp 1 0, ship 0 1, add_force 2, votes 0 1, votes 1 0, durations 0,
velocity 0 2, add_velocity 1, named_rows, onset_sums 1, onset_list 1, reflect 0 1, send_onsets 1, add_velocity 2, votes 1 1,
durations 1, block_scan, send_amp 1 1, block_sum, block_parts 1, send_blocks 1, ship 0 2, reflect 0 2, ship 0 3, edge, ramps 0,
send_amp 1 2, evens 0 0 a, own_sums, const_late, own_list, marks 1 0, onset_rows 1, odd_marks 0, amplitudes a, evens 0 1 v, marks 1 1,
ramp_sum 0, amp_turn 1 1, count 1 0, const_positions, live, send_rates 1, diffs 1 0, amp_turn 1 0, const_quarters 1, position_sums 0,
rate_rows 1, count_out 0 a, positions 0, count_sums 0, places 0, amp_table 1 0 a, diffs 1 2, slopes 2, diffs 1 1, amp_table 1 1 a,
slopes 0, count 1 1, count_out 1 a, amp_turn 1 2, count 1 2, slopes 1, count_sums 1, places 1, fetch 0 1, fetch 0 0, amp_table 1 2 a,
count 1 3, count_out 2 v, count_sums 2, votes_open 1, count_out 3 v, count_sums 3, places 2, places 3, steps 0 0 a, samples 1 0 0,
open_v 1 0, steps 1 1 a, steps 3 3 v, list_back, steps 2 2 a, open_a 1 0, samples 1 1 1, list_out, ship 1 0, open_a 1 1, named 1 a,
open_v 1 1, samples 1 2 2, samples 1 3 3, compare 1 0, open_v 1 2, votes_open 0, lower, force 1 0 a, add_force 0, force 1 1 a,
compare 1 1, velocity 1 0, named 0 a, fetch 0 3, bounce, votes 0 0, force 1 2 a, named_rows, add_force 1, votes 0 1, velocity 1 1,
add_velocity 1, fallen, fill 2, add_force 2, durations 0, reflect 1 1, onset_sums 2, onset_list 2, own_rows 1, fetch 0 2,
add_velocity 0, reflect 1 0, send_list 1, odd_marks 1, velocity 1 2, send_onsets 2, votes 1 0, votes 1 1, own_last, evens 1 1 a,
ship 1 1, durations 1, ramps 1, ramps 0, product 0 2, send_amp 2 1, block_scan, open_a 1 2, add_velocity 2, product 0 0, send_amp 2 0,
reflect 1 2, tanh 0 2, block_sum, send_amp 2 2, ramp_sum 0, tanh 0 0, amp_turn 2 1, ramp_sum 1, product 0 3, evens 1 0 a, tanh 0 3,
send_rates 2, ramp_sum 2, diffs 2 2, diffs 2 1, amp_turn 2 2, gain 0 0 a, rate_rows 2, marks 2 0, amp_table 2 2 a, block_parts 2,
diffs 2 0, amp_turn 2 0, amp_table 2 0 a, ship 1 2, count 2 0, count_out 0 a, marks 2 1, product 0 1, amp_table 2 1 a, count 2 1,
count_out 1 a, count 2 2, count_out 2 a, send_blocks 2, count_sums 0, places 0, count 2 3, slopes 1, own_rows 2, tanh 0 1, gain 0 1 a,
count_sums 2, count_out 3 v, count_sums 3, slopes 2, slopes 0, count_sums 1, places 1, places 2, steps 0 0 a, onset_rows 2, fetch 1 0,
steps 2 2 a, gain 0 3 v, position_sums 1, own_rates, named 0 v, store 0 1, named 1 a, named_rows, gain 0 2 a, samples 2 0 0, places 3,
positions 1, own_diffs 0, store 0 0, own_table 0, steps 1 1 a, steps 3 3 a, list_back, fetch 1 2, list_out, product 1 0, own_diffs 1,
tanh 1 0, own_table 1, own_diffs 2, samples 2 1 1, ship 1 3, samples 2 2 2, send_list 2, own_table 2, gain 1 0 a, own_last,
evens 2 0 a, own_table 3, own_ends, fetch 1 1, evens 2 1 a, store 0 3, own_steps 0 0 a, product 1 1, tanh 1 1, store 1 0, product 1 2,
samples 2 3 3, tanh 1 2, gain 1 1 a, odd_marks 2, position_sums 2, own_samples 0 0, store 0 2, fetch 1 3, positions 2, own_steps 2 2 a,
own_steps 1 1 a, product 2 0, product 1 3, gain 1 2 a, own_steps 3 3 a, store 1 1, tanh 1 3, store 1 2, gain 1 3 a, store 1 3,
own_samples 1 1, own_samples 2 2, tanh 2 0, gain 2 0 a, store 2 0, product 2 1, tanh 2 1, gain 2 1 a, store 2 1, own_samples 3 3,
product 2 3, product 2 2, tanh 2 3 0, gain 2 3 v 0, store 2 3 0, tanh 2 3 1, gain 2 3 v 1, store 2 3 1, tanh 2 2, gain 2 2 a,
store 2 2
"""


def bits(m):
    return bin(m).count("1")


def helper_of(c, topo):
    mine = [k for k in topo.cores_of(c) if topo.die(k) == topo.die(c)]
    other = [k for k in topo.cores_of(c) if topo.die(k) != topo.die(c)]
    return other[mine.index(c)]


def engines(src, dst, part, T, topo):
    e = topo.engines(src, dst)
    if T.rank_of(src) is not None and topo.chip(src) == topo.chip(dst):
        e = e[part * len(e) // 2:(part + 1) * len(e) // 2]
    return sum(1 << k for k in e)


def remote(g, T, topo, src, dst, out, in_, rsem, lsem, part):
    rid, pid, _ = topo.addr(dst)
    g.remote_dma(out, in_, T.sem[rsem], T.sem[lsem], pid, rid, engines(src, dst, part, T, topo))


def way(src, dst, t, c, T, topo):
    h = helper_of(src, topo)
    if topo.chip(src) == topo.chip(dst) or BACK[t][c] == "s" or T.rank_of(h) is not None or not topo.may_write(h, dst):
        return [src, dst]
    far = [f for f in range(SIM) if topo.mates(topo.chip(f), topo.chip(dst)) and topo.may_write(h, f) and topo.may_write(f, dst)
           and topo.die(f) == topo.die(h)]
    if BACK[t][c] == "f" and far:
        return [src, h, far[T.rank_of(src) % len(far)], dst]
    return [src, h, dst]


def relay(src, t, T, topo):
    dst, mine = T.cores[(T.rank_of(src) - 1 - t) % N], [k for k in T.cores if topo.chip(k) == topo.chip(src)]
    if t not in RELAY or topo.chip(src) == topo.chip(dst):
        return None
    k = mine.index(src)
    return helper_of(mine[k % 2], topo), slice(512 * (k // 2), 512 * (k // 2) + 512), "r%s%d" % ("de"[k // 2], t), dst


def helper_program(g, core, T, topo):
    sent = 0
    for t in RELAY:
        for src in T.cores:
            h, x, sem, dst = relay(src, t, T, topo) or [None] * 4
            if h == core:
                g.wait_ge(T.sem[sem], bits(engines(src, core, 0, T, topo)))
                remote(g, T, topo, core, dst, T["la%d" % t][:, 0:512], T["la%d" % t][:, x], "rd%d" % t, "hs", 0)
                sent += bits(engines(core, dst, 0, T, topo))
    for t in range(NB):
        for c in range(NC):
            for r in range(N):
                w = way(T.cores[r], T.cores[(r + 1 + t) % N], t, c, T, topo)
                if core in w and BACK[t][c] != "-":
                    k = w.index(core)
                    stage = T[STAGE[t]][:, CH * c:CH * c + CH]
                    g.wait_ge(T.sem["q%d" % (NC * t + c)], bits(engines(w[k - 1], core, 1, T, topo)))
                    if k + 2 == len(w):
                        remote(g, T, topo, core, w[k + 1], T["yd%d" % t][c], stage, "ry%d%d" % (t, c), "hs", 1)
                    else:
                        remote(g, T, topo, core, w[k + 1], stage, stage, "q%d" % (NC * t + c), "hs", 1)
                    sent += bits(engines(core, w[k + 1], 1, T, topo))
    if sent:
        g.wait_ge(T.sem["hs"], sent)


def rank_program(g, core, T, topo):
    if T.rank_of(core) is None:
        helper_program(g, core, T, topo)
        return
    r = T.rank_of(core)
    v, a, pe = g.vector, g.scalar, g.tensor
    queue = {"dve": v, "act": a, "pe": pe, "pool": g, "g": g, "sp": g.sync}
    issued = {"dve": 0, "act": 0, "pe": 0, "pool": 0}
    lastw, readers, waited, total, ndma = {}, {}, {}, {}, [0]

    def call(q, fn, reads, writes, tok=None):
        need = {}
        for s, n in [lastw[k] for k in reads + writes if k in lastw] + [x for k in writes for x in readers.get(k, [])]:
            need[s] = max(need.get(s, 0), n)
        qq = "g" if q == "pool" else q
        for s, n in need.items():
            if waited.get((qq, s), 0) < n:
                queue[q].wait_ge(T.sem[s], n)
                waited[(qq, s)] = n
        ins = fn()
        if tok is None:
            ins.then_inc(T.sem[q], 1)
            issued[q] += 1
            tok = (q, issued[q])
        total[tok[0]] = tok[1]
        for k in reads:
            readers.setdefault(k, []).append(tok)
        for k in writes:
            lastw[k], readers[k] = tok, []

    def lands(key, sem, n):
        lastw[key] = (sem, n)
        total[sem] = n

    def select(out, in_, pat, op, fill_, base, cm, rk, wk):
        call("pool", lambda: g.affine_select(out, in_, pat, op, fill_, base, cm), [rk], [wk])

    def ts(out, in0, s1, s2, op0, op1, reads, writes):
        call(V, lambda: v.tensor_scalar(out, in0, s1, s2, op0, op1) if op1 else v.tensor_scalar(out, in0, s1, None, op0), reads, writes)

    def tt(out, in0, in1, op, reads, writes):
        call(V, lambda: v.tensor_tensor(out, in0, in1, op), reads, writes)

    def cp(out, in_, reads, writes, q=V):
        call(q, lambda: v.tensor_copy(out, in_) if q == V else a.activation(out, in_, AF.Identity), reads, writes)

    def ms(out, c, writes):
        call(V, lambda: v.memset(out, c), [], writes)

    def scan(out, d0, d1, ini, reads, writes, op0=ALU.add):
        call(V, lambda: v.tensor_tensor_scan(out, d0, d1, ini, op0, ALU.add), reads, writes)

    def ac(out, in_, f, reads, writes, bias=0.0, scale=1.0):
        call(A_, lambda: a.activation(out, in_, f, bias=bias, scale=scale), reads, writes)

    def lin(q, out, in_, scale, bias, reads, writes):
        if q == V:
            ts(out, in_, scale, bias, ALU.mult, ALU.add, reads, writes)
        else:
            ac(out, in_, AF.Identity, reads, writes, bias, scale)

    def mm(grp, reads, writes, start=True, stop=True):
        def fn():
            for i, (o, l, x) in enumerate(grp):
                ins = pe.matmul(o, l, x, start and i == 0, stop and i == len(grp) - 1)
            return ins
        call("pe", fn, reads, writes)

    def dma(outs, ins, reads, writes, how="sp"):
        s = "q%d" % ndma[0]
        ndma[0] += 1

        def fn():
            for o, i in zip(outs, ins):
                d = g.dma_start(o, i, accum_op=ALU.add) if how == "add" else queue[how].dma_start(o, i)
                d.then_inc(T.sem[s], 16)
        call("g" if how == "add" else how, fn, reads, writes, (s, 16 * len(outs)))

    def send(m, t, out, src_ap, reads, land, back=False):
        dst, src = T.cores[(r - 1 - t) % N], T.cores[(r + 1 + t) % N]
        if back:
            dst, src = src, dst
        ls, rs, got = "s%s%d" % (m, t), "r%s%d" % (m, t), "r%s%d" % (m, t)
        if m == "d" and relay(core, t, T, topo):
            dst, x, rs, _ = relay(core, t, T, topo)
            out = T["la%d" % t][:, x]
        if m == "d" and relay(src, t, T, topo):
            src = relay(src, t, T, topo)[0]
        call("g", lambda: remote(g, T, topo, core, dst, out, src_ap, rs, ls, 0), reads, [], (ls, bits(engines(core, dst, 0, T, topo))))
        lands(land, got, bits(engines(src, core, 0, T, topo)))

    kn = {}

    def kc(name):
        return T.K[:, kn.setdefault(name, len(kn)):kn[name] + 1]

    def oh(j):
        return T.OH[:, j:j + 1]

    def mv(i):
        return T.MV[:, 15 - i:143 - i]

    def third(j):
        return slice(512 * j, 512 * j + 512)

    def chunk(c):
        return slice(CH * c, CH * c + CH)

    def fills(what):
        for out, w, c, key in what:
            lin(A_, out, T.zero[:, 0:w], 0.0, c, ["zero"], [key])

    XB, WB, OB = [T.X0, T.X1, T.X0], [T.W0, T.W1, T.W0], "YZY"
    XK = [["X%d%d" % (t % 2, c) for c in range(NC)] for t in range(NB)]
    WK = [["W%d%d" % (t % 2, k) for k in range(2)] for t in range(NB)]
    bA, bB, AK = ["b0", "b1", "b2"], ["b3", "b4", "b5"], ["A0", "A1", "A2", "A3"]
    TXK = ["TX0", "TX1", "TX2", "TXz", "TXa0", "TXa1", "TXa2"]
    TYK = ["TY0", "TY1", "TY2", "TY3", "TJ0", "TJ1", "TJ2", "TJ3", "TYz", "TYa"]
    Lb, Ub, Ib = (T.C[:, 128 * k:128 * k + 128] for k in range(3))
    Lr, Ur, Irb = (T.Cr[:, 128 * k:128 * k + 128] for k in range(3))
    LB = [(T.p6, 0, "b6"), (T.pB, 0, "b3"), (T.pB, 512, "b4"), (T.pB, 1024, "b5")]
    PB = [(T.p7, "b7")] * NB
    step = {}

    def unit(f):
        step[str(f).split(".")[-1].split()[0]] = f
        return f

    dma([T.dur[0:112, :], T.dur[112:128, :]], [T.du[16:128, :], T.du[0:16, :]], [], ["dur"])
    dma([T.dui[:]], [T.du[:]], [], ["dui"])
    dma([T.A[:, 0:B]], [T.am[:]], [], AK[0:3])
    dma([T.V0[:], T.mpi[:], T.gn[:, 0:3]], [T.ve[:], T.mp[:], T.gain[:]], [], ["V0", "mpi", "gn"])
    call("pool", lambda: g.iota(T.pi[:, 0:1], [[0, 1]], 0, 1), [], ["pi0"])
    call("pool", lambda: g.iota(T.qrow[:], [[1, 256]], 0, 0, allow_small_or_imprecise_dtypes=True), [], ["qrow"])
    ms(T.ones[:, 0:CH], 1.0, ["ones"])
    ms(T.zero[:], 0.0, ["zero"])
    select(T.t2[:], T.ones[:, 0:128], [[-16, 8], [0, 16]], ALU.is_ge, 0.0, 0, 1, "ones", "t2")
    select(T.t3[:], T.t2[:], [[16, 8], [0, 16]], ALU.is_ge, 0.0, 15, -1, "t2", "t3")
    select(Lb, T.t3[:], [[1, 128]], ALU.is_gt, 0.0, 0, -1, "t3", "Lb")
    select(Ub, T.t3[:], [[-1, 128]], ALU.is_ge, 0.0, 0, 1, "t3", "Ub")
    select(Ib, T.zero[:, 0:128], [[-1, 128]], ALU.not_equal, 1.0, 0, 1, "zero", "Ib")
    dma([T.Cr[16:128, :], T.Cr[0:16, :]], [T.C[0:112, :], T.C[112:128, :]], ["Lb", "Ub", "Ib"], ["Cr"])
    ts(T.pi[:, 4:5], T.pi[:, 0:1], 15, None, ALU.bitwise_and, None, ["pi0"], ["pi4"])
    cp(kc("p"), T.pi[:, 0:1], ["pi0"], ["p"])
    cp(kc("r"), T.pi[:, 4:5], ["pi4"], ["r"])
    ms(T.offw[:, 96:98], 0, ["ow1"])
    ms(T.RD[:], 0.0, ["RD"])
    lin(A_, kc("cap"), kc("r"), 1.0, 7690.0 - CH, ["r"], ["cap"])
    lin(A_, kc("g"), kc("r"), -1.0, kc("p"), ["p", "r"], ["g"])
    fills(((T.dd[:, 96:104], 8, 2560.0, "dz"), (T.dr[:, 96:104], 8, 2560.0, "dz"), (T.A[:, B:AW], 8, 0.0, "A3")))

    @unit
    def sums_matrix():
        ts(T.MV[:], T.qrow[:, 0:144], -15.0, kc("g"), ALU.add, ALU.is_equal, ["qrow", "g"], ["MV"])

    @unit
    def const_quarters(n):
        if n == 0:
            call("pool", lambda: g.iota(T.q4[:], [[16, 8], [0, 4], [4, 4]], 0, 0, allow_small_or_imprecise_dtypes=True), [], ["q4"])
            ts(kc("p1"), kc("p"), 16.0, 128.0, ALU.is_lt, ALU.mult, ["p"], ["p1"])
            ts(kc("pr"), kc("p1"), kc("p"), -16.0, ALU.add, ALU.add, ["p1", "p"], ["pr"])
        for y in range(4):
            ts((T.Qr, T.Q)[n][:, 128 * y:128 * y + 128], T.q4[:], float(y), kc(("pr", "p")[n]), ALU.add, ALU.is_equal, ["q4", "pr"], [("Qr", "Q")[n]])

    @unit
    def first_ones():
        ms(T.W0[:, 0:S], 1.0, WK[0])

    @unit
    def clear_rows():
        for x in (slice(0, CH), slice(CH, B)):
            cp(T.RX[:, x], T.zero[:, 0:x.stop - x.start], ["zero"], ["RX"], A_)

    @unit
    def const_blocks():
        cp(T.Lf[:], Lb, ["Lb"], ["Lf"], A_)
        fills(((T.inc[:, 0:1], 1, 0.0, "inc"), (T.of[:, 96:104], 8, 0.0, "ofz")))
        cp(T.dd[:, 0:96], T.dui[:], ["dui"], ["dl"])
        ts(T.OH[:], T.qrow[:, 0:16], kc("r"), None, ALU.is_equal, None, ["qrow", "r"], ["OH"])

    @unit
    def mp_list():
        cp(T.mpu[:], T.mpi[:], ["mpi"], ["mpu"])

    @unit
    def const_counts():
        select(T.T1[:], Lb, [[-1, 128]], ALU.not_equal, JB + 1.0, 0, 1, "Lb", "T1")
        select(T.T2[:], Ub, [[-1, 128]], ALU.not_equal, -float(JB), 0, 1, "Ub", "T2")
        fills(((T.c16[:], 64, 16.0, "c16"), (T.ph[:, 0:8], 8, -1.0, "phz"), (T.TX[:, B:JB], 8, 0.0, "TXz")))
        lin(A_, T.Nrb[:], Irb, -1.0, 0.0, ["Cr"], ["Nrb"])

    @unit
    def const_dead():
        for name, w in (("Z1", -256.0), ("Z2", -64.0), ("Z3", 64.0), ("Z4", 720.0)):
            lin(A_, kc(name), oh(0), w, 0.0, ["OH"], ["k" + name])
            lin(A_, T[name][:], T.t3[:], kc(name), 0.0, ["t3", "k" + name], [name])

    @unit
    def const_back():
        lin(A_, kc("x0"), kc("r"), 0.5, kc("g"), ["r", "g"], ["x"])
        lin(A_, kc("x1"), kc("x0"), 1.0, 8.0, [], ["x"])
        lin(A_, T.F[:, 0:128], Ib, 1.0, 0.0, ["Ib"], ["F"])
        for k in range(2):
            ac(T.t1[:], T.qrow[:, 0:128], AF.Abs, ["qrow", "x"], ["t1"], kc("x%d" % k), -1.0)
            ac(T.F[:, 128 + 128 * k:256 + 128 * k], T.t1[:], AF.Relu, ["t1"], ["F"], 1.0, -2.0)
        dma([T.Fr[0:112, :], T.Fr[112:128, :]], [T.F[16:128, :], T.F[0:16, :]], ["F"], ["Fr"])

    @unit
    def const_even():
        lin(A_, T.Ej[:], T.Fr[:, 128:384], -float(JB), 0.0, ["Fr"], ["Ej"])

    @unit
    def const_walk():
        for name, w in (("Nb", -1.0), ("I32", 32.0)):
            lin(A_, T[name][:], Ib, w, 0.0, ["Ib"], [name])
        fills(((T.X0[:, S:S + 8], 8, 0.0, "Xe0"), (T.a2[:, B:AW], 8, 0.0, "a23"), (T.X1[:, S:S + 8], 8, 0.0, "Xe1")))

    @unit
    def const_half():
        for name, w in (("Irh", 1.0), ("Nrh", -1.0)):
            lin(A_, T[name][:], Irb, w, 0.0, ["Cr"], [name])
        dma([T.PT[:, 0:CH], T.PT[:, CH:AW]], [T.zero[:], T.zero[:, 0:AW - CH]], ["zero"], ["PTm", "PTo"])
        fills(((T.c45[:], 256, 45.0, "c45"),))

    @unit
    def const_late():
        for name, w in (("Ih", 1.0), ("Nh", -1.0)):
            lin(A_, T[name][:], Ib, w, 0.0, ["Ib"], [name])
        fills(((T.TY[:, B:JB], 8, 0.0, "TYz"),))

    @unit
    def const_positions():
        for name, x, w, y in (("w0", oh(0), 1.0, oh(8)), ("w1", oh(1), 1.0, oh(9)), ("wU", kc("w1"), -45.0, kc("w0")),
                              ("w4", oh(4), 1.0, oh(12)), ("w5", oh(5), 1.0, oh(13)), ("w6", kc("w5"), -45.0, kc("w4")),
                              ("wV", kc("wU"), -1.0, kc("w6")), ("g14", kc("g"), 1.0, 14.5)):
            lin(A_, kc(name), x, w, y, ["OH", "g"], ["w"])
        lin(A_, T.VB[:], T.MV[:], kc("wV"), 0.0, ["MV", "w"], ["VB"])
        ac(T.UB[:], T.qrow[:, 0:144], AF.Abs, ["qrow", "w"], ["UB"], kc("g14"), -1.0)
        ac(T.UB[:], T.UB[:], AF.Relu, [], ["UB"], 2.0, -2.0)
        lin(A_, T.UB[:], T.UB[:], kc("wU"), 0.0, ["w"], ["UB"])

    @unit
    def first_lists():
        cp(T.dr[:, 0:96], T.dur[:], ["dur"], ["dr"])
        cp(T.dl[:], T.dui[:], ["dui"], ["du16"])

    @unit
    def rows(h, q):
        cp(T.cmp[:, 768 * h:768 * h + 768], T.qrow[:, 0:16].indirect(T.dl[:, 48 * h:48 * h + 48]), ["qrow", "du16"], ["cmp%d" % h], q)

    @unit
    def blocks():
        mm([(T.p7[:, 0:96], mv(i), T.cmp[:, 96 * i:96 * i + 96]) for i in range(16)], ["MV", "cmp0", "cmp1"], ["b7"])

    @unit
    def blocks_out():
        lin(A_, T.dd[:, 104:200], T.p7[:, 0:96], 1.0 / 16, 0.0, [], ["b7", "db"])

    @unit
    def onset_sums(t):
        L, U, d, ks = (Lr, Ur, T.dd, ["Cr", "dl"]) if t else (Lb, Ub, T.dr, ["Lb", "Ub", "dr"])
        mm([(T.p6[:, 0:97], L, d[:, 0:97]), (T.p6[:, 1:97], U, d[:, 0:96])], ks + ["dz"], ["b6"])

    @unit
    def onset_list(t):
        scan(T.orot[:, 0:97], T.p6[:, 0:97], T.zero[:, 0:97], 0.0, ["zero"], ["b6", "orot"])
        cp(T.offw[:, 0:64], T.orot[:, 0:64], ["orot"], ["ow0"])
        ts(T.offw[:, 64:96], T.orot[:, 64:96], -float(CH), None, ALU.add, None, ["orot"], ["ow2"])
        ts(T.offw[:, 96:97], T.orot[:, 96:97], 1.0 - CH, kc("cap"), ALU.add, ALU.min, ["orot", "cap"], ["ow1"])

    @unit
    def send_onsets(t):
        send("o", t, T["lo%d" % t][:], T.offw[:], ["ow0", "ow1", "ow2"], "lo%d" % t)

    @unit
    def send_amp(t, j):
        src, k, x = T.a2 if t else T.A, "a2" if t else "A", slice(512 * j, AW if j == 2 else 512 * j + 512)
        if j == 0:
            cp(src[:, B:B + 1], src[:, 0:1], [k + "0"], [k + "3"], A_)
        send("def"[j], t, T["la%d" % t][:, x], src[:, x], [k + str(j)] + [k + "3"] * (j == 2), "la%d%d" % (t, j))

    @unit
    def ramps(k):
        for j, (b0, sl) in enumerate((((97.0, 21.0), (236.0, 107.0)), ((100.0, 22.0), (232.0, 106.0)))[k]):
            ac(T.rp[:, 192 * k + 96 * j:192 * k + 96 * j + 96], T.dd[:, 104:200], AF.Relu, ["db"], ["rp%d%d" % (k, j)], b0 / 256, -sl / 256)

    @unit
    def ramp_sum(n):
        k, M, out, base = ((0, T.Qr, T.Ro[:], 51.0), (0, T.Q, T.Rb[:, 0:384], 51.0), (1, T.Q, T.Rb[:, 384:768], 52.0))[n]
        for y in range(4):
            mm([(T.p7[:, 96 * y:96 * y + 96], M[:, 128 * y:128 * y + 128], T.rp[:, 192 * k + 96 * j:192 * k + 96 * j + 96]) for j in range(2)],
               ["Qr" if n == 0 else "Q", "rp%d0" % k, "rp%d1" % k], ["b7"])
        lin(A_, out, T.p7[:, 0:384], 1.0, base / 256, [], ["b7", "Rb%d" % n])

    @unit
    def send_rates(t):
        send("r", t, T["lr%d" % t][:], T.Ro[:], ["Rb0"], "lr%d" % t)

    @unit
    def block_scan():
        scan(T.inc[:, 1:97], T.dd[:, 104:200], T.zero[:, 0:96], 0.0, ["db", "zero"], ["inc"])

    @unit
    def block_sum():
        mm([(T.p6[:, 0:1], T.Lf[:], T.inc[:, 96:97])], ["Lf", "inc"], ["b6"])

    @unit
    def block_parts(t):
        bun, bh, bl = T["bun%d" % (t % 2)], "bh%d" % (t % 2), "bl%d" % (t % 2)
        ts(bun[:, 0:96], T.inc[:, 0:96], T.p6[:, 0:1], None, ALU.add, None, ["inc"], ["b6", bh])
        ts(T.of[:, 104:200], T.inc[:, 0:96], T.p6[:, 0:1], None, ALU.add, None, ["inc"], ["b6", "ofb"])
        tt(bun[:, 96:192], T.of[:, 104:200], bun[:, 0:96], ALU.subtract, ["ofb", bh], [bl])

    @unit
    def send_blocks(t):
        send("b", t, T["lb%d" % t][:], T["bun%d" % (t % 2)][:], ["bh%d" % (t % 2), "bl%d" % (t % 2)], "lb%d" % t)

    @unit
    def rate_rows(t):
        dma([T.RR[i:128:4, :] for i in range(4)], [T["lr%d" % t][:]] * 4, ["lr%d" % t], ["RR"])

    @unit
    def amp_turn(t, j):
        mm([(T.pB[:, third(j)], T.Irh[:] if t else Irb, T["la%d" % t][:, third(j)])], ["Irh" if t else "Cr", "la%d%d" % (t, j)], [bB[j]])

    @unit
    def amp_table(t, j, q):
        x0 = JB + 512 * j
        lin(q, T.TX[:, x0:x0 + 512], T.pB[:, third(j)], 1.0, -256.0 if t else 0.0, [], [bB[j], "TXa%d" % j])
        if j == 0:
            cp(T.TX[:, JB + B:JB + B + 1], T.TX[:, JB:JB + 1], [], ["TXa0"], q)

    @unit
    def diffs(t, j):
        la, x0 = T["la%d" % t], 512 * j
        I, N_, ks = (T.Irh[:], T.Nrh[:], ["Irh", "Nrh"]) if t else (Irb, T.Nrb[:], ["Cr", "Nrb"])
        mm([(T.pA[:, third(j)], I, la[:, x0 + 1:x0 + 513]), (T.pA[:, third(j)], N_, la[:, third(j)])],
           ks + ["la%d%d" % (t, j), "la%d%d" % (t, min(j + 1, 2))], [bA[j]])

    @unit
    def slopes(j):
        tt(T.TX[:, third(j)], T.RR[:, third(j)], T.pA[:, third(j)], ALU.mult, ["RR"], [bA[j], "TX%d" % j])

    @unit
    def fill(t):
        dma([WB[t][:, 0:S // 2], WB[t][:, S // 2:S]], [T.ones[:]] * 2, ["ones", "ones2"], WK[t])

    @unit
    def more_ones():
        lin(A_, T.ones[:, CH:2 * CH], T.zero[:], 0.0, 1.0, ["zero"], ["ones2"])

    @unit
    def marks(t, k):
        lo = T["lo%d" % t]
        if k == 0:
            cp(WB[t][:].indirect(lo[:, 0:64]), T.zero[:, 0:CH], ["lo%d" % t, "zero"], WK[t])
        else:
            cp(WB[t][:, CH:WW].indirect(lo[:, 64:97]), T.zero[:, 0:528], ["lo%d" % t, "zero"], WK[t][1:])

    @unit
    def count(t, c):
        P, x0, bk = LB[c]
        mm([(P[:, x0:x0 + 64], mv(i), WB[t][:, CH * c + i:CH * c + CH:16]) for i in range(16)], ["MV"] + WK[t][0:1 + (c > 0)], [bk])

    @unit
    def count_out(c, q):
        P, x0, bk = LB[c]
        lin(q, T.ph[:, 8 + 64 * c:72 + 64 * c], P[:, x0:x0 + 64], -1.0 / 16, 0.0, [], [bk, "ph%d" % c])

    @unit
    def count_sums(c):
        P, x0, bk = LB[c]
        mm([(P[:, x0 + 64:x0 + 128], T.T1[:], T.ph[:, 8 + 64 * c:72 + 64 * c]), (P[:, x0 + 64:x0 + 128], T.T2[:], T.ph[:, 7 + 64 * c:71 + 64 * c])],
           ["T1", "T2", "ph%d" % c, "ph%d" % (c - 1) if c else "phz"], [bk])

    @unit
    def places(c):
        (P, x0, bk), x = LB[c], slice(64 * c, 64 * c + 64)
        scan(T.sa[:, x], P[:, x0 + 64:x0 + 128], T.c16[:], T.sa[:, 64 * c - 1:64 * c] if c else -1.0, ["c16"] + ["sa%d" % (c - 1)] * (c > 0),
             [bk, "sa%d" % c])
        cp(T.idx[:, x], T.sa[:, x], ["sa%d" % c], ["idx%d" % c])

    @unit
    def steps(c, k, q):
        cp(T.DX[:, chunk(k)], T.TX[:, 0:JB + B + 1].indirect(T.idx[:, 64 * c:64 * c + 64]), TXK + ["idx%d" % c], ["D%d" % k], q)

    @unit
    def samples(t, c, k):
        X = XB[t]
        scan(X[:, chunk(c)], WB[t][:, chunk(c)], T.DX[:, chunk(k)], X[:, CH * c - 1:CH * c] if c else 0.0,
             ["D%d" % k] + WK[t][0:1 + (c > 0)] + XK[t][c - 1:c], [XK[t][c]], ALU.mult)

    @unit
    def ship(t, c):
        w = way(core, T.cores[(r + 1 + t) % N], t, c, T, topo)
        wi = way(T.cores[(r - 1 - t) % N], core, t, c, T, topo)
        out, rs = (T["yd%d" % t][c], "ry%d%d" % (t, c)) if len(w) == 2 else (T[STAGE[t]][:, chunk(c)], "q%d" % (NC * t + c))
        ls = "sy%d%d" % (t, c)
        call("g", lambda: remote(g, T, topo, core, w[1], out, XB[t][:, chunk(c)], rs, ls, 1), [XK[t][c]], [],
             (ls, bits(engines(core, w[1], 1, T, topo))))
        lands("yd%d%d" % (t, c), "ry%d%d" % (t, c), bits(engines(wi[-2], core, 1, T, topo)))

    @unit
    def list_back():
        ks = ["sa%d" % c for c in range(NC)]
        mm([(T.p6[:, 0:256], T.Fr[:, 0:128], T.sa[:])], ["Fr"] + ks, ["b6"])
        mm([(T.p6[:, 256:384], T.Fr[:, 128 + 128 * k:256 + 128 * k], T.sa[:, k:256:2]) for k in range(2)] +
           [(T.p6[:, 256:384], T.Ej[:, 128 * k:128 * k + 128], T.ph[:, 8 + k:264:2]) for k in range(2)],
           ["Fr", "Ej"] + ks + ["ph%d" % c for c in range(NC)], ["b6"])

    @unit
    def list_out():
        cp(T.lst[:, 0:256], T.p6[:, 0:256], [], ["b6", "lst"])
        ts(T.lst[:, 256:384], T.p6[:, 256:384], 1.0 - JB, float(B), ALU.add, ALU.min, [], ["b6", "lst"])

    @unit
    def send_list(t):
        send("l", t, T["ll%d" % t][:], T.lst[:], ["lst"], "ll%d" % t, True)

    @unit
    def onset_rows(t):
        lb = T["lb%d" % t]
        dma([T.RX[0:112:16, :], T.RX[112:113, :], T.RX[8:112:16, :], T.RX[120:121, :]],
            [lb[16:128, 0:96], lb[0:16, 0:96], lb[16:128, 96:192], lb[0:16, 96:192]], ["lb%d" % t], ["RX"])

    @unit
    def named(h, q):
        cp(T.PM[:, 768 * h:768 * h + 768], T.RX[:].indirect(T.mpu[:, 48 * h:48 * h + 48]), ["RX", "mpu"], ["PM%d" % h], q)

    @unit
    def named_rows():
        cp(T.PM[:, B:B + 1], T.PM[:, B - 1:B], [], ["PM1"], A_)
        dma([T.PT[0:128:8, 1:B + 2], T.PT[4:128:8, 0:B + 1]], [T.PM[0:128:8, 0:B + 1]] * 2, ["PM0", "PM1"], ["PTm"], A_)

    @unit
    def own_rows(t):
        bun = T["bun%d" % (t % 2)]
        dma([T.PT[row:128:16, x0:x0 + B] for row, x0 in ((1, 1), (9, 1), (5, 0), (13, 0))], [bun[:, 0:96], bun[:, 96:192]] * 2,
            ["bh%d" % (t % 2), "bl%d" % (t % 2)], ["PTo"])

    @unit
    def own_last():
        dma([T.PT[5:128:8, B:B + 1]], [T.PT[1:128:8, B:B + 1]], [], ["PTo"])

    @unit
    def evens(t, c, q):
        cp(T.G[:, chunk(c)], T.PT[:].indirect(T["ll%d" % t][:, 256 + 64 * c:320 + 64 * c]), ["PTm", "PTo", "ll%d" % t], ["G%d" % c], q)

    @unit
    def position_sums(t):
        P, bk = PB[t]
        mm([(P[:, 0:256], T.VB[:, 14 - 2 * i:142 - 2 * i], T.G[:, i:2048:8]) for i in range(8)], ["VB", "G0", "G1"], [bk])
        mm([(P[:, 256:512], T.Z4[:], T.qrow[:]), (P[:, 256:512], Lb, T.c45[:])] +
           [(P[:, 256:512], T.UB[:, 14 - 2 * i:142 - 2 * i], T.G[:, i:2048:8]) for i in range(8)], ["UB", "Z4", "Lb", "qrow", "c45", "G0", "G1"], [bk])

    @unit
    def odd_marks(t):
        ts(T.mask[:], T["ll%d" % t][:, 0:256], float(JB), None, ALU.is_ge, None, ["ll%d" % t], ["mask"])

    @unit
    def positions(t):
        P, bk = PB[t]
        tt(T.vm[:], T.mask[:], P[:, 0:256], ALU.mult, ["mask"], [bk, "vm"])
        tt(T.ea[:], T.vm[:], P[:, 256:512], ALU.add, ["vm"], [bk, "ea"])
        ts(T.eb[:], T.ea[:], S - 1, None, ALU.bitwise_and, None, ["ea"], ["eb"])
        cp(T["el%d" % t][:], T.eb[:], ["eb"], ["el%d" % t])

    def piece(t, c, h=None):
        x0, x1 = {None: (0, CH), 0: (0, 512), 1: (512, CH)}[h]
        x = slice(CH * c + x0, CH * c + x1)
        return x, T[OB[t]][:, x], ["%s%d%s" % (OB[t], c, k) for k in ("ab" if h is None else "ab"[h])]

    @unit
    def fetch(t, c):
        yd, z = T["yd%d" % t], T[OB[t]]
        dma([z[16:128, chunk(c)], z[0:16, chunk(c)]], [yd[c, 0:112, :], yd[c, 112:128, :]], ["yd%d%d" % (t, c)], piece(t, c)[2])

    @unit
    def product(t, c):
        x, z, ks = piece(t, c)
        tt(z, XB[t][:, 0:S].indirect(T["el%d" % t][:, 64 * c:64 * c + 64]), z, ALU.mult, XK[t] + ["el%d" % t], ks)

    @unit
    def tanh(t, c, h=None):
        x, z, ks = piece(t, c, h)
        ac(z, z, AF.Tanh, [], ks, scale=2.0 ** -14)

    @unit
    def gain(t, c, q, h=None):
        x, z, ks = piece(t, c, h)
        lin(q, z, z, T.gn[:, t:t + 1], 0.0, ["gn"], ks)

    @unit
    def store(t, c, h=None):
        x, z, ks = piece(t, c, h)
        dma([T.yo[:, x]], [z], ks, ["yo" + k[1:] for k in ks], "add" if t > FIRST else "sp")

    @unit
    def gains():
        for t in range(2):
            lin(A_, T.Dg[:, 128 * t:128 * t + 128], T.F[:, 0:128], T.gn[:, t:t + 1], 0.0, ["F", "gn"], ["Dg"])

    @unit
    def mix(c, h):
        j = (2 * c + h) % 3
        mm([(T.pA[:, third(j)], T.Dg[:, 128 * t:128 * t + 128], piece(t, c, h)[1]) for t in range(2)],
           ["Dg"] + piece(0, c, h)[2] + piece(1, c, h)[2], [bA[j]])

    @unit
    def mix_out(c, h, q):
        j = (2 * c + h) % 3
        cp(piece(1, c, h)[1], T.pA[:, third(j)], [], [bA[j]] + piece(1, c, h)[2], q)

    @unit
    def own_rates():
        dma([T.RC[i:128:4, :] for i in range(4)], [T.Rb[:]] * 4, ["Rb1", "Rb2"], ["RC"])

    @unit
    def own_diffs(j):
        x0 = 512 * j
        mm([(T.pB[:, third(j)], T.Ih[:], T.a2[:, x0 + 1:x0 + 513]), (T.pB[:, third(j)], T.Nh[:], T.a2[:, third(j)])],
           ["Ih", "Nh", "a2%d" % j, "a2%d" % (j + 1)], [bB[j]])

    @unit
    def own_table(j):
        x0, banks = 384 * j, bB[max(j - 1, 0):j + 1]
        for h, out, key in ((0, 0, "TY%d"), (1, JB + 1, "TJ%d")):
            tt(T.TY[:, out + x0:out + x0 + 384], T.RC[:, 2 * x0 + 384 * h:2 * x0 + 384 * h + 384], T.pB[:, x0:x0 + 384], ALU.mult,
               ["RC"], banks + [key % j])

    @unit
    def own_ends():
        lin(V, T.TY[:, JB:JB + 1], T.a2[:, 0:1], 1.0, -256.0, ["a20"], ["TYa"])
        tt(T.TY[:, JB + B:JB + B + 1], T.TY[:, JB + B:JB + B + 1], T.TY[:, B - 1:B], ALU.subtract, ["TY3"], ["TJ3"])

    @unit
    def own_steps(c, k, q):
        cp(T.DX[:, chunk(k)], T.TY[:, 0:JB + B + 1].indirect(T.ll2[:, 64 * c:64 * c + 64]), TYK + ["ll2"], ["D%d" % k], q)

    @unit
    def own_samples(c, k):
        scan(T.Y[:, chunk(c)], T.DX[:, chunk(k)], T.zero[:], T.yl[:, c - 1:c] if c else 0.0, ["D%d" % k, "zero"] + ["yl%d" % (c - 1)] * (c > 0),
             piece(2, c)[2])
        if BACK[2][c + 1:c + 2] == "-":
            cp(T.yl[:, c:c + 1], T.Y[:, CH * c + CH - 1:CH * c + CH], piece(2, c)[2], ["yl%d" % c])

    @unit
    def own_sums():
        mm([(T.p7[:, 0:96], Lb, T.dd[:, 0:96]), (T.p7[:, 1:96], Ub, T.dd[:, 0:95])], ["Lb", "Ub", "dl"], ["b7"])

    @unit
    def own_list():
        scan(T.of[:, 0:96], T.p7[:, 0:96], T.zero[:, 0:96], 0.0, ["zero"], ["b7", "ofl"])
        ts(T.offs[:], T.of[:, 0:96], float(S), None, ALU.min, None, ["ofl"], ["offs"])

    @unit
    def live():
        ts(T.lv[:], T.of[:], float(S), None, ALU.is_lt, None, ["ofl", "ofb", "ofz"], ["lv"])
        dma([T.RD[0:128:16, :]], [T.lv[:, 104:200]], ["lv"], ["RD"])

    @unit
    def lower():
        tt(T.x1[:], T.dd[:], T.lv[:], ALU.subtract, ["dl", "db", "dz", "lv"], ["x1"])

    @unit
    def edge():
        ac(T.e1[:], T.dd[:], AF.Abs, ["dl", "db", "dz"], ["e1"], -3.0)
        ac(T.e5[:], T.e1[:], AF.Relu, ["e1"], ["e5"], -32.0, 32.0)

    @unit
    def bounce():
        ac(T.z2[:], T.x1[:], AF.Relu, ["x1"], ["z2"], 2.0, -2.0)

    @unit
    def fallen():
        tt(T.dn[:], T.x1[:], T.z2[:], ALU.add, ["x1", "z2"], ["dn"])

    @unit
    def dead_sum(j):
        mm([(T.pB[:, third(j)], Ib, T.V0[:, third(j)]), (T.pB[:, third(j)], T.Z1[:], T.RD[:, third(j)])], ["Ib", "Z1", "V0", "RD"], [bB[j]])

    @unit
    def dead(j, q):
        if q == V:
            ts(T.zv[:, third(j)], T.pB[:, third(j)], 64.0, 0.0, ALU.add, ALU.max, [], [bB[j], "zv%d" % j])
        else:
            ac(T.zv[:, third(j)], T.pB[:, third(j)], AF.Relu, [], [bB[j], "zv%d" % j], 64.0)

    @unit
    def open_v(t, j):
        old, ks = ([(Ib, T.uh), (T.Z1[:], T.RD)], ["Z1", "RD", "uh%d" % j]) if t else ([(Ib, T.V0)], ["V0"])
        mm([(T.pA[:, third(j)], l, w[:, third(j)]) for l, w in old], ["Ib"] + ks, [bA[j]], True, False)

    @unit
    def open_a(t, j):
        old, ks = ([(T.Z3[:], T.RD)], ["Z3"]) if t else ([(T.Z2[:], T.RD), (T.Nb[:], T.zv)], ["Z2", "Nb", "zv%d" % j])
        mm([(T.pB[:, third(j)], l, w[:, third(j)]) for l, w in [(Ib, T.A)] + old], ["Ib", "RD", AK[j]] + ks, [bB[j]], True, False)

    @unit
    def votes_open(f):
        x = slice(104 * f, 104 * f + 96)
        P = (T.p6, T.p7)[f]
        mm([(P[:, 0:96], T.Nb[:], T.e5[:, x]), (P[:, 0:96], T.I32[:], T.lv[:, x])], ["Nb", "I32", "e5", "lv"], ["b%d" % (6 + f)], True, False)

    @unit
    def compare(t, h):
        tt(T.cmp[:, 768 * h:768 * h + 768], XB[t][:, 0:S + 1].indirect(T.offs[:, 48 * h:48 * h + 48]), T.A[:, 768 * h:768 * h + 768],
           ALU.is_gt, XK[t] + ["Xe%d" % t, "offs", AK[h], AK[h + 1]], ["cmp%d" % h])

    @unit
    def votes(f, h):
        if f == 0:
            mm([(T.p6[:, 48 * h:48 * h + 48], mv(i), T.cmp[:, 768 * h + i:768 * h + 768:16]) for i in range(16)], ["MV", "cmp%d" % h], ["b6"], False, h == 1)
        else:
            mm([(T.p7[:, 0:96], mv(i), T.cmp[:, 96 * i:96 * i + 96]) for i in range(8 * h, 8 * h + 8)], ["MV", "cmp%d" % h], ["b7"], False, h == 1)

    @unit
    def durations(f):
        x, P, bk, dk = slice(104 * f, 104 * f + 96), (T.p6, T.p7)[f], "b%d" % (6 + f), ("dl", "db")[f]
        ts(T.u2[:, x], P[:, 0:96], 40.5, 2.0, ALU.is_ge, ALU.mult, [], [bk, "u2" + dk])
        tt(T.dd[:, x], T.u2[:, x], T.dn[:, x], ALU.add, ["u2" + dk, "dn"], [dk])

    @unit
    def force(t, j, q):
        lin(q, T.fb[:, third(j)], XB[t][:, 0:S + 1].indirect(T.offs[:, 32 * j:32 * j + 32]), 1.0 / 16, 145.0 - 2047.5 / 4096,
            XK[t] + ["Xe%d" % t, "offs"], ["fb%d" % j])

    @unit
    def add_force(j):
        mm([(T.pA[:, third(j)], Ib, T.fb[:, third(j)])], ["Ib", "fb%d" % j], [bA[j]], False, True)

    @unit
    def velocity(t, j):
        mid = (145.0, 34.0)[t]
        ts(T.uh[:, third(j)], T.pA[:, third(j)], mid - 64, mid + 64, ALU.max, ALU.min, [], [bA[j], "uh%d" % j])

    @unit
    def add_velocity(j):
        mm([(T.pB[:, third(j)], Ib, T.uh[:, third(j)])], ["Ib", "uh%d" % j], [bB[j]], False, True)

    @unit
    def reflect(t, j):
        ac(T.a1[:, third(j)], T.pB[:, third(j)], AF.Abs, [], [bB[j], "a1%d" % j], -(337.0, 354.0)[t])
        ac(T.a2[:, third(j)], T.a1[:, third(j)], AF.Abs, ["a1%d" % j], ["a2%d" % j], 512.0, -1.0)

    @unit
    def amplitudes(q):
        lin(q, T.A[:, 0:B], T.a2[:, 0:B], 1.0, -256.0, ["a20", "a21", "a22"], AK[0:3])

    for line in PLAN.split(","):
        name, *args = line.split()
        step[name](*[{"v": V, "a": A_}.get(x) or int(x) for x in args])
    for s, n in total.items():
        if waited.get(("g", s), 0) < n:
            g.wait_ge(T.sem[s], n)
